import numpy as np
import ml_dtypes


def mxq(x, axis, fmt="e4m3"):
    dtype, down = {"e4m3": (ml_dtypes.float8_e4m3fn, 7), "e5m2": (ml_dtypes.float8_e5m2, 14)}[fmt]
    v = np.moveaxis(np.asarray(x, np.float32).astype(ml_dtypes.bfloat16).astype(np.float64), axis, -1)
    blocks = v.reshape(v.shape[:-1] + (-1, 32))
    amax = np.abs(blocks).max(-1, keepdims=True)
    byte = np.maximum(np.where(amax > 0, np.frexp(amax)[1] - 1 + 127, 0) - down, 1)
    scale = np.exp2(byte - 127.0)
    codes = (blocks / scale).astype(np.float32).astype(dtype).astype(np.float64)
    return np.moveaxis((codes * scale).reshape(v.shape), -1, axis)


WIDE = False


def mx_kscale(k):
    if not WIDE:
        return np.ones(k)
    levels = np.array([10, -10, 5, -5, 0])
    if k % 512:
        return np.exp2(np.random.permutation(np.resize(levels, k // 32))).repeat(32)
    a = np.empty((k // 512, 16))
    for p in range(k // 512):
        a[p, :8] = np.random.permutation(np.resize(levels, 8))
        for g in range(8):
            far = levels[np.abs(levels - a[p, g]) >= 10]
            a[p, g + 8] = far[np.random.randint(len(far))]
    return np.exp2(a.ravel()).repeat(32)


def f64(x):
    return np.asarray(x).astype(np.float64)


def striped(idx):
    return np.tile(idx.reshape(-1, 16).T, (8, 1)).astype(np.uint16)


def unstriped(offs):
    return offs[:16].T.reshape(-1).astype(np.int64)


E2M1 = np.array([0.0, 0.5, 1.0, 1.5, 2.0, 3.0, 4.0, 6.0, -0.0, -0.5, -1.0, -1.5, -2.0, -3.0, -4.0, -6.0])


def pack_weight(w, fmt):
    k, n = w.shape
    w = f64(np.asarray(w, np.float32).astype(ml_dtypes.bfloat16)).reshape(k // 32, 32, n)
    amax = np.abs(w).max(1)
    if fmt == "e4m3":
        byte = np.frexp(amax)[1] - 1 + 127 - 7
    else:
        mant, ex = np.frexp(amax / 6.0)
        byte = np.where(mant > 0.5, ex, ex - 1) + 127
    byte = np.clip(np.where(amax > 0, byte, 1), 1, 254)
    scaled = (w * np.exp2(127.0 - byte)[:, None, :]).reshape(k, n).astype(np.float32)
    by_word = np.ascontiguousarray(scaled.reshape(k // 512, 128, 4, n).transpose(0, 1, 3, 2))
    if fmt == "e4m3":
        words = by_word.astype(ml_dtypes.float8_e4m3fn).view(np.uint8)
    else:
        c = by_word.astype(ml_dtypes.float4_e2m1fn).view(np.uint8) & 0xF
        words = (c[..., 0::2] | (c[..., 1::2] << 4)).reshape(k // 512, 128, 2 * n)
    return np.ascontiguousarray(words), np.ascontiguousarray(byte.astype(np.uint8).reshape(k // 512, 16, n))


def unpack_weight(words, scales, fmt):
    g, _, n = scales.shape
    words = np.ascontiguousarray(words).reshape(g, 128, n, -1)
    if fmt == "e4m3":
        vals = words.view(ml_dtypes.float8_e4m3fn).astype(np.float64)
    else:
        nib = np.empty((g, 128, n, 4), np.uint8)
        nib[..., 0::2] = words & 0xF
        nib[..., 1::2] = words >> 4
        vals = E2M1[nib]
    vals = vals * np.repeat(np.exp2(scales.astype(np.float64) - 127.0), 8, axis=1)[..., None]
    return vals.transpose(0, 1, 3, 2).reshape(g * 512, n)


def gelu(v):
    return 0.5 * v * (1.0 + np.tanh(np.sqrt(2.0 / np.pi) * (v + 0.044715 * v**3)))


K, T, S, T2, P, H, N = 1024, 4096, 1024, 2048, 1024, 1024, 512

def setup_inputs():
    n = np.random.standard_normal
    s = mx_kscale(K)[:, None]
    u = mx_kscale(H)[:, None]
    tab_words, tab_scales = pack_weight(n((K, T)) * s, "e4m3")
    w2_words, w2_scales = pack_weight(n((H, N)) / np.sqrt(H) / u, "e2m1")
    return {
        "tab_words": tab_words, "tab_scales": tab_scales,
        "offs": striped(np.random.permutation(T)[:S]),
        "w1": (n((K, H)) / np.sqrt(K) / s).astype(np.float32),
        "page0": n((H, T2)).astype(np.float32),
        "wgs": np.exp(0.3 * n((128, S))).astype(np.float32),
        "offs2": striped(np.random.permutation(T2)[:S]),
        "offs3": striped(np.random.permutation(T2)[:P]),
        "gain": (np.exp(0.3 * n(H)) * u[:, 0]).astype(np.float32),
        "stock": (0.7 * n((H, P)) * u).astype(np.float32),
        "w2_words": w2_words, "w2_scales": w2_scales,
    }

def reference(tab_words, tab_scales, offs, w1, page0, wgs, offs2, offs3, gain, stock, w2_words, w2_scales):
    v = unpack_weight(tab_words, tab_scales, "e4m3")[:, unstriped(offs)]
    h = mxq(f64(w1), 0, "e4m3").T @ v
    page = f64(page0).copy()
    page[:, unstriped(offs2)] = np.tile(f64(wgs), (H // 128, 1)) * h
    x = page[:, unstriped(offs3)]
    sp = np.log(1.0 + np.exp(x))
    z = f64(gain)[:, None] * sp - f64(stock)
    w2 = unpack_weight(w2_words, w2_scales, "e2m1")
    return w2.T @ mxq(z, 0, "e4m3")

@@ -1,0 +1,314 @@
+from contextlib import ExitStack
+
+import concourse.mybir as mybir
+from concourse.masks import make_identity
+
+K, T, S, T2, NP, H, N = 1024, 4096, 1024, 2048, 1024, 1024, 512
+FLOPS = 2 * K * H * S + 2 * H * N * NP
+
+F32 = mybir.dt.float32
+BF16 = mybir.dt.bfloat16
+I32 = mybir.dt.int32
+U32 = mybir.dt.uint32
+U16 = mybir.dt.uint16
+U8 = mybir.dt.uint8
+FP8X4 = mybir.dt.float8_e4m3fn_x4
+FP4X4 = mybir.dt.float4_e2m1fn_x4
+ALU = mybir.AluOpType
+ACT = mybir.ActivationFunctionType
+
+P = 128
+BANK = 512
+TILES = H // P
+W1_BLOCKS = ((0,), (1, 2), (3, 4), (5, 6), (7,))
+LN_GROUPS = ((0, 1, 2, 3), (4, 5), (6, 7))
+
+
+def tile_list_vaccine_dispatch_kernel(
+    tc, tab_words, tab_scales, offs, w1, page0, wgs, offs2, offs3, gain, stock, w2_words, w2_scales, out
+):
+    nc = tc.nc
+    with ExitStack() as ctx:
+        sb = ctx.enter_context(tc.tile_pool(name="sb", bufs=1))
+        ps = ctx.enter_context(tc.psum_pool(name="ps", bufs=1))
+
+        list1 = sb.tile([P, S // 16], U16, name="list1")
+        list2 = sb.tile([P, S // 16], U16, name="list2")
+        list3 = sb.tile([P, NP // 16], U16, name="list3")
+        words = [sb.tile([P, T], I32, name=f"words{a}") for a in range(2)]
+        planes = sb.tile([P, T], U8, name="planes")
+        picked = [sb.tile([P, S], U32, name=f"picked{a}", align_bytes=64) for a in range(2)]
+        picked_scales = sb.tile([P, S], U8, name="picked_scales", align_bytes=64)
+        weights = sb.tile([P, S], F32, name="weights")
+        w2c = sb.tile([P, 2, 2 * N], U8, name="w2c", align_bytes=64)
+        w2s = sb.tile([P, 2, N], U8, name="w2s", align_bytes=64)
+        ident = sb.tile([P, P], F32, name="ident")
+        gain_rows = sb.tile([P, P], F32, name="gain_rows")
+        gain_cols = sb.tile([P, TILES], F32, name="gain_cols")
+        first_stage = sb.tile([P, 2 * P * 4], BF16, name="first_stage", align_bytes=64)
+
+        raw, pages, stocks, hs, xs, soft, pos = {}, {}, {}, {}, {}, {}, {}
+        ring = [sb.tile([P, S], F32, name=f"ring{i}", align_bytes=64) for i in range(4)]
+
+        def load_w1(block):
+            width = len(block) * P
+            t = sb.tile([P, 2, 4, width], F32, name="w1_raw", tag="w1_raw", bufs=2)
+            for a in range(2):
+                rows = w1[a * BANK : (a + 1) * BANK, block[0] * P : block[0] * P + width]
+                nc.sync.dma_start(out=t[:, a, :, :], in_=rows.rearrange("(p j) c -> p j c", j=4))
+            for i, c in enumerate(block):
+                raw[c] = t[:, :, :, i * P : (i + 1) * P]
+
+        def load_page(c):
+            pages[c] = sb.tile([P, T2], F32, name="page", tag="page", bufs=3)
+            nc.sync.dma_start(out=pages[c][:], in_=page0[c * P : (c + 1) * P, :])
+
+        def load_stock(c):
+            if c == 0:
+                stocks[c] = ring[3]
+            else:
+                stocks[c] = sb.tile([P, NP], F32, name="stock", tag="stock", bufs=4)
+            nc.sync.dma_start(out=stocks[c][:], in_=stock[c * P : (c + 1) * P, :])
+
+        def quantise_w1(c, stage):
+            nc.scalar.copy(
+                out=stage.rearrange("p (a c i t) -> p a c t i", a=2, i=4, t=4),
+                in_=raw[c].rearrange("p a t (c i) -> p a c t i", i=4),
+            )
+            codes = sb.tile([P, 2 * P], U32, name="w1c", tag="w1c", bufs=3, align_bytes=64)
+            scales = sb.tile([P, 2 * P], U8, name="w1s", tag="w1s", bufs=3, align_bytes=64)
+            nc.vector.quantize_mx(out=codes[:].bitcast(FP8X4), scales=scales[:], in_=stage)
+            return codes, scales
+
+        def first_product(c, codes, scales):
+            for half in range(2):
+                cols = slice(half * BANK, (half + 1) * BANK)
+                acc = ps.tile([P, BANK], F32, name="acc", tag="acc", bufs=2)
+                for a in range(2):
+                    nc.tensor.matmul_mx(
+                        out=acc[:],
+                        lhsT=codes[:, a * P : (a + 1) * P].bitcast(FP8X4),
+                        lhsT_scale=scales[:, a * P : (a + 1) * P],
+                        rhs=picked[a][:, cols].bitcast(FP8X4),
+                        rhs_scale=picked_scales[4 * a : P, cols],
+                        start=(a == 0),
+                        stop=(a == 1),
+                    )
+                nc.scalar.copy(out=hs[c][:, cols], in_=acc[:])
+
+        def scatter(c, lo, hi):
+            nc.vector.tensor_tensor(
+                pages[c][:].indirect(list2[:, lo // 16 : hi // 16]), hs[c][:, lo:hi], weights[:, lo:hi], ALU.mult
+            )
+
+        def gather(c, lo, hi):
+            nc.vector.tensor_copy(xs[c][:, lo:hi], pages[c][:].indirect(list3[:, lo // 16 : hi // 16]))
+
+        zt = [[sb.tile([P, 4, 2, P, 2], BF16, name=f"zt{a}{half}") for half in range(2)] for a in range(2)]
+        zc = [sb.tile([P, NP], U32, name=f"zc{a}", align_bytes=64) for a in range(2)]
+        zs = [sb.tile([P, NP], U8, name=f"zs{a}", align_bytes=64) for a in range(2)]
+
+        def copy_on(engine, dst, src):
+            if engine == "scalar":
+                nc.scalar.copy(out=dst, in_=src)
+            else:
+                nc.vector.tensor_copy(out=dst, in_=src)
+
+        def halves(t):
+            return t[:].rearrange("p (h m) -> p h m", h=2)
+
+        def minus_stock(c, lo, hi):
+            nc.vector.scalar_tensor_tensor(
+                out=soft[c][:, lo:hi, :], in0=soft[c][:, lo:hi, :], scalar=gain_cols[:, c : c + 1],
+                in1=halves(stocks[c])[:, lo:hi, :], op0=ALU.mult, op1=ALU.subtract,
+            )
+
+        def sum_and_round(c, half, engine):
+            a, cc = divmod(c, 4)
+            turned = ps.tile([P, 4, P], F32, name="turned", tag="turn", bufs=4)
+            for term, src in enumerate((halves(pos[c]), soft[c])):
+                for b in range(4):
+                    nc.tensor.matmul(
+                        turned[:, b, :], src[:, half, b * P : (b + 1) * P], ident[:], is_transpose=True,
+                        start=(term == 0 and b == 0), stop=(term == 1 and b == 3),
+                    )
+            copy_on(
+                engine,
+                zt[a][half][:, :, :, cc * 32 : cc * 32 + 32, :],
+                turned[:].rearrange("m b (p u e) -> m b u p e", u=2, e=2),
+            )
+
+        def quantise_z(a, half, engines):
+            woven = sb.tile([P, BANK, 2], F32, name="woven", tag="woven", bufs=2, align_bytes=64)
+            for pair in range(2):
+                back = ps.tile([P, 2, 2, P], F32, name="back", tag="turn", bufs=4)
+                for b in range(2):
+                    for u in range(2):
+                        src = zt[a][half][:, pair * 2 + b, u, :, :].rearrange("m p e -> m (p e)").bitcast(F32)
+                        nc.tensor.transpose(back[:, b, u, :], src, ident[:])
+                copy_on(
+                    engines[pair],
+                    woven[:, pair * 256 : (pair + 1) * 256, :].rearrange("p (b m) u -> p b m u", b=2),
+                    back[:].rearrange("p b u m -> p b m u"),
+                )
+            cols = slice(half * BANK, (half + 1) * BANK)
+            nc.vector.quantize_mx(
+                out=zc[a][:, cols].bitcast(FP8X4), scales=zs[a][:, cols],
+                in_=woven[:].rearrange("p m u -> p (m u)").bitcast(BF16),
+            )
+
+        def second_pass(acc, a, nt, half):
+            cols = slice(half * BANK, (half + 1) * BANK)
+            nc.tensor.matmul_mx(
+                out=acc[:],
+                lhsT=w2c[:, a, nt * 2 * P : (nt + 1) * 2 * P].bitcast(FP4X4),
+                lhsT_scale=w2s[:, a, nt * P : (nt + 1) * P],
+                rhs=zc[a][:, cols].bitcast(FP8X4),
+                rhs_scale=zs[a][:, cols],
+                start=(a == 0),
+                stop=(a == 1),
+            )
+
+        nc.vector.memset(planes[:].bitcast(I32), 0)
+        nc.sync.dma_start(list1[:], offs)
+        nc.sync.dma_start(out=words[0][:], in_=tab_words[0].rearrange("p t i -> p (t i)").bitcast(I32))
+        for q in range(4):
+            nc.scalar.dma_start(
+                out=planes[32 * q : 32 * q + 8, :].bitcast(I32), in_=tab_scales[:, 4 * q : 4 * q + 4, :].bitcast(I32)
+            )
+        load_w1(W1_BLOCKS[0])
+        nc.sync.dma_start(out=words[1][:], in_=tab_words[1].rearrange("p t i -> p (t i)").bitcast(I32))
+        nc.sync.dma_start(out=weights[:, :BANK], in_=wgs[:, :BANK])
+        load_page(0)
+        nc.sync.dma_start(list2[:], offs2)
+        nc.sync.dma_start(out=weights[:, BANK:], in_=wgs[:, BANK:])
+        nc.sync.dma_start(list3[:], offs3)
+        load_w1(W1_BLOCKS[1])
+        load_page(1)
+
+        make_identity(nc, ident[:])
+        nc.gpsimd.memset(gain_rows[:], 0.0)
+        nc.gpsimd.memset(w2s[:].rearrange("p a n -> p (a n)").bitcast(I32), 0)
+        nc.sync.dma_start(out=gain_rows[0:TILES, :], in_=gain.rearrange("(c p) -> c p", p=P))
+
+        nc.vector.tensor_copy(picked[0][:], words[0][:].bitcast(U32).indirect(list1[:]))
+        nc.vector.tensor_copy(picked_scales[:], planes[:].indirect(list1[:]))
+        q0 = quantise_w1(0, first_stage[:])
+        for half in range(2):
+            nc.vector.tensor_copy(
+                picked[1][:, half * BANK : (half + 1) * BANK],
+                words[1][:].bitcast(U32).indirect(list1[:, half * 32 : (half + 1) * 32]),
+            )
+        hs[0], hs[1], xs[0] = ring[0], ring[1], ring[2]
+        first_product(0, *q0)
+
+        gain_t = ps.tile([P, P], F32, name="gain_t", tag="turn", bufs=4)
+        nc.tensor.transpose(gain_t[:], gain_rows[:], ident[:])
+        nc.scalar.copy(out=gain_cols[:], in_=gain_t[:, 0:TILES])
+
+        group_of = {c: g for g in LN_GROUPS for c in g}
+        group_tile = {}
+        accs = {}
+        quantised = {}
+        last = TILES - 1
+        for c in range(TILES):
+            if c < 2:
+                scatter(c, 0, BANK)
+                scatter(c, BANK, S)
+            else:
+                scatter(c, 0, S)
+            if c == 0:
+                for i in range(2):
+                    quantised[1 + i] = quantise_w1(1 + i, xs[0][:].bitcast(BF16)[:, i * 1024 : (i + 1) * 1024])
+                first_product(1, *quantised[1])
+            for block in W1_BLOCKS[2:]:
+                if block[0] == c + 3:
+                    load_w1(block)
+            if c + 2 < TILES:
+                load_page(c + 2)
+            load_stock(c)
+            if c == 1:
+                for a in range(2):
+                    nc.sync.dma_start(out=w2c[:, a, :].bitcast(I32), in_=w2_words[a].bitcast(I32))
+                for q in range(4):
+                    nc.sync.dma_start(
+                        out=w2s[32 * q : 32 * q + 4, :, :].bitcast(I32),
+                        in_=w2_scales[:, 4 * q : 4 * q + 4, :].rearrange("a r n -> r a n").bitcast(I32),
+                    )
+            if c == last:
+                break
+            if c + 3 < TILES:
+                quantised[c + 3] = quantise_w1(c + 3, hs[c][:].bitcast(BF16)[:, 0:1024])
+            xs[c + 1] = hs[c]
+            gather(c, 0, NP)
+            if c == 4:
+                for d in LN_GROUPS[0]:
+                    minus_stock(d, 0, 2)
+                    if d == 0:
+                        hs[5] = stocks[0]
+                        first_product(5, *quantised[5])
+                for d in LN_GROUPS[0]:
+                    for half in range(2):
+                        sum_and_round(d, half, "scalar")
+                for half in range(2):
+                    quantise_z(0, half, ("scalar", "scalar"))
+            g = group_of[c]
+            if c == g[0]:
+                group_tile[g] = sb.tile([P, len(g) * NP], F32, name="soft", tag="soft", bufs=2)
+                for i, d in enumerate(g):
+                    if last in g:
+                        soft[d] = group_tile[g][:].rearrange("p (h i m) -> p i h m", h=2, i=len(g))[:, i, :, :]
+                    else:
+                        soft[d] = group_tile[g][:].rearrange("p (i h m) -> p i h m", h=2, i=len(g))[:, i, :, :]
+            pos[c] = sb.tile([P, NP], F32, name="pos", tag="pos", bufs=5)
+            gain_c = gain_cols[:, c : c + 1]
+            nc.scalar.activation(out=soft[c], in_=halves(xs[c]), func=ACT.Abs)
+            nc.scalar.activation(out=pos[c][:, :BANK], in_=xs[c][:, :BANK], func=ACT.Relu, scale=gain_c)
+            nc.scalar.activation(out=soft[c], in_=soft[c], func=ACT.Exp, scale=-1.0)
+            nc.scalar.activation(out=pos[c][:, BANK:], in_=xs[c][:, BANK:], func=ACT.Relu, scale=gain_c)
+            if c + 2 < TILES and c + 2 != 5:
+                hs[c + 2] = xs[c]
+                first_product(c + 2, *quantised[c + 2])
+            if c == g[-1]:
+                nc.scalar.activation(out=group_tile[g][:], in_=group_tile[g][:], func=ACT.Ln, bias=1.0)
+
+        for nt in range(4):
+            accs[nt, 0] = ps.tile([P, BANK], F32, name="res", tag=("res", "acc")[nt // 2], bufs=2)
+            second_pass(accs[nt, 0], 0, nt, 0)
+
+        pos[last] = sb.tile([P, NP], F32, name="pos", tag="pos", bufs=5)
+        for half in range(2):
+            gather(last, half * BANK, (half + 1) * BANK)
+            nc.scalar.activation(out=soft[last][:, half, :], in_=halves(xs[last])[:, half, :], func=ACT.Abs)
+        for half in range(2):
+            nc.scalar.activation(out=soft[last][:, half, :], in_=soft[last][:, half, :], func=ACT.Exp, scale=-1.0)
+        both = group_tile[LN_GROUPS[-1]]
+        for half in range(2):
+            cols = slice(half * NP, (half + 1) * NP)
+            nc.scalar.activation(out=both[:, cols], in_=both[:, cols], func=ACT.Ln, bias=1.0)
+        nc.vector.tensor_scalar(
+            out=pos[last][:], in0=xs[last][:], scalar1=0.0, scalar2=gain_cols[:, last : last + 1],
+            op0=ALU.max, op1=ALU.mult,
+        )
+        for d in LN_GROUPS[1]:
+            minus_stock(d, 0, 2)
+        for d, half, engine in ((4, 0, "vector"), (5, 0, "vector"), (4, 1, "vector"), (5, 1, "scalar")):
+            sum_and_round(d, half, engine)
+        rounders = (("scalar", "scalar"), ("vector", "scalar"))
+        for half in range(2):
+            for d in LN_GROUPS[2]:
+                minus_stock(d, half, half + 1)
+            for d in LN_GROUPS[2]:
+                sum_and_round(d, half, rounders[half][d - 6])
+        movers = (("scalar", "scalar", "vector", "scalar"), ("vector", "scalar", "vector", "scalar"))
+        for half in range(2):
+            quantise_z(1, half, ("scalar", "vector"))
+        for half in range(2):
+            for nt in range(4):
+                if half == 1:
+                    accs[nt, half] = ps.tile([P, BANK], F32, name="res_b", tag="turn", bufs=4)
+                    second_pass(accs[nt, half], 0, nt, half)
+                second_pass(accs[nt, half], 1, nt, half)
+                staged = sb.tile([P, BANK], F32, name="staged", tag="staged", bufs=4)
+                copy_on(movers[half][nt], staged[:], accs[nt, half][:])
+                nc.sync.dma_start(out=out[nt * P : (nt + 1) * P, half * BANK : (half + 1) * BANK], in_=staged[:])

@@ -21,6 +21,8 @@ P = 128
 BANK = 512
 TILES = H // P
 W1_BLOCKS = ((0,), (1, 2), (3, 4), (5, 6), (7,))
+BANKS = {"turn": 4, "acc": 2, "res": 2}
+LAST_PIECES = ((0, 512), (512, 768), (768, 1024))
 LN_GROUPS = ((0, 1, 2, 3), (4, 5), (6, 7))
 
 
@@ -36,8 +38,8 @@ def tile_list_vaccine_dispatch_kernel(
         list2 = sb.tile([P, S // 16], U16, name="list2")
         list3 = sb.tile([P, NP // 16], U16, name="list3")
         words = [sb.tile([P, T], I32, name=f"words{a}") for a in range(2)]
-        planes = sb.tile([P, T], U8, name="planes")
-        picked = [sb.tile([P, S], U32, name=f"picked{a}", align_bytes=64) for a in range(2)]
+        planes = sb.tile([P, T], U8, name="planes", tag="planes", align_bytes=64)
+        picked = [sb.tile([P, S], U32, name="picked0", align_bytes=64)]
         picked_scales = sb.tile([P, S], U8, name="picked_scales", align_bytes=64)
         weights = sb.tile([P, S], F32, name="weights")
         w2c = sb.tile([P, 2, 2 * N], U8, name="w2c", align_bytes=64)
@@ -48,7 +50,8 @@ def tile_list_vaccine_dispatch_kernel(
         first_stage = sb.tile([P, 2 * P * 4], BF16, name="first_stage", align_bytes=64)
 
         raw, pages, stocks, hs, xs, soft, pos = {}, {}, {}, {}, {}, {}, {}
-        ring = [sb.tile([P, S], F32, name=f"ring{i}", align_bytes=64) for i in range(4)]
+        ring = [sb.tile([P, S], F32, name=f"ring{i}", align_bytes=64) for i in range(3)]
+        first = sb.tile([P, S + BANK], F32, name="first", align_bytes=64)
 
         def load_w1(block):
             width = len(block) * P
@@ -65,7 +68,7 @@ def tile_list_vaccine_dispatch_kernel(
 
         def load_stock(c):
             if c == 0:
-                stocks[c] = ring[3]
+                stocks[c] = ring[2]
             else:
                 stocks[c] = sb.tile([P, NP], F32, name="stock", tag="stock", bufs=4)
             nc.sync.dma_start(out=stocks[c][:], in_=stock[c * P : (c + 1) * P, :])
@@ -75,8 +78,8 @@ def tile_list_vaccine_dispatch_kernel(
                 out=stage.rearrange("p (a c i t) -> p a c t i", a=2, i=4, t=4),
                 in_=raw[c].rearrange("p a t (c i) -> p a c t i", i=4),
             )
-            codes = sb.tile([P, 2 * P], U32, name="w1c", tag="w1c", bufs=3, align_bytes=64)
-            scales = sb.tile([P, 2 * P], U8, name="w1s", tag="w1s", bufs=3, align_bytes=64)
+            codes = sb.tile([P, 2 * P], U32, name="w1c", tag="w1c", bufs=5, align_bytes=64)
+            scales = sb.tile([P, 2 * P], U8, name="w1s", tag="w1s", bufs=5, align_bytes=64)
             nc.vector.quantize_mx(out=codes[:].bitcast(FP8X4), scales=scales[:], in_=stage)
             return codes, scales
 
@@ -114,6 +117,10 @@ def tile_list_vaccine_dispatch_kernel(
             else:
                 nc.vector.tensor_copy(out=dst, in_=src)
 
+        def log_one_plus(t):
+            for half in range(2):
+                nc.scalar.activation(out=halves(t)[:, half, :], in_=halves(t)[:, half, :], func=ACT.Ln, bias=1.0)
+
         def halves(t):
             return t[:].rearrange("p (h m) -> p h m", h=2)
 
@@ -123,9 +130,9 @@ def tile_list_vaccine_dispatch_kernel(
                 in1=halves(stocks[c])[:, lo:hi, :], op0=ALU.mult, op1=ALU.subtract,
             )
 
-        def sum_and_round(c, half, engine):
+        def sum_and_round(c, half, engine, tag):
             a, cc = divmod(c, 4)
-            turned = ps.tile([P, 4, P], F32, name="turned", tag="turn", bufs=4)
+            turned = ps.tile([P, 4, P], F32, name="turned", tag=tag, bufs=BANKS[tag])
             for term, src in enumerate((halves(pos[c]), soft[c])):
                 for b in range(4):
                     nc.tensor.matmul(
@@ -169,11 +176,11 @@ def tile_list_vaccine_dispatch_kernel(
                 stop=(a == 1),
             )
 
-        nc.vector.memset(planes[:].bitcast(I32), 0)
+        nc.gpsimd.memset(planes[:].bitcast(I32), 0)
         nc.sync.dma_start(list1[:], offs)
         nc.sync.dma_start(out=words[0][:], in_=tab_words[0].rearrange("p t i -> p (t i)").bitcast(I32))
         for q in range(4):
-            nc.scalar.dma_start(
+            nc.gpsimd.dma_start(
                 out=planes[32 * q : 32 * q + 8, :].bitcast(I32), in_=tab_scales[:, 4 * q : 4 * q + 4, :].bitcast(I32)
             )
         load_w1(W1_BLOCKS[0])
@@ -183,26 +190,27 @@ def tile_list_vaccine_dispatch_kernel(
         nc.sync.dma_start(list2[:], offs2)
         nc.sync.dma_start(out=weights[:, BANK:], in_=wgs[:, BANK:])
         nc.sync.dma_start(list3[:], offs3)
+        nc.gpsimd.memset(gain_rows[:], 0.0)
+        nc.sync.dma_start(out=gain_rows[0:TILES, :], in_=gain.rearrange("(c p) -> c p", p=P))
         load_w1(W1_BLOCKS[1])
         load_page(1)
 
         make_identity(nc, ident[:])
-        nc.gpsimd.memset(gain_rows[:], 0.0)
         nc.gpsimd.memset(w2s[:].rearrange("p a n -> p (a n)").bitcast(I32), 0)
-        nc.sync.dma_start(out=gain_rows[0:TILES, :], in_=gain.rearrange("(c p) -> c p", p=P))
 
         nc.vector.tensor_copy(picked[0][:], words[0][:].bitcast(U32).indirect(list1[:]))
         nc.vector.tensor_copy(picked_scales[:], planes[:].indirect(list1[:]))
         q0 = quantise_w1(0, first_stage[:])
+        picked.append(sb.tile([P, S], U32, name="picked1", tag="planes", align_bytes=64))
         for half in range(2):
             nc.vector.tensor_copy(
                 picked[1][:, half * BANK : (half + 1) * BANK],
                 words[1][:].bitcast(U32).indirect(list1[:, half * 32 : (half + 1) * 32]),
             )
-        hs[0], hs[1], xs[0] = ring[0], ring[1], ring[2]
+        hs[0], hs[1], hs[2], xs[0] = first[:, BANK:], ring[0], ring[1], first[:, :S]
         first_product(0, *q0)
 
-        gain_t = ps.tile([P, P], F32, name="gain_t", tag="turn", bufs=4)
+        gain_t = ps.tile([P, P], F32, name="gain_t", tag="acc", bufs=2)
         nc.tensor.transpose(gain_t[:], gain_rows[:], ident[:])
         nc.scalar.copy(out=gain_cols[:], in_=gain_t[:, 0:TILES])
 
@@ -217,13 +225,8 @@ def tile_list_vaccine_dispatch_kernel(
                 scatter(c, BANK, S)
             else:
                 scatter(c, 0, S)
-            if c == 0:
-                for i in range(2):
-                    quantised[1 + i] = quantise_w1(1 + i, xs[0][:].bitcast(BF16)[:, i * 1024 : (i + 1) * 1024])
-                first_product(1, *quantised[1])
-            for block in W1_BLOCKS[2:]:
-                if block[0] == c + 3:
-                    load_w1(block)
+            if c + 2 < len(W1_BLOCKS):
+                load_w1(W1_BLOCKS[c + 2])
             if c + 2 < TILES:
                 load_page(c + 2)
             load_stock(c)
@@ -237,29 +240,28 @@ def tile_list_vaccine_dispatch_kernel(
                     )
             if c == last:
                 break
-            if c + 3 < TILES:
-                quantised[c + 3] = quantise_w1(c + 3, hs[c][:].bitcast(BF16)[:, 0:1024])
+            if c + 1 < len(W1_BLOCKS):
+                for i, d in enumerate(W1_BLOCKS[c + 1]):
+                    quantised[d] = quantise_w1(d, hs[c][:].bitcast(BF16)[:, i * 1024 : (i + 1) * 1024])
+                    if d == 1:
+                        first_product(1, *quantised[1])
             xs[c + 1] = hs[c]
             gather(c, 0, NP)
             if c == 4:
-                for d in LN_GROUPS[0]:
-                    minus_stock(d, 0, 2)
-                    if d == 0:
-                        hs[5] = stocks[0]
-                        first_product(5, *quantised[5])
-                for d in LN_GROUPS[0]:
-                    for half in range(2):
-                        sum_and_round(d, half, "scalar")
                 for half in range(2):
+                    for d in LN_GROUPS[0]:
+                        minus_stock(d, half, half + 1)
+                hs[5] = stocks[0]
+                first_product(5, *quantised[5])
+                for half in range(2):
+                    for d in LN_GROUPS[0]:
+                        sum_and_round(d, half, "scalar", "turn")
                     quantise_z(0, half, ("scalar", "scalar"))
             g = group_of[c]
             if c == g[0]:
                 group_tile[g] = sb.tile([P, len(g) * NP], F32, name="soft", tag="soft", bufs=2)
                 for i, d in enumerate(g):
-                    if last in g:
-                        soft[d] = group_tile[g][:].rearrange("p (h i m) -> p i h m", h=2, i=len(g))[:, i, :, :]
-                    else:
-                        soft[d] = group_tile[g][:].rearrange("p (i h m) -> p i h m", h=2, i=len(g))[:, i, :, :]
+                    soft[d] = group_tile[g][:].rearrange("p (h i m) -> p i h m", h=2, i=len(g))[:, i, :, :]
             pos[c] = sb.tile([P, NP], F32, name="pos", tag="pos", bufs=5)
             gain_c = gain_cols[:, c : c + 1]
             nc.scalar.activation(out=soft[c], in_=halves(xs[c]), func=ACT.Abs)
@@ -267,39 +269,38 @@ def tile_list_vaccine_dispatch_kernel(
             nc.scalar.activation(out=soft[c], in_=soft[c], func=ACT.Exp, scale=-1.0)
             nc.scalar.activation(out=pos[c][:, BANK:], in_=xs[c][:, BANK:], func=ACT.Relu, scale=gain_c)
             if c + 2 < TILES and c + 2 != 5:
-                hs[c + 2] = xs[c]
+                if c > 0:
+                    hs[c + 2] = xs[c]
                 first_product(c + 2, *quantised[c + 2])
             if c == g[-1]:
-                nc.scalar.activation(out=group_tile[g][:], in_=group_tile[g][:], func=ACT.Ln, bias=1.0)
-
-        for nt in range(4):
-            accs[nt, 0] = ps.tile([P, BANK], F32, name="res", tag=("res", "acc")[nt // 2], bufs=2)
-            second_pass(accs[nt, 0], 0, nt, 0)
+                log_one_plus(group_tile[g])
 
         pos[last] = sb.tile([P, NP], F32, name="pos", tag="pos", bufs=5)
-        for half in range(2):
-            gather(last, half * BANK, (half + 1) * BANK)
-            nc.scalar.activation(out=soft[last][:, half, :], in_=halves(xs[last])[:, half, :], func=ACT.Abs)
-        for half in range(2):
-            nc.scalar.activation(out=soft[last][:, half, :], in_=soft[last][:, half, :], func=ACT.Exp, scale=-1.0)
-        both = group_tile[LN_GROUPS[-1]]
-        for half in range(2):
-            cols = slice(half * NP, (half + 1) * NP)
-            nc.scalar.activation(out=both[:, cols], in_=both[:, cols], func=ACT.Ln, bias=1.0)
+        pieces = [soft[last][:, lo // BANK, lo % BANK : (hi - 1) % BANK + 1] for lo, hi in LAST_PIECES]
+        for i, (lo, hi) in enumerate(LAST_PIECES):
+            gather(last, lo, hi)
+            nc.scalar.activation(out=pieces[i], in_=xs[last][:, lo:hi], func=ACT.Abs)
+            if i > 0:
+                nc.scalar.activation(out=pieces[i - 1], in_=pieces[i - 1], func=ACT.Exp, scale=-1.0)
+        nc.scalar.activation(out=pieces[-1], in_=pieces[-1], func=ACT.Exp, scale=-1.0)
+        log_one_plus(group_tile[LN_GROUPS[-1]])
         nc.vector.tensor_scalar(
             out=pos[last][:], in0=xs[last][:], scalar1=0.0, scalar2=gain_cols[:, last : last + 1],
             op0=ALU.max, op1=ALU.mult,
         )
         for d in LN_GROUPS[1]:
             minus_stock(d, 0, 2)
-        for d, half, engine in ((4, 0, "vector"), (5, 0, "vector"), (4, 1, "vector"), (5, 1, "scalar")):
-            sum_and_round(d, half, engine)
-        rounders = (("scalar", "scalar"), ("vector", "scalar"))
+        rounders = (("vector", "scalar"), ("vector", "scalar"))
         for half in range(2):
+            for d in LN_GROUPS[1]:
+                sum_and_round(d, half, ("vector", "scalar")[half], ("res", "acc")[half])
+            for nt in range(2 * half, 2 * half + 2):
+                accs[nt, 0] = ps.tile([P, BANK], F32, name="res", tag=("res", "acc")[half], bufs=2)
+                second_pass(accs[nt, 0], 0, nt, 0)
             for d in LN_GROUPS[2]:
                 minus_stock(d, half, half + 1)
             for d in LN_GROUPS[2]:
-                sum_and_round(d, half, rounders[half][d - 6])
+                sum_and_round(d, half, rounders[half][d - 6], "turn")
         movers = (("scalar", "scalar", "vector", "scalar"), ("vector", "scalar", "vector", "scalar"))
         for half in range(2):
             quantise_z(1, half, ("scalar", "vector"))
@@ -309,6 +310,6 @@ def tile_list_vaccine_dispatch_kernel(
                     accs[nt, half] = ps.tile([P, BANK], F32, name="res_b", tag="turn", bufs=4)
                     second_pass(accs[nt, half], 0, nt, half)
                 second_pass(accs[nt, half], 1, nt, half)
-                staged = sb.tile([P, BANK], F32, name="staged", tag="staged", bufs=4)
+                staged = sb.tile([P, BANK], F32, name="staged", tag="staged", bufs=8)
                 copy_on(movers[half][nt], staged[:], accs[nt, half][:])
                 nc.sync.dma_start(out=out[nt * P : (nt + 1) * P, half * BANK : (half + 1) * BANK], in_=staged[:])

@@ -23,7 +23,9 @@ TILES = H // P
 W1_BLOCKS = ((0,), (1, 2), (3, 4), (5, 6), (7,))
 BANKS = {"turn": 4, "acc": 2, "res": 2}
 LAST_PIECES = ((0, 512), (512, 768), (768, 1024))
-LN_GROUPS = ((0, 1, 2, 3), (4, 5), (6, 7))
+FUSED = 2
+STAGED = {0: (1, 2, 3), 1: (4, 5), 2: (6, 7)}
+LN_GROUPS = ((0, 1), (2, 3), (4, 5), (6, 7))
 
 
 def tile_list_vaccine_dispatch_kernel(
@@ -37,7 +39,7 @@ def tile_list_vaccine_dispatch_kernel(
         list1 = sb.tile([P, S // 16], U16, name="list1")
         list2 = sb.tile([P, S // 16], U16, name="list2")
         list3 = sb.tile([P, NP // 16], U16, name="list3")
-        words = [sb.tile([P, T], I32, name=f"words{a}") for a in range(2)]
+        words = [sb.tile([P, T], I32, name=f"words{a}", tag=f"wide{a}") for a in range(2)]
         planes = sb.tile([P, T], U8, name="planes", tag="planes", align_bytes=64)
         picked = [sb.tile([P, S], U32, name="picked0", align_bytes=64)]
         picked_scales = sb.tile([P, S], U8, name="picked_scales", align_bytes=64)
@@ -50,7 +52,7 @@ def tile_list_vaccine_dispatch_kernel(
         first_stage = sb.tile([P, 2 * P * 4], BF16, name="first_stage", align_bytes=64)
 
         raw, pages, stocks, hs, xs, soft, pos = {}, {}, {}, {}, {}, {}, {}
-        ring = [sb.tile([P, S], F32, name=f"ring{i}", align_bytes=64) for i in range(3)]
+        ring = [sb.tile([P, S], F32, name=f"ring{i}", align_bytes=64) for i in range(2)]
         first = sb.tile([P, S + BANK], F32, name="first", align_bytes=64)
 
         def load_w1(block):
@@ -67,10 +69,7 @@ def tile_list_vaccine_dispatch_kernel(
             nc.sync.dma_start(out=pages[c][:], in_=page0[c * P : (c + 1) * P, :])
 
         def load_stock(c):
-            if c == 0:
-                stocks[c] = ring[2]
-            else:
-                stocks[c] = sb.tile([P, NP], F32, name="stock", tag="stock", bufs=4)
+            stocks[c] = sb.tile([P, NP], F32, name="stock", tag="stock", bufs=5)
             nc.sync.dma_start(out=stocks[c][:], in_=stock[c * P : (c + 1) * P, :])
 
         def quantise_w1(c, stage):
@@ -84,6 +83,10 @@ def tile_list_vaccine_dispatch_kernel(
             return codes, scales
 
         def first_product(c, codes, scales):
+            if c < FUSED:
+                sums = hs[c]
+            else:
+                sums = sb.tile([P, S], F32, name="sums", tag="sums", bufs=2)
             for half in range(2):
                 cols = slice(half * BANK, (half + 1) * BANK)
                 acc = ps.tile([P, BANK], F32, name="acc", tag="acc", bufs=2)
@@ -97,7 +100,8 @@ def tile_list_vaccine_dispatch_kernel(
                         start=(a == 0),
                         stop=(a == 1),
                     )
-                nc.scalar.copy(out=hs[c][:, cols], in_=acc[:])
+                nc.scalar.copy(out=sums[:, cols], in_=acc[:])
+            return sums
 
         def scatter(c, lo, hi):
             nc.vector.tensor_tensor(
@@ -130,14 +134,20 @@ def tile_list_vaccine_dispatch_kernel(
                 in1=halves(stocks[c])[:, lo:hi, :], op0=ALU.mult, op1=ALU.subtract,
             )
 
+        def times(t, factor):
+            nc.gpsimd.tensor_scalar(out=t, in0=t, scalar1=factor, scalar2=0.0, op0=ALU.mult, op1=ALU.add)
+
         def sum_and_round(c, half, engine, tag):
             a, cc = divmod(c, 4)
             turned = ps.tile([P, 4, P], F32, name="turned", tag=tag, bufs=BANKS[tag])
-            for term, src in enumerate((halves(pos[c]), soft[c])):
+            terms = [halves(pos[c]), soft[c]]
+            if c not in LN_GROUPS[-1]:
+                terms = [halves(stocks[c])] + terms
+            for term, src in enumerate(terms):
                 for b in range(4):
                     nc.tensor.matmul(
                         turned[:, b, :], src[:, half, b * P : (b + 1) * P], ident[:], is_transpose=True,
-                        start=(term == 0 and b == 0), stop=(term == 1 and b == 3),
+                        start=(term == 0 and b == 0), stop=(term == len(terms) - 1 and b == 3),
                     )
             copy_on(
                 engine,
@@ -220,11 +230,11 @@ def tile_list_vaccine_dispatch_kernel(
         quantised = {}
         last = TILES - 1
         for c in range(TILES):
-            if c < 2:
+            if c < FUSED:
                 scatter(c, 0, BANK)
                 scatter(c, BANK, S)
             else:
-                scatter(c, 0, S)
+                nc.vector.tensor_copy(pages[c][:].indirect(list2[:]), hs[c][:])
             if c + 2 < len(W1_BLOCKS):
                 load_w1(W1_BLOCKS[c + 2])
             if c + 2 < TILES:
@@ -240,40 +250,44 @@ def tile_list_vaccine_dispatch_kernel(
                     )
             if c == last:
                 break
-            if c + 1 < len(W1_BLOCKS):
-                for i, d in enumerate(W1_BLOCKS[c + 1]):
-                    quantised[d] = quantise_w1(d, hs[c][:].bitcast(BF16)[:, i * 1024 : (i + 1) * 1024])
-                    if d == 1:
-                        first_product(1, *quantised[1])
+            for d in STAGED.get(c, ()):
+                i = min(d - STAGED[c][0], 1)
+                quantised[d] = quantise_w1(d, hs[c][:].bitcast(BF16)[:, i * 1024 : (i + 1) * 1024])
+                if d == 1:
+                    first_product(1, *quantised[1])
+            if c + 2 < TILES:
+                sums = first_product(c + 2, *quantised[c + 2])
             xs[c + 1] = hs[c]
             gather(c, 0, NP)
-            if c == 4:
-                for half in range(2):
-                    for d in LN_GROUPS[0]:
-                        minus_stock(d, half, half + 1)
-                hs[5] = stocks[0]
-                first_product(5, *quantised[5])
-                for half in range(2):
-                    for d in LN_GROUPS[0]:
-                        sum_and_round(d, half, "scalar", "turn")
-                    quantise_z(0, half, ("scalar", "scalar"))
             g = group_of[c]
             if c == g[0]:
-                group_tile[g] = sb.tile([P, len(g) * NP], F32, name="soft", tag="soft", bufs=2)
+                group_tile[g] = sb.tile([P, len(g) * NP], F32, name="soft", tag=f"wide{LN_GROUPS.index(g) % 2}")
                 for i, d in enumerate(g):
                     soft[d] = group_tile[g][:].rearrange("p (h i m) -> p i h m", h=2, i=len(g))[:, i, :, :]
             pos[c] = sb.tile([P, NP], F32, name="pos", tag="pos", bufs=5)
             gain_c = gain_cols[:, c : c + 1]
             nc.scalar.activation(out=soft[c], in_=halves(xs[c]), func=ACT.Abs)
-            nc.scalar.activation(out=pos[c][:, :BANK], in_=xs[c][:, :BANK], func=ACT.Relu, scale=gain_c)
-            nc.scalar.activation(out=soft[c], in_=soft[c], func=ACT.Exp, scale=-1.0)
-            nc.scalar.activation(out=pos[c][:, BANK:], in_=xs[c][:, BANK:], func=ACT.Relu, scale=gain_c)
-            if c + 2 < TILES and c + 2 != 5:
+            nc.scalar.activation(out=pos[c][:], in_=xs[c][:], func=ACT.Relu, scale=gain_c)
+            for half in range(2):
+                nc.scalar.activation(out=soft[c][:, half, :], in_=soft[c][:, half, :], func=ACT.Exp, scale=-1.0)
+            if c + 2 < TILES:
                 if c > 0:
                     hs[c + 2] = xs[c]
-                first_product(c + 2, *quantised[c + 2])
+                nc.gpsimd.tensor_tensor(hs[c + 2][:], sums[:], weights[:], ALU.mult)
+            if c not in LN_GROUPS[-1]:
+                times(stocks[c][:], -1.0)
             if c == g[-1]:
                 log_one_plus(group_tile[g])
+                for half in range(2):
+                    for d in g:
+                        times(soft[d][:, half, :], gain_cols[:, d : d + 1])
+            if c in (2, 4):
+                for half in range(2):
+                    for d in (c - 2, c - 1):
+                        sum_and_round(d, half, "scalar", "turn")
+            if c == 4:
+                for half in range(2):
+                    quantise_z(0, half, ("scalar", "scalar"))
 
         pos[last] = sb.tile([P, NP], F32, name="pos", tag="pos", bufs=5)
         pieces = [soft[last][:, lo // BANK, lo % BANK : (hi - 1) % BANK + 1] for lo, hi in LAST_PIECES]
@@ -288,18 +302,17 @@ def tile_list_vaccine_dispatch_kernel(
             out=pos[last][:], in0=xs[last][:], scalar1=0.0, scalar2=gain_cols[:, last : last + 1],
             op0=ALU.max, op1=ALU.mult,
         )
-        for d in LN_GROUPS[1]:
-            minus_stock(d, 0, 2)
-        rounders = (("vector", "scalar"), ("vector", "scalar"))
         for half in range(2):
-            for d in LN_GROUPS[1]:
-                sum_and_round(d, half, ("vector", "scalar")[half], ("res", "acc")[half])
+            for d in LN_GROUPS[2]:
+                sum_and_round(d, half, "vector", ("res", "acc")[half])
             for nt in range(2 * half, 2 * half + 2):
                 accs[nt, 0] = ps.tile([P, BANK], F32, name="res", tag=("res", "acc")[half], bufs=2)
                 second_pass(accs[nt, 0], 0, nt, 0)
-            for d in LN_GROUPS[2]:
+        rounders = (("vector", "scalar"), ("vector", "scalar"))
+        for half in range(2):
+            for d in LN_GROUPS[3]:
                 minus_stock(d, half, half + 1)
-            for d in LN_GROUPS[2]:
+            for d in LN_GROUPS[3]:
                 sum_and_round(d, half, rounders[half][d - 6], "turn")
         movers = (("scalar", "scalar", "vector", "scalar"), ("vector", "scalar", "vector", "scalar"))
         for half in range(2):

@@ -20,12 +20,10 @@ ACT = mybir.ActivationFunctionType
 P = 128
 BANK = 512
 TILES = H // P
-W1_BLOCKS = ((0,), (1, 2), (3, 4), (5, 6), (7,))
+W1_BLOCKS = ((0,), (1, 2), (3, 4), (5, 6, 7))
 BANKS = {"turn": 4, "acc": 2, "res": 2}
-LAST_PIECES = ((0, 512), (512, 768), (768, 1024))
-FUSED = 2
-STAGED = {0: (1, 2, 3), 1: (4, 5), 2: (6, 7)}
-LN_GROUPS = ((0, 1), (2, 3), (4, 5), (6, 7))
+LN_GROUPS = ((0, 1, 2), (3, 4), (5, 6))
+KNEE = 30.0
 
 
 def tile_list_vaccine_dispatch_kernel(
@@ -34,6 +32,9 @@ def tile_list_vaccine_dispatch_kernel(
     nc = tc.nc
     with ExitStack() as ctx:
         sb = ctx.enter_context(tc.tile_pool(name="sb", bufs=1))
+        shared = ctx.enter_context(tc.tile_pool(name="shared", bufs=1))
+        streamed = ctx.enter_context(tc.tile_pool(name="streamed", bufs=1))
+        logs = ctx.enter_context(tc.tile_pool(name="logs", bufs=1))
         ps = ctx.enter_context(tc.psum_pool(name="ps", bufs=1))
 
         list1 = sb.tile([P, S // 16], U16, name="list1")
@@ -48,16 +49,20 @@ def tile_list_vaccine_dispatch_kernel(
         w2s = sb.tile([P, 2, N], U8, name="w2s", align_bytes=64)
         ident = sb.tile([P, P], F32, name="ident")
         gain_rows = sb.tile([P, P], F32, name="gain_rows")
-        gain_cols = sb.tile([P, TILES], F32, name="gain_cols")
-        first_stage = sb.tile([P, 2 * P * 4], BF16, name="first_stage", align_bytes=64)
+        factor = {
+            name: sb.tile([P, TILES], F32, name=name)
+            for name in ("gain", "minus_gain", "half_gain", "minus_half_gain", "inverse", "minus_two_inverse")
+        }
 
-        raw, pages, stocks, hs, xs, soft, pos = {}, {}, {}, {}, {}, {}, {}
-        ring = [sb.tile([P, S], F32, name=f"ring{i}", align_bytes=64) for i in range(2)]
-        first = sb.tile([P, S + BANK], F32, name="first", align_bytes=64)
+        raw, pages, stocks, quantised = {}, {}, {}, {}
+        sums, put, got, soft, size, signed = {}, {}, {}, {}, {}, {}
+
+        def half_cols(half):
+            return slice(half * BANK, (half + 1) * BANK)
 
         def load_w1(block):
             width = len(block) * P
-            t = sb.tile([P, 2, 4, width], F32, name="w1_raw", tag="w1_raw", bufs=2)
+            t = streamed.tile([P, 2, 4, width], F32, name=f"w1_raw{block[0]}", offset=block[0] * 4096)
             for a in range(2):
                 rows = w1[a * BANK : (a + 1) * BANK, block[0] * P : block[0] * P + width]
                 nc.sync.dma_start(out=t[:, a, :, :], in_=rows.rearrange("(p j) c -> p j c", j=4))
@@ -65,30 +70,30 @@ def tile_list_vaccine_dispatch_kernel(
                 raw[c] = t[:, :, :, i * P : (i + 1) * P]
 
         def load_page(c):
-            pages[c] = sb.tile([P, T2], F32, name="page", tag="page", bufs=3)
+            pages[c] = sb.tile([P, T2], F32, name="page", tag="page", bufs=2)
             nc.sync.dma_start(out=pages[c][:], in_=page0[c * P : (c + 1) * P, :])
 
         def load_stock(c):
-            stocks[c] = sb.tile([P, NP], F32, name="stock", tag="stock", bufs=5)
+            stocks[c] = streamed.tile([P, NP], F32, name=f"stock{c}", offset=c * 4096)
             nc.sync.dma_start(out=stocks[c][:], in_=stock[c * P : (c + 1) * P, :])
 
-        def quantise_w1(c, stage):
+        def round_w1(c, stage, i):
             nc.scalar.copy(
-                out=stage.rearrange("p (a c i t) -> p a c t i", a=2, i=4, t=4),
+                out=stage[:, i * 1024 : (i + 1) * 1024].rearrange("p (a c i t) -> p a c t i", a=2, i=4, t=4),
                 in_=raw[c].rearrange("p a t (c i) -> p a c t i", i=4),
             )
-            codes = sb.tile([P, 2 * P], U32, name="w1c", tag="w1c", bufs=5, align_bytes=64)
-            scales = sb.tile([P, 2 * P], U8, name="w1s", tag="w1s", bufs=5, align_bytes=64)
-            nc.vector.quantize_mx(out=codes[:].bitcast(FP8X4), scales=scales[:], in_=stage)
-            return codes, scales
 
-        def first_product(c, codes, scales):
-            if c < FUSED:
-                sums = hs[c]
-            else:
-                sums = sb.tile([P, S], F32, name="sums", tag="sums", bufs=2)
+        def quantise_w1(group, stage):
+            codes = sb.tile([P, len(group) * 2 * P], U32, name=f"w1c{group[0]}", align_bytes=64)
+            scales = sb.tile([P, len(group) * 2 * P], U8, name=f"w1s{group[0]}", align_bytes=64)
+            nc.vector.quantize_mx(out=codes[:].bitcast(FP8X4), scales=scales[:], in_=stage[:])
+            for i, c in enumerate(group):
+                quantised[c] = (codes[:, i * 2 * P : (i + 1) * 2 * P], scales[:, i * 2 * P : (i + 1) * 2 * P])
+
+        def first_product(c):
+            codes, scales = quantised[c]
             for half in range(2):
-                cols = slice(half * BANK, (half + 1) * BANK)
+                cols = half_cols(half)
                 acc = ps.tile([P, BANK], F32, name="acc", tag="acc", bufs=2)
                 for a in range(2):
                     nc.tensor.matmul_mx(
@@ -100,20 +105,29 @@ def tile_list_vaccine_dispatch_kernel(
                         start=(a == 0),
                         stop=(a == 1),
                     )
-                nc.scalar.copy(out=sums[:, cols], in_=acc[:])
-            return sums
+                nc.scalar.copy(out=sums[c][:, cols], in_=acc[:])
 
-        def scatter(c, lo, hi):
+        def weigh_and_scatter(c, pieces):
+            width = S // pieces
+            for lo in range(0, S, width):
+                cols = slice(lo, lo + width)
+                nc.gpsimd.tensor_tensor(put[c][:, cols], sums[c][:, cols], weights[:, cols], ALU.mult)
+                nc.vector.tensor_copy(pages[c][:].indirect(list2[:, lo // 16 : (lo + width) // 16]), put[c][:, cols])
+
+        def fused_scatter(c, lo, hi):
             nc.vector.tensor_tensor(
-                pages[c][:].indirect(list2[:, lo // 16 : hi // 16]), hs[c][:, lo:hi], weights[:, lo:hi], ALU.mult
+                pages[c][:].indirect(list2[:, lo // 16 : hi // 16]), sums[c][:, lo:hi], weights[:, lo:hi], ALU.mult
             )
 
         def gather(c, lo, hi):
-            nc.vector.tensor_copy(xs[c][:, lo:hi], pages[c][:].indirect(list3[:, lo // 16 : hi // 16]))
+            nc.vector.tensor_copy(got[c][:, lo:hi], pages[c][:].indirect(list3[:, lo // 16 : hi // 16]))
 
-        zt = [[sb.tile([P, 4, 2, P, 2], BF16, name=f"zt{a}{half}") for half in range(2)] for a in range(2)]
-        zc = [sb.tile([P, NP], U32, name=f"zc{a}", align_bytes=64) for a in range(2)]
-        zs = [sb.tile([P, NP], U8, name=f"zs{a}", align_bytes=64) for a in range(2)]
+        def times(engine, dst, src, name, c):
+            by = -1.0 if name is None else factor[name][:, c : c + 1]
+            engine.tensor_scalar(out=dst, in0=src, scalar1=by, scalar2=0.0, op0=ALU.mult, op1=ALU.add)
+
+        zt = [[sb.tile([P, 8, P, 2], BF16, name=f"zt{a}{half}") for half in range(2)] for a in range(2)]
+        zc, zs, woven = {}, {}, {}
 
         def copy_on(engine, dst, src):
             if engine == "scalar":
@@ -121,61 +135,49 @@ def tile_list_vaccine_dispatch_kernel(
             else:
                 nc.vector.tensor_copy(out=dst, in_=src)
 
-        def log_one_plus(t):
-            for half in range(2):
-                nc.scalar.activation(out=halves(t)[:, half, :], in_=halves(t)[:, half, :], func=ACT.Ln, bias=1.0)
-
-        def halves(t):
-            return t[:].rearrange("p (h m) -> p h m", h=2)
-
-        def minus_stock(c, lo, hi):
-            nc.vector.scalar_tensor_tensor(
-                out=soft[c][:, lo:hi, :], in0=soft[c][:, lo:hi, :], scalar=gain_cols[:, c : c + 1],
-                in1=halves(stocks[c])[:, lo:hi, :], op0=ALU.mult, op1=ALU.subtract,
-            )
-
-        def times(t, factor):
-            nc.gpsimd.tensor_scalar(out=t, in0=t, scalar1=factor, scalar2=0.0, op0=ALU.mult, op1=ALU.add)
-
-        def sum_and_round(c, half, engine, tag):
+        def sum_and_round(c, half, engine):
             a, cc = divmod(c, 4)
-            turned = ps.tile([P, 4, P], F32, name="turned", tag=tag, bufs=BANKS[tag])
-            terms = [halves(pos[c]), soft[c]]
-            if c not in LN_GROUPS[-1]:
-                terms = [halves(stocks[c])] + terms
+            turned = ps.tile([P, 32, 4, 4], F32, name="turned", tag="turn", bufs=BANKS["turn"])
+            cols = half_cols(half)
+            terms = [signed[c][:, cols], size[c][:, cols], stocks[c][:, cols], soft[c][half]]
+            if c == TILES - 1:
+                terms = [stocks[c][:, cols], signed[c][:, cols], soft[c][half]]
             for term, src in enumerate(terms):
                 for b in range(4):
                     nc.tensor.matmul(
-                        turned[:, b, :], src[:, half, b * P : (b + 1) * P], ident[:], is_transpose=True,
+                        turned[:, :, b, :], src[:, b * P : (b + 1) * P], ident[:], is_transpose=True,
                         start=(term == 0 and b == 0), stop=(term == len(terms) - 1 and b == 3),
                     )
-            copy_on(
-                engine,
-                zt[a][half][:, :, :, cc * 32 : cc * 32 + 32, :],
-                turned[:].rearrange("m b (p u e) -> m b u p e", u=2, e=2),
-            )
+            dst = zt[a][half][:, :, cc * 32 : cc * 32 + 32, :]
+            src = turned[:].rearrange("m p b (u e) -> m (b u) p e", u=2)
+            if engine == "scalar":
+                nc.scalar.activation(out=dst, in_=src, func=ACT.Copy, scale=-1.0)
+            else:
+                nc.vector.tensor_scalar(out=dst, in0=src, scalar1=-1.0, scalar2=None, op0=ALU.mult)
 
-        def quantise_z(a, half, engines):
-            woven = sb.tile([P, BANK, 2], F32, name="woven", tag="woven", bufs=2, align_bytes=64)
+        def weave_z(a, half, engines, tag):
+            woven[a, half] = sb.tile([P, BANK, 2], F32, name=f"woven{a}{half}", align_bytes=64)
             for pair in range(2):
-                back = ps.tile([P, 2, 2, P], F32, name="back", tag="turn", bufs=4)
+                back = ps.tile([P, 2, 2, P], F32, name="back", tag=tag, bufs=BANKS[tag])
                 for b in range(2):
                     for u in range(2):
-                        src = zt[a][half][:, pair * 2 + b, u, :, :].rearrange("m p e -> m (p e)").bitcast(F32)
+                        src = zt[a][half][:, (pair * 2 + b) * 2 + u, :, :].rearrange("m p e -> m (p e)").bitcast(F32)
                         nc.tensor.transpose(back[:, b, u, :], src, ident[:])
                 copy_on(
                     engines[pair],
-                    woven[:, pair * 256 : (pair + 1) * 256, :].rearrange("p (b m) u -> p b m u", b=2),
+                    woven[a, half][:, pair * 256 : (pair + 1) * 256, :].rearrange("p (b m) u -> p b m u", b=2),
                     back[:].rearrange("p b u m -> p b m u"),
                 )
-            cols = slice(half * BANK, (half + 1) * BANK)
+
+        def quantise_z(a, half):
+            cols = half_cols(half)
             nc.vector.quantize_mx(
                 out=zc[a][:, cols].bitcast(FP8X4), scales=zs[a][:, cols],
-                in_=woven[:].rearrange("p m u -> p (m u)").bitcast(BF16),
+                in_=woven[a, half][:].rearrange("p m u -> p (m u)").bitcast(BF16),
             )
 
         def second_pass(acc, a, nt, half):
-            cols = slice(half * BANK, (half + 1) * BANK)
+            cols = half_cols(half)
             nc.tensor.matmul_mx(
                 out=acc[:],
                 lhsT=w2c[:, a, nt * 2 * P : (nt + 1) * 2 * P].bitcast(FP4X4),
@@ -186,11 +188,11 @@ def tile_list_vaccine_dispatch_kernel(
                 stop=(a == 1),
             )
 
-        nc.gpsimd.memset(planes[:].bitcast(I32), 0)
+        nc.vector.memset(planes[:].bitcast(I32), 0)
         nc.sync.dma_start(list1[:], offs)
         nc.sync.dma_start(out=words[0][:], in_=tab_words[0].rearrange("p t i -> p (t i)").bitcast(I32))
         for q in range(4):
-            nc.gpsimd.dma_start(
+            nc.scalar.dma_start(
                 out=planes[32 * q : 32 * q + 8, :].bitcast(I32), in_=tab_scales[:, 4 * q : 4 * q + 4, :].bitcast(I32)
             )
         load_w1(W1_BLOCKS[0])
@@ -199,130 +201,210 @@ def tile_list_vaccine_dispatch_kernel(
         load_page(0)
         nc.sync.dma_start(list2[:], offs2)
         nc.sync.dma_start(out=weights[:, BANK:], in_=wgs[:, BANK:])
+        load_w1(W1_BLOCKS[1])
         nc.sync.dma_start(list3[:], offs3)
         nc.gpsimd.memset(gain_rows[:], 0.0)
         nc.sync.dma_start(out=gain_rows[0:TILES, :], in_=gain.rearrange("(c p) -> c p", p=P))
-        load_w1(W1_BLOCKS[1])
+        load_w1(W1_BLOCKS[2])
         load_page(1)
+        load_w1(W1_BLOCKS[3])
 
         make_identity(nc, ident[:])
         nc.gpsimd.memset(w2s[:].rearrange("p a n -> p (a n)").bitcast(I32), 0)
 
         nc.vector.tensor_copy(picked[0][:], words[0][:].bitcast(U32).indirect(list1[:]))
         nc.vector.tensor_copy(picked_scales[:], planes[:].indirect(list1[:]))
-        q0 = quantise_w1(0, first_stage[:])
+        stage0 = sb.tile([P, 1024], BF16, name="stage0", align_bytes=64)
+        round_w1(0, stage0, 0)
+        quantise_w1((0,), stage0)
         picked.append(sb.tile([P, S], U32, name="picked1", tag="planes", align_bytes=64))
         for half in range(2):
             nc.vector.tensor_copy(
-                picked[1][:, half * BANK : (half + 1) * BANK],
+                picked[1][:, half_cols(half)],
                 words[1][:].bitcast(U32).indirect(list1[:, half * 32 : (half + 1) * 32]),
             )
-        hs[0], hs[1], hs[2], xs[0] = first[:, BANK:], ring[0], ring[1], first[:, :S]
-        first_product(0, *q0)
-
-        gain_t = ps.tile([P, P], F32, name="gain_t", tag="acc", bufs=2)
-        nc.tensor.transpose(gain_t[:], gain_rows[:], ident[:])
-        nc.scalar.copy(out=gain_cols[:], in_=gain_t[:, 0:TILES])
-
-        group_of = {c: g for g in LN_GROUPS for c in g}
-        group_tile = {}
-        accs = {}
-        quantised = {}
+        slots = [sb.tile([P, 4, S], F32, name=f"slots{a}", tag=f"wide{a}") for a in range(2)]
+        slot = [slots[i // 4][:, i % 4, :] for i in range(TILES)]
+        for c in range(2):
+            sums[c] = sb.tile([P, S], F32, name=f"sums{c}")
+        for c in range(2, TILES):
+            sums[c] = slot[c - 2]
         last = TILES - 1
         for c in range(TILES):
-            if c < FUSED:
-                scatter(c, 0, BANK)
-                scatter(c, BANK, S)
-            else:
-                nc.vector.tensor_copy(pages[c][:].indirect(list2[:]), hs[c][:])
-            if c + 2 < len(W1_BLOCKS):
-                load_w1(W1_BLOCKS[c + 2])
+            size[c] = slot[c]
+        softs = [
+            logs.tile([P, count, NP], F32, name=f"softs{i}", offset=offset, align_bytes=64)
+            for i, (count, offset) in enumerate(((3, 0), (2, 3 * 4096), (3, 0)))
+        ]
+        for group, t in zip(LN_GROUPS, softs):
+            for i, c in enumerate(group):
+                soft[c] = [t[:, i, half_cols(half)] for half in range(2)]
+        soft_last = logs.tile([P, NP], F32, name="soft_last", offset=0, align_bytes=64)
+        soft[last] = [soft_last[:, half_cols(half)] for half in range(2)]
+
+        first_product(0)
+        fused_scatter(0, 0, BANK)
+        fused_scatter(0, BANK, S)
+
+        stage12 = sb.tile([P, 2048], BF16, name="stage12", tag="stage12", align_bytes=64)
+        round_w1(1, stage12, 0)
+        round_w1(2, stage12, 1)
+        quantise_w1((1, 2), stage12)
+        got[0] = sb.tile([P, NP], F32, name="got0", tag="stage12", align_bytes=64)
+        gather(0, 0, NP)
+        load_page(2)
+        stage3 = sb.tile([P, 1024], BF16, name="stage3", align_bytes=64)
+        round_w1(3, stage3, 0)
+        quantise_w1((3,), stage3)
+        stage47 = shared.tile([P, 4096], BF16, name="stage47", offset=0, align_bytes=64)
+        round_w1(4, stage47, 0)
+        first_product(1)
+        fused_scatter(1, 0, S)
+        for c in range(5, TILES):
+            round_w1(c, stage47, c - 4)
+        quantise_w1((4, 5, 6, 7), stage47)
+        got[1] = shared.tile([P, NP], F32, name="got1", offset=4096, align_bytes=64)
+        put[2] = shared.tile([P, S], F32, name="put2", offset=0, align_bytes=64)
+        gather(1, 0, NP)
+        load_page(3)
+        for c in range(TILES):
+            load_stock(c)
+        for a in range(2):
+            nc.sync.dma_start(out=w2c[:, a, :].bitcast(I32), in_=w2_words[a].bitcast(I32))
+        for q in range(4):
+            nc.sync.dma_start(
+                out=w2s[32 * q : 32 * q + 4, :, :].bitcast(I32),
+                in_=w2_scales[:, 4 * q : 4 * q + 4, :].rearrange("a r n -> r a n").bitcast(I32),
+            )
+
+        gain_t = ps.tile([P, P], F32, name="gain_t", tag="res", bufs=BANKS["res"])
+        nc.tensor.transpose(gain_t[:], gain_rows[:], ident[:])
+        nc.scalar.copy(out=factor["gain"][:], in_=gain_t[:, 0:TILES])
+        nc.vector.reciprocal(factor["inverse"][:], factor["gain"][:])
+        for name, source, by in (
+            ("minus_gain", "gain", -1.0), ("half_gain", "gain", 0.5), ("minus_half_gain", "gain", -0.5),
+            ("minus_two_inverse", "inverse", -2.0),
+        ):
+            nc.scalar.activation(out=factor[name][:], in_=factor[source][:], func=ACT.Copy, scale=by)
+
+        for c in range(3, TILES):
+            put[c] = sb.tile([P, S], F32, name=f"put{c}", tag=f"put{c}", align_bytes=64)
+        for c in range(2, TILES - 1):
+            got[c] = put[c]
+        got[last] = sb.tile([P, NP], F32, name="got_last")
+        for c in range(last):
+            signed[c] = got[c]
+        signed[last] = logs.tile([P, NP], F32, name="signed_last", offset=4096, align_bytes=64)
+        first_product(2)
+        first_product(3)
+
+        def stream(c):
+            weigh_and_scatter(c, 2 if c == 2 else 1)
+            if c < last:
+                gather(c, 0, NP)
             if c + 2 < TILES:
                 load_page(c + 2)
-            load_stock(c)
-            if c == 1:
-                for a in range(2):
-                    nc.sync.dma_start(out=w2c[:, a, :].bitcast(I32), in_=w2_words[a].bitcast(I32))
-                for q in range(4):
-                    nc.sync.dma_start(
-                        out=w2s[32 * q : 32 * q + 4, :, :].bitcast(I32),
-                        in_=w2_scales[:, 4 * q : 4 * q + 4, :].rearrange("a r n -> r a n").bitcast(I32),
-                    )
-            if c == last:
-                break
-            for d in STAGED.get(c, ()):
-                i = min(d - STAGED[c][0], 1)
-                quantised[d] = quantise_w1(d, hs[c][:].bitcast(BF16)[:, i * 1024 : (i + 1) * 1024])
-                if d == 1:
-                    first_product(1, *quantised[1])
-            if c + 2 < TILES:
-                sums = first_product(c + 2, *quantised[c + 2])
-            xs[c + 1] = hs[c]
-            gather(c, 0, NP)
-            g = group_of[c]
-            if c == g[0]:
-                group_tile[g] = sb.tile([P, len(g) * NP], F32, name="soft", tag=f"wide{LN_GROUPS.index(g) % 2}")
-                for i, d in enumerate(g):
-                    soft[d] = group_tile[g][:].rearrange("p (h i m) -> p i h m", h=2, i=len(g))[:, i, :, :]
-            pos[c] = sb.tile([P, NP], F32, name="pos", tag="pos", bufs=5)
-            gain_c = gain_cols[:, c : c + 1]
-            nc.scalar.activation(out=soft[c], in_=halves(xs[c]), func=ACT.Abs)
-            nc.scalar.activation(out=pos[c][:], in_=xs[c][:], func=ACT.Relu, scale=gain_c)
-            for half in range(2):
-                nc.scalar.activation(out=soft[c][:, half, :], in_=soft[c][:, half, :], func=ACT.Exp, scale=-1.0)
-            if c + 2 < TILES:
-                if c > 0:
-                    hs[c + 2] = xs[c]
-                nc.gpsimd.tensor_tensor(hs[c + 2][:], sums[:], weights[:], ALU.mult)
-            if c not in LN_GROUPS[-1]:
-                times(stocks[c][:], -1.0)
-            if c == g[-1]:
-                log_one_plus(group_tile[g])
-                for half in range(2):
-                    for d in g:
-                        times(soft[d][:, half, :], gain_cols[:, d : d + 1])
-            if c in (2, 4):
-                for half in range(2):
-                    for d in (c - 2, c - 1):
-                        sum_and_round(d, half, "scalar", "turn")
-            if c == 4:
-                for half in range(2):
-                    quantise_z(0, half, ("scalar", "scalar"))
+                first_product(c + 2)
 
-        pos[last] = sb.tile([P, NP], F32, name="pos", tag="pos", bufs=5)
-        pieces = [soft[last][:, lo // BANK, lo % BANK : (hi - 1) % BANK + 1] for lo, hi in LAST_PIECES]
-        for i, (lo, hi) in enumerate(LAST_PIECES):
-            gather(last, lo, hi)
-            nc.scalar.activation(out=pieces[i], in_=xs[last][:, lo:hi], func=ACT.Abs)
-            if i > 0:
-                nc.scalar.activation(out=pieces[i - 1], in_=pieces[i - 1], func=ACT.Exp, scale=-1.0)
-        nc.scalar.activation(out=pieces[-1], in_=pieces[-1], func=ACT.Exp, scale=-1.0)
-        log_one_plus(group_tile[LN_GROUPS[-1]])
-        nc.vector.tensor_scalar(
-            out=pos[last][:], in0=xs[last][:], scalar1=0.0, scalar2=gain_cols[:, last : last + 1],
-            op0=ALU.max, op1=ALU.mult,
+        def soften(c):
+            for half in range(2):
+                cols = half_cols(half)
+                nc.scalar.activation(
+                    out=size[c][:, cols], in_=got[c][:, cols], func=ACT.Abs, scale=factor["half_gain"][:, c : c + 1]
+                )
+            for half in range(2):
+                nc.scalar.activation(
+                    out=soft[c][half], in_=size[c][:, half_cols(half)], func=ACT.Exp,
+                    scale=factor["minus_two_inverse"][:, c : c + 1],
+                )
+            times(nc.gpsimd, signed[c][:], got[c][:], "minus_half_gain", c)
+            times(nc.gpsimd, size[c], size[c], None, c)
+
+        def logarithm(group):
+            for half in range(2):
+                t = softs[LN_GROUPS.index(group)][:, 0 : len(group), half_cols(half)]
+                nc.scalar.activation(out=t, in_=t, func=ACT.Ln, bias=1.0)
+
+        def scale_logs(group):
+            for half in range(2):
+                for c in group:
+                    times(nc.gpsimd, soft[c][half], soft[c][half], "minus_gain", c)
+
+        def finish(c, engine):
+            for half in range(2):
+                sum_and_round(c, half, engine)
+
+        stream(2)
+        stream(3)
+        soften(0)
+        stream(4)
+        soften(1)
+        stream(5)
+        soften(2)
+        logarithm(LN_GROUPS[0])
+        scale_logs(LN_GROUPS[0])
+        stream(6)
+        soften(3)
+        for c in LN_GROUPS[0]:
+            finish(c, "scalar")
+        stream(7)
+        for half in range(2):
+            gather(last, half * BANK, (half + 1) * BANK)
+        for half in range(2):
+            cols = half_cols(half)
+            nc.vector.tensor_scalar(
+                out=size[last][:, cols], in0=got[last][:, cols], scalar1=KNEE,
+                scalar2=factor["gain"][:, last : last + 1], op0=ALU.min, op1=ALU.mult,
+            )
+        soften(4)
+        logarithm(LN_GROUPS[1])
+        scale_logs(LN_GROUPS[1])
+        finish(3, "scalar")
+        soften(5)
+        finish(4, "scalar")
+        for half in range(2):
+            weave_z(0, half, ("scalar", "scalar"), ("res", "acc")[half])
+        soften(6)
+        logarithm(LN_GROUPS[2])
+        scale_logs(LN_GROUPS[2])
+        sum_and_round(5, 0, "scalar")
+        sum_and_round(5, 1, "vector")
+        sum_and_round(6, 0, "vector")
+
+        zc[0] = logs.tile([P, NP], U32, name="zc0", offset=2 * 4096, align_bytes=64)
+        zc[1] = sb.tile([P, NP], U32, name="zc1", align_bytes=64)
+        for a in range(2):
+            zs[a] = sb.tile([P, NP], U8, name=f"zs{a}", align_bytes=64)
+        quantise_z(0, 0)
+        nc.vector.scalar_tensor_tensor(
+            out=signed[last][:], in0=got[last][:], scalar=factor["minus_gain"][:, last : last + 1], in1=size[last],
+            op0=ALU.mult, op1=ALU.add,
         )
+        nc.scalar.activation(
+            out=soft_last[:], in_=size[last], func=ACT.Exp, scale=factor["inverse"][:, last : last + 1]
+        )
+        accs = {}
+        sum_and_round(6, 1, "vector")
+        quantise_z(0, 1)
+        for nt in range(4):
+            tag = ("res", "acc")[nt // 2]
+            accs[nt, 0] = ps.tile([P, BANK], F32, name="res", tag=tag, bufs=BANKS[tag])
+            second_pass(accs[nt, 0], 0, nt, 0)
         for half in range(2):
-            for d in LN_GROUPS[2]:
-                sum_and_round(d, half, "vector", ("res", "acc")[half])
-            for nt in range(2 * half, 2 * half + 2):
-                accs[nt, 0] = ps.tile([P, BANK], F32, name="res", tag=("res", "acc")[half], bufs=2)
-                second_pass(accs[nt, 0], 0, nt, 0)
-        rounders = (("vector", "scalar"), ("vector", "scalar"))
+            nc.scalar.activation(out=soft[last][half], in_=soft[last][half], func=ACT.Ln, bias=1.0)
         for half in range(2):
-            for d in LN_GROUPS[3]:
-                minus_stock(d, half, half + 1)
-            for d in LN_GROUPS[3]:
-                sum_and_round(d, half, rounders[half][d - 6], "turn")
-        movers = (("scalar", "scalar", "vector", "scalar"), ("vector", "scalar", "vector", "scalar"))
+            times(nc.vector, soft[last][half], soft[last][half], "minus_gain", last)
+            sum_and_round(last, half, ("vector", "scalar")[half])
         for half in range(2):
-            quantise_z(1, half, ("scalar", "vector"))
+            weave_z(1, half, (("vector", "scalar"), ("scalar", "scalar"))[half], "turn")
+            quantise_z(1, half)
+        movers = (("vector", "scalar", "vector", "scalar"), ("vector", "scalar", "vector", "scalar"))
         for half in range(2):
             for nt in range(4):
                 if half == 1:
-                    accs[nt, half] = ps.tile([P, BANK], F32, name="res_b", tag="turn", bufs=4)
+                    accs[nt, half] = ps.tile([P, BANK], F32, name="res_b", tag="turn", bufs=BANKS["turn"])
                     second_pass(accs[nt, half], 0, nt, half)
                 second_pass(accs[nt, half], 1, nt, half)
                 staged = sb.tile([P, BANK], F32, name="staged", tag="staged", bufs=8)
                 copy_on(movers[half][nt], staged[:], accs[nt, half][:])
-                nc.sync.dma_start(out=out[nt * P : (nt + 1) * P, half * BANK : (half + 1) * BANK], in_=staged[:])
+                nc.sync.dma_start(out=out[nt * P : (nt + 1) * P, half_cols(half)], in_=staged[:])

@@ -20,7 +20,7 @@ ACT = mybir.ActivationFunctionType
 P = 128
 BANK = 512
 TILES = H // P
-W1_BLOCKS = ((0,), (1, 2), (3, 4), (5, 6, 7))
+W1_BLOCKS = ((0,), (1,), (2, 3), (4, 5), (6, 7))
 BANKS = {"turn": 4, "acc": 2, "res": 2}
 LN_GROUPS = ((0, 1, 2), (3, 4), (5, 6))
 KNEE = 30.0
@@ -51,11 +51,11 @@ def tile_list_vaccine_dispatch_kernel(
         gain_rows = sb.tile([P, P], F32, name="gain_rows")
         factor = {
             name: sb.tile([P, TILES], F32, name=name)
-            for name in ("gain", "minus_gain", "half_gain", "minus_half_gain", "inverse", "minus_two_inverse")
+            for name in ("minus_gain", "minus_half_gain")
         }
 
         raw, pages, stocks, quantised = {}, {}, {}, {}
-        sums, put, got, soft, size, signed = {}, {}, {}, {}, {}, {}
+        sums, put, got, soft, size, signed, sized = {}, {}, {}, {}, {}, {}, {}
 
         def half_cols(half):
             return slice(half * BANK, (half + 1) * BANK)
@@ -84,9 +84,12 @@ def tile_list_vaccine_dispatch_kernel(
             )
 
         def quantise_w1(group, stage):
-            codes = sb.tile([P, len(group) * 2 * P], U32, name=f"w1c{group[0]}", align_bytes=64)
-            scales = sb.tile([P, len(group) * 2 * P], U8, name=f"w1s{group[0]}", align_bytes=64)
-            nc.vector.quantize_mx(out=codes[:].bitcast(FP8X4), scales=scales[:], in_=stage[:])
+            if group == (1,):
+                codes = shared.tile([P, 2 * P], U32, name="w1c1", offset=4096, align_bytes=64)
+            else:
+                codes = sb.tile([P, len(group) * 2 * P], U32, name=f"w1c{group[0]}", tag=f"w1c{group[0]}", align_bytes=64)
+            scales = sb.tile([P, len(group) * 2 * P], U8, name=f"w1s{group[0]}", tag=f"w1s{group[0]}", align_bytes=64)
+            nc.vector.quantize_mx(out=codes[:].bitcast(FP8X4), scales=scales[:], in_=stage[:, : len(group) * 1024])
             for i, c in enumerate(group):
                 quantised[c] = (codes[:, i * 2 * P : (i + 1) * 2 * P], scales[:, i * 2 * P : (i + 1) * 2 * P])
 
@@ -123,10 +126,10 @@ def tile_list_vaccine_dispatch_kernel(
             nc.vector.tensor_copy(got[c][:, lo:hi], pages[c][:].indirect(list3[:, lo // 16 : hi // 16]))
 
         def times(engine, dst, src, name, c):
-            by = -1.0 if name is None else factor[name][:, c : c + 1]
+            by = factor[name][:, c : c + 1]
             engine.tensor_scalar(out=dst, in0=src, scalar1=by, scalar2=0.0, op0=ALU.mult, op1=ALU.add)
 
-        zt = [[sb.tile([P, 8, P, 2], BF16, name=f"zt{a}{half}") for half in range(2)] for a in range(2)]
+        zt = [[sb.tile([P, 8, P, 2], BF16, name=f"zt{a}{half}", tag=f"zt{a}{half}") for half in range(2)] for a in range(2)]
         zc, zs, woven = {}, {}, {}
 
         def copy_on(engine, dst, src):
@@ -135,13 +138,13 @@ def tile_list_vaccine_dispatch_kernel(
             else:
                 nc.vector.tensor_copy(out=dst, in_=src)
 
-        def sum_and_round(c, half, engine):
+        def sum_and_round(c, half, engine, tag="turn"):
             a, cc = divmod(c, 4)
-            turned = ps.tile([P, 32, 4, 4], F32, name="turned", tag="turn", bufs=BANKS["turn"])
+            turned = ps.tile([P, 32, 4, 4], F32, name="turned", tag=tag, bufs=BANKS[tag])
             cols = half_cols(half)
-            terms = [signed[c][:, cols], size[c][:, cols], stocks[c][:, cols], soft[c][half]]
-            if c == TILES - 1:
-                terms = [stocks[c][:, cols], signed[c][:, cols], soft[c][half]]
+            terms = [stocks[c][:, cols], soft[c][half]]
+            if c < TILES - 1:
+                terms = [signed[c][:, cols], sized[c][:, cols]] + terms
             for term, src in enumerate(terms):
                 for b in range(4):
                     nc.tensor.matmul(
@@ -156,7 +159,7 @@ def tile_list_vaccine_dispatch_kernel(
                 nc.vector.tensor_scalar(out=dst, in0=src, scalar1=-1.0, scalar2=None, op0=ALU.mult)
 
         def weave_z(a, half, engines, tag):
-            woven[a, half] = sb.tile([P, BANK, 2], F32, name=f"woven{a}{half}", align_bytes=64)
+            woven[a, half] = sb.tile([P, BANK, 2], F32, name=f"woven{a}{half}", tag=f"woven{a}{half}", align_bytes=64)
             for pair in range(2):
                 back = ps.tile([P, 2, 2, P], F32, name="back", tag=tag, bufs=BANKS[tag])
                 for b in range(2):
@@ -172,7 +175,7 @@ def tile_list_vaccine_dispatch_kernel(
         def quantise_z(a, half):
             cols = half_cols(half)
             nc.vector.quantize_mx(
-                out=zc[a][:, cols].bitcast(FP8X4), scales=zs[a][:, cols],
+                out=zc[a, half].bitcast(FP8X4), scales=zs[a][:, cols],
                 in_=woven[a, half][:].rearrange("p m u -> p (m u)").bitcast(BF16),
             )
 
@@ -182,7 +185,7 @@ def tile_list_vaccine_dispatch_kernel(
                 out=acc[:],
                 lhsT=w2c[:, a, nt * 2 * P : (nt + 1) * 2 * P].bitcast(FP4X4),
                 lhsT_scale=w2s[:, a, nt * P : (nt + 1) * P],
-                rhs=zc[a][:, cols].bitcast(FP8X4),
+                rhs=zc[a, half].bitcast(FP8X4),
                 rhs_scale=zs[a][:, cols],
                 start=(a == 0),
                 stop=(a == 1),
@@ -190,6 +193,7 @@ def tile_list_vaccine_dispatch_kernel(
 
         nc.vector.memset(planes[:].bitcast(I32), 0)
         nc.sync.dma_start(list1[:], offs)
+        nc.sync.dma_start(list2[:], offs2)
         nc.sync.dma_start(out=words[0][:], in_=tab_words[0].rearrange("p t i -> p (t i)").bitcast(I32))
         for q in range(4):
             nc.scalar.dma_start(
@@ -199,7 +203,6 @@ def tile_list_vaccine_dispatch_kernel(
         nc.sync.dma_start(out=words[1][:], in_=tab_words[1].rearrange("p t i -> p (t i)").bitcast(I32))
         nc.sync.dma_start(out=weights[:, :BANK], in_=wgs[:, :BANK])
         load_page(0)
-        nc.sync.dma_start(list2[:], offs2)
         nc.sync.dma_start(out=weights[:, BANK:], in_=wgs[:, BANK:])
         load_w1(W1_BLOCKS[1])
         nc.sync.dma_start(list3[:], offs3)
@@ -208,6 +211,7 @@ def tile_list_vaccine_dispatch_kernel(
         load_w1(W1_BLOCKS[2])
         load_page(1)
         load_w1(W1_BLOCKS[3])
+        load_w1(W1_BLOCKS[4])
 
         make_identity(nc, ident[:])
         nc.gpsimd.memset(w2s[:].rearrange("p a n -> p (a n)").bitcast(I32), 0)
@@ -225,16 +229,18 @@ def tile_list_vaccine_dispatch_kernel(
             )
         slots = [sb.tile([P, 4, S], F32, name=f"slots{a}", tag=f"wide{a}") for a in range(2)]
         slot = [slots[i // 4][:, i % 4, :] for i in range(TILES)]
-        for c in range(2):
-            sums[c] = sb.tile([P, S], F32, name=f"sums{c}")
-        for c in range(2, TILES):
+        sums[0] = shared.tile([P, S], F32, name="sums0", offset=0, align_bytes=64)
+        for c, offset in ((1, 2 * 4096), (2, 6 * 4096), (3, 7 * 4096)):
+            sums[c] = streamed.tile([P, S], F32, name=f"sums{c}", offset=offset)[:]
+        for c in range(4, TILES):
             sums[c] = slot[c - 2]
         last = TILES - 1
-        for c in range(TILES):
-            size[c] = slot[c]
+        for c in range(last):
+            sized[c] = sums[c + 2] if c + 2 < TILES else slot[c]
+        size[last] = slot[last]
         softs = [
             logs.tile([P, count, NP], F32, name=f"softs{i}", offset=offset, align_bytes=64)
-            for i, (count, offset) in enumerate(((3, 0), (2, 3 * 4096), (3, 0)))
+            for i, (count, offset) in enumerate(((3, 0), (2, 3 * 4096), (2, 0)))
         ]
         for group, t in zip(LN_GROUPS, softs):
             for i, c in enumerate(group):
@@ -246,28 +252,37 @@ def tile_list_vaccine_dispatch_kernel(
         fused_scatter(0, 0, BANK)
         fused_scatter(0, BANK, S)
 
-        stage12 = sb.tile([P, 2048], BF16, name="stage12", tag="stage12", align_bytes=64)
-        round_w1(1, stage12, 0)
-        round_w1(2, stage12, 1)
-        quantise_w1((1, 2), stage12)
-        got[0] = sb.tile([P, NP], F32, name="got0", tag="stage12", align_bytes=64)
+        stage1 = sb.tile([P, 1024], BF16, name="stage1", tag="w1c0", align_bytes=64)
+        round_w1(1, stage1, 0)
+        quantise_w1((1,), stage1)
+        got[0] = sb.tile([P, NP], F32, name="got0", tag="w1c0", align_bytes=64)
         gather(0, 0, NP)
         load_page(2)
-        stage3 = sb.tile([P, 1024], BF16, name="stage3", align_bytes=64)
-        round_w1(3, stage3, 0)
-        quantise_w1((3,), stage3)
-        stage47 = shared.tile([P, 4096], BF16, name="stage47", offset=0, align_bytes=64)
-        round_w1(4, stage47, 0)
+        stage23 = sb.tile([P, 2048], BF16, name="stage23", tag="w1s0", align_bytes=64)
+        round_w1(2, stage23, 0)
+        round_w1(3, stage23, 1)
+        quantise_w1((2, 3), stage23)
+        stage47 = shared.tile([P, 6144], BF16, name="stage47", offset=0, align_bytes=64)
         first_product(1)
-        fused_scatter(1, 0, S)
-        for c in range(5, TILES):
+        gain_t = ps.tile([P, P], F32, name="gain_t", tag="acc", bufs=BANKS["acc"])
+        nc.tensor.transpose(gain_t[:], gain_rows[:], ident[:])
+        for name, by in (("minus_gain", -1.0), ("minus_half_gain", -0.5)):
+            nc.scalar.activation(out=factor[name][:], in_=gain_t[:, 0:TILES], func=ACT.Copy, scale=by)
+        fused_scatter(1, 0, BANK)
+        fused_scatter(1, BANK, S)
+        for c in range(4, TILES):
             round_w1(c, stage47, c - 4)
         quantise_w1((4, 5, 6, 7), stage47)
         got[1] = shared.tile([P, NP], F32, name="got1", offset=4096, align_bytes=64)
         put[2] = shared.tile([P, S], F32, name="put2", offset=0, align_bytes=64)
+        early_size = shared.tile([P, NP], F32, name="early_size", offset=8192, align_bytes=64)
+        for c in range(4):
+            size[c] = early_size[:]
+        for c in (4, 5):
+            size[c] = logs.tile([P, NP], F32, name=f"size{c}", offset=2 * 4096, align_bytes=64)[:]
         gather(1, 0, NP)
         load_page(3)
-        for c in range(TILES):
+        for c in range(TILES - 2):
             load_stock(c)
         for a in range(2):
             nc.sync.dma_start(out=w2c[:, a, :].bitcast(I32), in_=w2_words[a].bitcast(I32))
@@ -277,15 +292,6 @@ def tile_list_vaccine_dispatch_kernel(
                 in_=w2_scales[:, 4 * q : 4 * q + 4, :].rearrange("a r n -> r a n").bitcast(I32),
             )
 
-        gain_t = ps.tile([P, P], F32, name="gain_t", tag="res", bufs=BANKS["res"])
-        nc.tensor.transpose(gain_t[:], gain_rows[:], ident[:])
-        nc.scalar.copy(out=factor["gain"][:], in_=gain_t[:, 0:TILES])
-        nc.vector.reciprocal(factor["inverse"][:], factor["gain"][:])
-        for name, source, by in (
-            ("minus_gain", "gain", -1.0), ("half_gain", "gain", 0.5), ("minus_half_gain", "gain", -0.5),
-            ("minus_two_inverse", "inverse", -2.0),
-        ):
-            nc.scalar.activation(out=factor[name][:], in_=factor[source][:], func=ACT.Copy, scale=by)
 
         for c in range(3, TILES):
             put[c] = sb.tile([P, S], F32, name=f"put{c}", tag=f"put{c}", align_bytes=64)
@@ -294,7 +300,6 @@ def tile_list_vaccine_dispatch_kernel(
         got[last] = sb.tile([P, NP], F32, name="got_last")
         for c in range(last):
             signed[c] = got[c]
-        signed[last] = logs.tile([P, NP], F32, name="signed_last", offset=4096, align_bytes=64)
         first_product(2)
         first_product(3)
 
@@ -309,16 +314,11 @@ def tile_list_vaccine_dispatch_kernel(
         def soften(c):
             for half in range(2):
                 cols = half_cols(half)
-                nc.scalar.activation(
-                    out=size[c][:, cols], in_=got[c][:, cols], func=ACT.Abs, scale=factor["half_gain"][:, c : c + 1]
-                )
+                nc.scalar.activation(out=size[c][:, cols], in_=got[c][:, cols], func=ACT.Abs)
             for half in range(2):
-                nc.scalar.activation(
-                    out=soft[c][half], in_=size[c][:, half_cols(half)], func=ACT.Exp,
-                    scale=factor["minus_two_inverse"][:, c : c + 1],
-                )
+                nc.scalar.activation(out=soft[c][half], in_=size[c][:, half_cols(half)], func=ACT.Exp, scale=-1.0)
             times(nc.gpsimd, signed[c][:], got[c][:], "minus_half_gain", c)
-            times(nc.gpsimd, size[c], size[c], None, c)
+            times(nc.gpsimd, sized[c], size[c], "minus_half_gain", c)
 
         def logarithm(group):
             for half in range(2):
@@ -343,18 +343,19 @@ def tile_list_vaccine_dispatch_kernel(
         soften(2)
         logarithm(LN_GROUPS[0])
         scale_logs(LN_GROUPS[0])
+        load_stock(6)
+        load_stock(7)
         stream(6)
         soften(3)
         for c in LN_GROUPS[0]:
             finish(c, "scalar")
         stream(7)
         for half in range(2):
-            gather(last, half * BANK, (half + 1) * BANK)
-        for half in range(2):
             cols = half_cols(half)
+            gather(last, half * BANK, half * BANK + BANK // 2)
+            gather(last, half * BANK + BANK // 2, (half + 1) * BANK)
             nc.vector.tensor_scalar(
-                out=size[last][:, cols], in0=got[last][:, cols], scalar1=KNEE,
-                scalar2=factor["gain"][:, last : last + 1], op0=ALU.min, op1=ALU.mult,
+                out=size[last][:, cols], in0=got[last][:, cols], scalar1=KNEE, scalar2=None, op0=ALU.min
             )
         soften(4)
         logarithm(LN_GROUPS[1])
@@ -364,28 +365,33 @@ def tile_list_vaccine_dispatch_kernel(
         finish(4, "scalar")
         for half in range(2):
             weave_z(0, half, ("scalar", "scalar"), ("res", "acc")[half])
+        size[6] = sb.tile([P, NP], F32, name="size6", tag="zt01")[:]
         soften(6)
         logarithm(LN_GROUPS[2])
         scale_logs(LN_GROUPS[2])
         sum_and_round(5, 0, "scalar")
-        sum_and_round(5, 1, "vector")
+        sum_and_round(5, 1, "vector", "acc")
         sum_and_round(6, 0, "vector")
 
-        zc[0] = logs.tile([P, NP], U32, name="zc0", offset=2 * 4096, align_bytes=64)
-        zc[1] = sb.tile([P, NP], U32, name="zc1", align_bytes=64)
+        zc[0, 0] = logs.tile([P, BANK], U32, name="zc00", offset=4096, align_bytes=64)[:]
+        signed[last] = logs.tile([P, NP], F32, name="signed_last", offset=4096 + 2048, align_bytes=64)
+        for half in range(2):
+            zc[1, half] = sb.tile([P, BANK], U32, name=f"zc1{half}", align_bytes=64)[:]
         for a in range(2):
             zs[a] = sb.tile([P, NP], U8, name=f"zs{a}", align_bytes=64)
         quantise_z(0, 0)
-        nc.vector.scalar_tensor_tensor(
-            out=signed[last][:], in0=got[last][:], scalar=factor["minus_gain"][:, last : last + 1], in1=size[last],
-            op0=ALU.mult, op1=ALU.add,
-        )
-        nc.scalar.activation(
-            out=soft_last[:], in_=size[last], func=ACT.Exp, scale=factor["inverse"][:, last : last + 1]
-        )
+        for half in range(2):
+            cols = half_cols(half)
+            nc.vector.tensor_scalar(
+                out=signed[last][:, cols], in0=got[last][:, cols], scalar1=KNEE, scalar2=0.0,
+                op0=ALU.subtract, op1=ALU.max,
+            )
+            nc.scalar.activation(out=soft[last][half], in_=size[last][:, cols], func=ACT.Exp)
+        for half in range(2):
+            cols = half_cols(half)
+            times(nc.vector, signed[last][:, cols], signed[last][:, cols], "minus_gain", last)
+        sum_and_round(6, 1, "vector", "acc")
         accs = {}
-        sum_and_round(6, 1, "vector")
-        quantise_z(0, 1)
         for nt in range(4):
             tag = ("res", "acc")[nt // 2]
             accs[nt, 0] = ps.tile([P, BANK], F32, name="res", tag=tag, bufs=BANKS[tag])
@@ -393,12 +399,18 @@ def tile_list_vaccine_dispatch_kernel(
         for half in range(2):
             nc.scalar.activation(out=soft[last][half], in_=soft[last][half], func=ACT.Ln, bias=1.0)
         for half in range(2):
-            times(nc.vector, soft[last][half], soft[last][half], "minus_gain", last)
+            nc.vector.scalar_tensor_tensor(
+                out=soft[last][half], in0=soft[last][half], scalar=factor["minus_gain"][:, last : last + 1],
+                in1=signed[last][:, half_cols(half)], op0=ALU.mult, op1=ALU.add,
+            )
             sum_and_round(last, half, ("vector", "scalar")[half])
-        for half in range(2):
-            weave_z(1, half, (("vector", "scalar"), ("scalar", "scalar"))[half], "turn")
-            quantise_z(1, half)
-        movers = (("vector", "scalar", "vector", "scalar"), ("vector", "scalar", "vector", "scalar"))
+        weave_z(1, 0, ("vector", "scalar"), "turn")
+        quantise_z(1, 0)
+        zc[0, 1] = sb.tile([P, BANK], U32, name="zc01", tag="woven10", align_bytes=64)[:]
+        quantise_z(0, 1)
+        weave_z(1, 1, ("scalar", "scalar"), "turn")
+        quantise_z(1, 1)
+        movers = (("scalar", "vector", "scalar", "scalar"), ("vector", "scalar", "vector", "scalar"))
         for half in range(2):
             for nt in range(4):
                 if half == 1:

@@ -24,6 +24,7 @@ W1_BLOCKS = ((0,), (1,), (2, 3), (4, 5), (6, 7))
 BANKS = {"turn": 4, "acc": 2, "res": 2}
 LN_GROUPS = ((0, 1, 2), (3, 4), (5, 6))
 KNEE = 30.0
+PIECES = (((0, 512), (512, 1024)), ((0, 256), (256, 512), (512, 1024)))
 
 
 def tile_list_vaccine_dispatch_kernel(
@@ -48,6 +49,8 @@ def tile_list_vaccine_dispatch_kernel(
         w2c = sb.tile([P, 2, 2 * N], U8, name="w2c", align_bytes=64)
         w2s = sb.tile([P, 2, N], U8, name="w2s", align_bytes=64)
         ident = sb.tile([P, P], F32, name="ident")
+        gain_last = sb.tile([P, 1], F32, name="gain_last")
+        gain_wide = sb.tile([P, 32, 4, 4], F32, name="gain_wide")
         gain_rows = sb.tile([P, P], F32, name="gain_rows")
         factor = {
             name: sb.tile([P, TILES], F32, name=name)
@@ -74,8 +77,11 @@ def tile_list_vaccine_dispatch_kernel(
             nc.sync.dma_start(out=pages[c][:], in_=page0[c * P : (c + 1) * P, :])
 
         def load_stock(c):
-            stocks[c] = streamed.tile([P, NP], F32, name=f"stock{c}", offset=c * 4096)
-            nc.sync.dma_start(out=stocks[c][:], in_=stock[c * P : (c + 1) * P, :])
+            if c < TILES - 2:
+                stocks[c] = streamed.tile([P, NP], F32, name=f"stock{c}", offset=c * 4096)[:]
+            else:
+                stocks[c] = slot[c - (TILES - 2)]
+            nc.sync.dma_start(out=stocks[c], in_=stock[c * P : (c + 1) * P, :])
 
         def round_w1(c, stage, i):
             nc.scalar.copy(
@@ -129,7 +135,11 @@ def tile_list_vaccine_dispatch_kernel(
             by = factor[name][:, c : c + 1]
             engine.tensor_scalar(out=dst, in0=src, scalar1=by, scalar2=0.0, op0=ALU.mult, op1=ALU.add)
 
-        zt = [[sb.tile([P, 8, P, 2], BF16, name=f"zt{a}{half}", tag=f"zt{a}{half}") for half in range(2)] for a in range(2)]
+        zt = {
+            (a, lo): sb.tile([P, (hi - lo) // 64, P, 2], BF16, name=f"zt{a}_{lo}", tag=f"zt{a}_{lo}")
+            for a in range(2)
+            for lo, hi in PIECES[a]
+        }
         zc, zs, woven = {}, {}, {}
 
         def copy_on(engine, dst, src):
@@ -138,58 +148,72 @@ def tile_list_vaccine_dispatch_kernel(
             else:
                 nc.vector.tensor_copy(out=dst, in_=src)
 
-        def sum_and_round(c, half, engine, tag="turn"):
-            a, cc = divmod(c, 4)
-            turned = ps.tile([P, 32, 4, 4], F32, name="turned", tag=tag, bufs=BANKS[tag])
-            cols = half_cols(half)
-            terms = [stocks[c][:, cols], soft[c][half]]
-            if c < TILES - 1:
-                terms = [signed[c][:, cols], sized[c][:, cols]] + terms
+        def turn(terms, tag):
+            blocks = terms[0].shape[1] // P
+            turned = ps.tile([P, 32, blocks, 4], F32, name="turned", tag=tag, bufs=BANKS[tag])
             for term, src in enumerate(terms):
-                for b in range(4):
+                for b in range(blocks):
                     nc.tensor.matmul(
                         turned[:, :, b, :], src[:, b * P : (b + 1) * P], ident[:], is_transpose=True,
-                        start=(term == 0 and b == 0), stop=(term == len(terms) - 1 and b == 3),
+                        start=(term == 0 and b == 0), stop=(term == len(terms) - 1 and b == blocks - 1),
                     )
-            dst = zt[a][half][:, :, cc * 32 : cc * 32 + 32, :]
-            src = turned[:].rearrange("m p b (u e) -> m (b u) p e", u=2)
-            if engine == "scalar":
-                nc.scalar.activation(out=dst, in_=src, func=ACT.Copy, scale=-1.0)
-            else:
-                nc.vector.tensor_scalar(out=dst, in0=src, scalar1=-1.0, scalar2=None, op0=ALU.mult)
+            return turned
 
-        def weave_z(a, half, engines, tag):
-            woven[a, half] = sb.tile([P, BANK, 2], F32, name=f"woven{a}{half}", tag=f"woven{a}{half}", align_bytes=64)
-            for pair in range(2):
+        def by_words(t):
+            return t.rearrange("m p b (u e) -> m (b u) p e", u=2)
+
+        def sum_and_round(c, half, engine, tag="turn"):
+            a, cc = divmod(c, 4)
+            cols = half_cols(half)
+            turned = turn([signed[c][:, cols], sized[c][:, cols], stocks[c][:, cols], soft[c][half]], tag)
+            for lo, hi in PIECES[a]:
+                if lo // BANK == half:
+                    dst = zt[a, lo][:, :, cc * 32 : cc * 32 + 32, :]
+                    src = by_words(turned[:, :, lo % BANK // P : lo % BANK // P + (hi - lo) // P, :])
+                    if engine == "scalar":
+                        nc.scalar.activation(out=dst, in_=src, func=ACT.Copy, scale=-1.0)
+                    else:
+                        nc.vector.tensor_scalar(out=dst, in0=src, scalar1=-1.0, scalar2=None, op0=ALU.mult)
+
+        def weave_z(a, lo, hi, engines, tag):
+            woven[a, lo] = sb.tile([P, hi - lo, 2], F32, name=f"woven{a}_{lo}", tag=f"woven{a}_{lo}", align_bytes=64)
+            for pair in range((hi - lo) // 256):
                 back = ps.tile([P, 2, 2, P], F32, name="back", tag=tag, bufs=BANKS[tag])
                 for b in range(2):
                     for u in range(2):
-                        src = zt[a][half][:, (pair * 2 + b) * 2 + u, :, :].rearrange("m p e -> m (p e)").bitcast(F32)
+                        src = zt[a, lo][:, (pair * 2 + b) * 2 + u, :, :].rearrange("m p e -> m (p e)").bitcast(F32)
                         nc.tensor.transpose(back[:, b, u, :], src, ident[:])
                 copy_on(
                     engines[pair],
-                    woven[a, half][:, pair * 256 : (pair + 1) * 256, :].rearrange("p (b m) u -> p b m u", b=2),
+                    woven[a, lo][:, pair * 256 : (pair + 1) * 256, :].rearrange("p (b m) u -> p b m u", b=2),
                     back[:].rearrange("p b u m -> p b m u"),
                 )
 
-        def quantise_z(a, half):
-            cols = half_cols(half)
+        def quantise_z(a, lo, hi):
             nc.vector.quantize_mx(
-                out=zc[a, half].bitcast(FP8X4), scales=zs[a][:, cols],
-                in_=woven[a, half][:].rearrange("p m u -> p (m u)").bitcast(BF16),
+                out=zc[a, lo].bitcast(FP8X4), scales=zs[a][:, lo:hi],
+                in_=woven[a, lo][:].rearrange("p m u -> p (m u)").bitcast(BF16),
             )
 
-        def second_pass(acc, a, nt, half):
-            cols = half_cols(half)
+        def second_pass(acc, a, nt, lo, hi, start, stop):
+            first = max(x for x, end in PIECES[a] if x <= lo)
             nc.tensor.matmul_mx(
-                out=acc[:],
+                out=acc,
                 lhsT=w2c[:, a, nt * 2 * P : (nt + 1) * 2 * P].bitcast(FP4X4),
                 lhsT_scale=w2s[:, a, nt * P : (nt + 1) * P],
-                rhs=zc[a, half].bitcast(FP8X4),
-                rhs_scale=zs[a][:, cols],
-                start=(a == 0),
-                stop=(a == 1),
+                rhs=zc[a, first][:, lo - first : hi - first].bitcast(FP8X4),
+                rhs_scale=zs[a][:, lo:hi],
+                start=start,
+                stop=stop,
             )
+
+        def narrow_passes(acc, a, pair, lo):
+            for i in range(2):
+                for s in range(2):
+                    second_pass(
+                        acc[:, i, s * P : (s + 1) * P], a, 2 * pair + i, lo + s * P, lo + (s + 1) * P,
+                        a == 0 and i == 0 and s == 0, a == 1 and i == 1 and s == 1,
+                    )
 
         nc.vector.memset(planes[:].bitcast(I32), 0)
         nc.sync.dma_start(list1[:], offs)
@@ -210,6 +234,7 @@ def tile_list_vaccine_dispatch_kernel(
         nc.sync.dma_start(out=gain_rows[0:TILES, :], in_=gain.rearrange("(c p) -> c p", p=P))
         load_w1(W1_BLOCKS[2])
         load_page(1)
+        nc.sync.dma_start(out=gain_last[:], in_=gain[H - P : H].rearrange("(p o) -> p o", o=1))
         load_w1(W1_BLOCKS[3])
         load_w1(W1_BLOCKS[4])
 
@@ -240,7 +265,7 @@ def tile_list_vaccine_dispatch_kernel(
         size[last] = slot[last]
         softs = [
             logs.tile([P, count, NP], F32, name=f"softs{i}", offset=offset, align_bytes=64)
-            for i, (count, offset) in enumerate(((3, 0), (2, 3 * 4096), (2, 0)))
+            for i, (count, offset) in enumerate(((4, 0), (2, 4 * 4096), (3, 0)))
         ]
         for group, t in zip(LN_GROUPS, softs):
             for i, c in enumerate(group):
@@ -262,7 +287,7 @@ def tile_list_vaccine_dispatch_kernel(
         round_w1(2, stage23, 0)
         round_w1(3, stage23, 1)
         quantise_w1((2, 3), stage23)
-        stage47 = shared.tile([P, 6144], BF16, name="stage47", offset=0, align_bytes=64)
+        stage47 = shared.tile([P, 6160], BF16, name="stage47", offset=0, align_bytes=64)
         first_product(1)
         gain_t = ps.tile([P, P], F32, name="gain_t", tag="acc", bufs=BANKS["acc"])
         nc.tensor.transpose(gain_t[:], gain_rows[:], ident[:])
@@ -279,10 +304,12 @@ def tile_list_vaccine_dispatch_kernel(
         for c in range(4):
             size[c] = early_size[:]
         for c in (4, 5):
-            size[c] = logs.tile([P, NP], F32, name=f"size{c}", offset=2 * 4096, align_bytes=64)[:]
+            size[c] = logs.tile([P, NP], F32, name=f"size{c}", offset=3 * 4096, align_bytes=64)[:]
+        inverse_last = shared.tile([P, 1], F32, name="inverse_last", offset=3 * 4096)
+        nc.vector.reciprocal(inverse_last[:], gain_last[:])
         gather(1, 0, NP)
         load_page(3)
-        for c in range(TILES - 2):
+        for c in range(TILES):
             load_stock(c)
         for a in range(2):
             nc.sync.dma_start(out=w2c[:, a, :].bitcast(I32), in_=w2_words[a].bitcast(I32))
@@ -330,9 +357,9 @@ def tile_list_vaccine_dispatch_kernel(
                 for c in group:
                     times(nc.gpsimd, soft[c][half], soft[c][half], "minus_gain", c)
 
-        def finish(c, engine):
+        def finish(c, engine, tag="turn"):
             for half in range(2):
-                sum_and_round(c, half, engine)
+                sum_and_round(c, half, engine, tag)
 
         stream(2)
         stream(3)
@@ -343,12 +370,16 @@ def tile_list_vaccine_dispatch_kernel(
         soften(2)
         logarithm(LN_GROUPS[0])
         scale_logs(LN_GROUPS[0])
-        load_stock(6)
-        load_stock(7)
         stream(6)
         soften(3)
         for c in LN_GROUPS[0]:
-            finish(c, "scalar")
+            finish(c, "scalar", "res" if c == 2 else "turn")
+        stock_over_gain = sb.tile([P, NP], F32, name="stock_over_gain", tag="w1c0", align_bytes=64)
+        nc.gpsimd.tensor_scalar(
+            out=stock_over_gain[:], in0=stocks[last], scalar1=inverse_last[:], scalar2=-1.0, op0=ALU.mult, op1=ALU.mult
+        )
+        spread = turn([gain_last[:].to_broadcast([P, BANK])], "res")
+        nc.scalar.copy(out=gain_wide[:], in_=spread[:])
         stream(7)
         for half in range(2):
             cols = half_cols(half)
@@ -364,22 +395,23 @@ def tile_list_vaccine_dispatch_kernel(
         soften(5)
         finish(4, "scalar")
         for half in range(2):
-            weave_z(0, half, ("scalar", "scalar"), ("res", "acc")[half])
-        size[6] = sb.tile([P, NP], F32, name="size6", tag="zt01")[:]
+            weave_z(0, half * BANK, (half + 1) * BANK, ("scalar", "scalar"), ("res", "acc")[half])
+        size[6] = sb.tile([P, NP], F32, name="size6", tag="zt0_512")[:]
         soften(6)
         logarithm(LN_GROUPS[2])
         scale_logs(LN_GROUPS[2])
         sum_and_round(5, 0, "scalar")
-        sum_and_round(5, 1, "vector", "acc")
+        sum_and_round(5, 1, "vector")
         sum_and_round(6, 0, "vector")
 
-        zc[0, 0] = logs.tile([P, BANK], U32, name="zc00", offset=4096, align_bytes=64)[:]
-        signed[last] = logs.tile([P, NP], F32, name="signed_last", offset=4096 + 2048, align_bytes=64)
+        codes0 = logs.tile([P, NP], U32, name="zc0", offset=4096, align_bytes=64)
         for half in range(2):
-            zc[1, half] = sb.tile([P, BANK], U32, name=f"zc1{half}", align_bytes=64)[:]
+            zc[0, half * BANK] = codes0[:, half_cols(half)]
+        signed[last] = logs.tile([P, NP], F32, name="signed_last", offset=2 * 4096, align_bytes=64)
+        for lo, hi in PIECES[1]:
+            zc[1, lo] = sb.tile([P, hi - lo], U32, name=f"zc1_{lo}", align_bytes=64)[:]
         for a in range(2):
             zs[a] = sb.tile([P, NP], U8, name=f"zs{a}", align_bytes=64)
-        quantise_z(0, 0)
         for half in range(2):
             cols = half_cols(half)
             nc.vector.tensor_scalar(
@@ -387,36 +419,35 @@ def tile_list_vaccine_dispatch_kernel(
                 op0=ALU.subtract, op1=ALU.max,
             )
             nc.scalar.activation(out=soft[last][half], in_=size[last][:, cols], func=ACT.Exp)
-        for half in range(2):
-            cols = half_cols(half)
-            times(nc.vector, signed[last][:, cols], signed[last][:, cols], "minus_gain", last)
-        sum_and_round(6, 1, "vector", "acc")
-        accs = {}
-        for nt in range(4):
-            tag = ("res", "acc")[nt // 2]
-            accs[nt, 0] = ps.tile([P, BANK], F32, name="res", tag=tag, bufs=BANKS[tag])
-            second_pass(accs[nt, 0], 0, nt, 0)
-        for half in range(2):
-            nc.scalar.activation(out=soft[last][half], in_=soft[last][half], func=ACT.Ln, bias=1.0)
-        for half in range(2):
-            nc.vector.scalar_tensor_tensor(
-                out=soft[last][half], in0=soft[last][half], scalar=factor["minus_gain"][:, last : last + 1],
-                in1=signed[last][:, half_cols(half)], op0=ALU.mult, op1=ALU.add,
+            if half == 0:
+                quantise_z(0, 0, BANK)
+        sum_and_round(6, 1, "vector")
+        quantise_z(0, BANK, NP)
+        for lo, hi in PIECES[1]:
+            nc.scalar.activation(out=soft_last[:, lo:hi], in_=soft_last[:, lo:hi], func=ACT.Ln, bias=1.0)
+        for lo, hi in PIECES[1]:
+            turned = turn([stock_over_gain[:, lo:hi], signed[last][:, lo:hi], soft_last[:, lo:hi]], "acc" if lo < BANK else "turn")
+            nc.vector.tensor_tensor(
+                zt[1, lo][:, :, 96:P, :], by_words(turned[:]), by_words(gain_wide[:, :, 0 : (hi - lo) // P, :]), ALU.mult
             )
-            sum_and_round(last, half, ("vector", "scalar")[half])
-        weave_z(1, 0, ("vector", "scalar"), "turn")
-        quantise_z(1, 0)
-        zc[0, 1] = sb.tile([P, BANK], U32, name="zc01", tag="woven10", align_bytes=64)[:]
-        quantise_z(0, 1)
-        weave_z(1, 1, ("scalar", "scalar"), "turn")
-        quantise_z(1, 1)
-        movers = (("scalar", "vector", "scalar", "scalar"), ("vector", "scalar", "vector", "scalar"))
-        for half in range(2):
-            for nt in range(4):
-                if half == 1:
-                    accs[nt, half] = ps.tile([P, BANK], F32, name="res_b", tag="turn", bufs=BANKS["turn"])
-                    second_pass(accs[nt, half], 0, nt, half)
-                second_pass(accs[nt, half], 1, nt, half)
-                staged = sb.tile([P, BANK], F32, name="staged", tag="staged", bufs=8)
-                copy_on(movers[half][nt], staged[:], accs[nt, half][:])
-                nc.sync.dma_start(out=out[nt * P : (nt + 1) * P, half_cols(half)], in_=staged[:])
+        for lo, hi in PIECES[1][:2]:
+            weave_z(1, lo, hi, ("vector" if lo == 0 else "scalar",), "turn")
+            quantise_z(1, lo, hi)
+        weave_z(1, BANK, NP, ("scalar", "scalar"), "turn")
+        quantise_z(1, BANK, NP)
+        for j in range(2):
+            for pair in range(2):
+                acc = ps.tile([P, 2, 256], F32, name="res", tag=("res", "acc")[j], bufs=2)
+                for a in range(2):
+                    narrow_passes(acc, a, pair, j * 256)
+                staged = sb.tile([P, 2, 256], F32, name="staged", tag="staged", bufs=8)
+                copy_on(("vector", "scalar", "vector", "scalar")[2 * j + pair], staged[:], acc[:])
+                rows = out[2 * pair * P : (2 * pair + 2) * P, j * 256 : (j + 1) * 256]
+                nc.sync.dma_start(out=rows.rearrange("(i p) n -> p i n", p=P), in_=staged[:])
+        for nt in range(4):
+            acc = ps.tile([P, BANK], F32, name="res_b", tag="turn", bufs=BANKS["turn"])
+            for a in range(2):
+                second_pass(acc[:], a, nt, BANK, NP, a == 0, a == 1)
+            staged = sb.tile([P, BANK], F32, name="staged", tag="staged", bufs=8)
+            copy_on(("scalar", "vector")[nt % 2], staged[:], acc[:])
+            nc.sync.dma_start(out=out[nt * P : (nt + 1) * P, BANK:], in_=staged[:])

@@ -24,6 +24,7 @@ W1_BLOCKS = ((0,), (1,), (2, 3), (4, 5), (6, 7))
 BANKS = {"turn": 4, "acc": 2, "res": 2}
 LN_GROUPS = ((0, 1, 2), (3, 4), (5, 6))
 KNEE = 30.0
+FLOOR = -3.0e38
 PIECES = (((0, 512), (512, 1024)), ((0, 256), (256, 512), (512, 1024)))
 
 
@@ -50,11 +51,11 @@ def tile_list_vaccine_dispatch_kernel(
         w2s = sb.tile([P, 2, N], U8, name="w2s", align_bytes=64)
         ident = sb.tile([P, P], F32, name="ident")
         gain_last = sb.tile([P, 1], F32, name="gain_last")
-        gain_wide = sb.tile([P, 32, 4, 4], F32, name="gain_wide")
+        gain_wide = sb.tile([P, 1, P], F32, name="gain_wide")
         gain_rows = sb.tile([P, P], F32, name="gain_rows")
         factor = {
             name: sb.tile([P, TILES], F32, name=name)
-            for name in ("minus_gain", "minus_half_gain")
+            for name in ("minus_gain",)
         }
 
         raw, pages, stocks, quantised = {}, {}, {}, {}
@@ -150,30 +151,31 @@ def tile_list_vaccine_dispatch_kernel(
 
         def turn(terms, tag):
             blocks = terms[0].shape[1] // P
-            turned = ps.tile([P, 32, blocks, 4], F32, name="turned", tag=tag, bufs=BANKS[tag])
+            turned = ps.tile([P, blocks, P], F32, name="turned", tag=tag, bufs=BANKS[tag])
             for term, src in enumerate(terms):
                 for b in range(blocks):
                     nc.tensor.matmul(
-                        turned[:, :, b, :], src[:, b * P : (b + 1) * P], ident[:], is_transpose=True,
+                        turned[:, b, :], src[:, b * P : (b + 1) * P], ident[:], is_transpose=True,
                         start=(term == 0 and b == 0), stop=(term == len(terms) - 1 and b == blocks - 1),
                     )
             return turned
 
-        def by_words(t):
-            return t.rearrange("m p b (u e) -> m (b u) p e", u=2)
+        def pairs(t, u):
+            return t.rearrange("m b (p u e) -> m b u p e", u=2, e=2)[:, :, u, :, :]
 
         def sum_and_round(c, half, engine, tag="turn"):
             a, cc = divmod(c, 4)
             cols = half_cols(half)
-            turned = turn([signed[c][:, cols], sized[c][:, cols], stocks[c][:, cols], soft[c][half]], tag)
+            turned = turn([stocks[c][:, cols], sized[c][:, cols], soft[c][half]], tag)
             for lo, hi in PIECES[a]:
                 if lo // BANK == half:
-                    dst = zt[a, lo][:, :, cc * 32 : cc * 32 + 32, :]
-                    src = by_words(turned[:, :, lo % BANK // P : lo % BANK // P + (hi - lo) // P, :])
-                    if engine == "scalar":
-                        nc.scalar.activation(out=dst, in_=src, func=ACT.Copy, scale=-1.0)
-                    else:
-                        nc.vector.tensor_scalar(out=dst, in0=src, scalar1=-1.0, scalar2=None, op0=ALU.mult)
+                    for u in range(2):
+                        dst = zt[a, lo][:, u::2, cc * 32 : cc * 32 + 32, :]
+                        src = pairs(turned[:, lo % BANK // P : lo % BANK // P + (hi - lo) // P, :], u)
+                        if engine == "scalar":
+                            nc.scalar.activation(out=dst, in_=src, func=ACT.Copy, scale=-1.0)
+                        else:
+                            nc.vector.tensor_scalar(out=dst, in0=src, scalar1=-1.0, scalar2=None, op0=ALU.mult)
 
         def weave_z(a, lo, hi, engines, tag):
             woven[a, lo] = sb.tile([P, hi - lo, 2], F32, name=f"woven{a}_{lo}", tag=f"woven{a}_{lo}", align_bytes=64)
@@ -291,7 +293,7 @@ def tile_list_vaccine_dispatch_kernel(
         first_product(1)
         gain_t = ps.tile([P, P], F32, name="gain_t", tag="acc", bufs=BANKS["acc"])
         nc.tensor.transpose(gain_t[:], gain_rows[:], ident[:])
-        for name, by in (("minus_gain", -1.0), ("minus_half_gain", -0.5)):
+        for name, by in (("minus_gain", -1.0),):
             nc.scalar.activation(out=factor[name][:], in_=gain_t[:, 0:TILES], func=ACT.Copy, scale=by)
         fused_scatter(1, 0, BANK)
         fused_scatter(1, BANK, S)
@@ -304,7 +306,7 @@ def tile_list_vaccine_dispatch_kernel(
         for c in range(4):
             size[c] = early_size[:]
         for c in (4, 5):
-            size[c] = logs.tile([P, NP], F32, name=f"size{c}", offset=3 * 4096, align_bytes=64)[:]
+            size[c] = logs.tile([P, NP], F32, name=f"size{c}", offset=3 * 4096 + (c - 4) * 2048, align_bytes=64)[:]
         inverse_last = shared.tile([P, 1], F32, name="inverse_last", offset=3 * 4096)
         nc.vector.reciprocal(inverse_last[:], gain_last[:])
         gather(1, 0, NP)
@@ -332,7 +334,10 @@ def tile_list_vaccine_dispatch_kernel(
 
         def stream(c):
             weigh_and_scatter(c, 2 if c == 2 else 1)
-            if c < last:
+            if c == last - 1:
+                gather(c, 0, BANK)
+                gather(c, BANK, NP)
+            elif c < last:
                 gather(c, 0, NP)
             if c + 2 < TILES:
                 load_page(c + 2)
@@ -344,8 +349,8 @@ def tile_list_vaccine_dispatch_kernel(
                 nc.scalar.activation(out=size[c][:, cols], in_=got[c][:, cols], func=ACT.Abs)
             for half in range(2):
                 nc.scalar.activation(out=soft[c][half], in_=size[c][:, half_cols(half)], func=ACT.Exp, scale=-1.0)
-            times(nc.gpsimd, signed[c][:], got[c][:], "minus_half_gain", c)
-            times(nc.gpsimd, sized[c], size[c], "minus_half_gain", c)
+            times(nc.gpsimd, got[c][:], got[c][:], "minus_gain", c)
+            nc.gpsimd.tensor_scalar(out=sized[c], in0=got[c][:], scalar1=0.0, scalar2=FLOOR, op0=ALU.min, op1=ALU.max)
 
         def logarithm(group):
             for half in range(2):
@@ -378,7 +383,7 @@ def tile_list_vaccine_dispatch_kernel(
         nc.gpsimd.tensor_scalar(
             out=stock_over_gain[:], in0=stocks[last], scalar1=inverse_last[:], scalar2=-1.0, op0=ALU.mult, op1=ALU.mult
         )
-        spread = turn([gain_last[:].to_broadcast([P, BANK])], "res")
+        spread = turn([gain_last[:].to_broadcast([P, P])], "res")
         nc.scalar.copy(out=gain_wide[:], in_=spread[:])
         stream(7)
         for half in range(2):
@@ -392,8 +397,8 @@ def tile_list_vaccine_dispatch_kernel(
         logarithm(LN_GROUPS[1])
         scale_logs(LN_GROUPS[1])
         finish(3, "scalar")
-        soften(5)
         finish(4, "scalar")
+        soften(5)
         for half in range(2):
             weave_z(0, half * BANK, (half + 1) * BANK, ("scalar", "scalar"), ("res", "acc")[half])
         size[6] = sb.tile([P, NP], F32, name="size6", tag="zt0_512")[:]
@@ -427,9 +432,9 @@ def tile_list_vaccine_dispatch_kernel(
             nc.scalar.activation(out=soft_last[:, lo:hi], in_=soft_last[:, lo:hi], func=ACT.Ln, bias=1.0)
         for lo, hi in PIECES[1]:
             turned = turn([stock_over_gain[:, lo:hi], signed[last][:, lo:hi], soft_last[:, lo:hi]], "acc" if lo < BANK else "turn")
-            nc.vector.tensor_tensor(
-                zt[1, lo][:, :, 96:P, :], by_words(turned[:]), by_words(gain_wide[:, :, 0 : (hi - lo) // P, :]), ALU.mult
-            )
+            for u in range(2):
+                along = pairs(gain_wide[:], u).to_broadcast([P, (hi - lo) // P, 32, 2])
+                nc.vector.tensor_tensor(zt[1, lo][:, u::2, 96:P, :], pairs(turned[:], u), along, ALU.mult)
         for lo, hi in PIECES[1][:2]:
             weave_z(1, lo, hi, ("vector" if lo == 0 else "scalar",), "turn")
             quantise_z(1, lo, hi)

@@ -221,10 +221,16 @@ def tile_list_vaccine_dispatch_kernel(
         nc.sync.dma_start(list1[:], offs)
         nc.sync.dma_start(list2[:], offs2)
         nc.sync.dma_start(out=words[0][:], in_=tab_words[0].rearrange("p t i -> p (t i)").bitcast(I32))
-        for q in range(4):
-            nc.scalar.dma_start(
+        for q in range(2):
+            nc.gpsimd.dma_start(
                 out=planes[32 * q : 32 * q + 8, :].bitcast(I32), in_=tab_scales[:, 4 * q : 4 * q + 4, :].bitcast(I32)
             )
+        for q in range(2, 4):
+            for a in range(2):
+                nc.scalar.dma_start(
+                    out=planes[32 * q + 4 * a : 32 * q + 4 * a + 4, :].bitcast(I32),
+                    in_=tab_scales[a, 4 * q : 4 * q + 4, :].bitcast(I32),
+                )
         load_w1(W1_BLOCKS[0])
         nc.sync.dma_start(out=words[1][:], in_=tab_words[1].rearrange("p t i -> p (t i)").bitcast(I32))
         nc.sync.dma_start(out=weights[:, :BANK], in_=wgs[:, :BANK])

@@ -19,13 +19,13 @@ ACT = mybir.ActivationFunctionType
 
 P = 128
 BANK = 512
+PASS = 512
 TILES = H // P
-W1_BLOCKS = ((0,), (1,), (2, 3), (4, 5), (6, 7))
-BANKS = {"turn": 4, "acc": 2, "res": 2}
-LN_GROUPS = ((0, 1, 2), (3, 4), (5, 6))
-KNEE = 30.0
-FLOOR = -3.0e38
-PIECES = (((0, 512), (512, 1024)), ((0, 256), (256, 512), (512, 1024)))
+PLAIN = 4
+CHUNK = 256
+CHUNKS = NP // CHUNK
+HUGE = 3.0e38
+KB = 1024
 
 
 def tile_list_vaccine_dispatch_kernel(
@@ -33,70 +33,87 @@ def tile_list_vaccine_dispatch_kernel(
 ):
     nc = tc.nc
     with ExitStack() as ctx:
-        sb = ctx.enter_context(tc.tile_pool(name="sb", bufs=1))
-        shared = ctx.enter_context(tc.tile_pool(name="shared", bufs=1))
-        streamed = ctx.enter_context(tc.tile_pool(name="streamed", bufs=1))
-        logs = ctx.enter_context(tc.tile_pool(name="logs", bufs=1))
+        held = ctx.enter_context(tc.tile_pool(name="held", bufs=1))
+        arena = ctx.enter_context(tc.tile_pool(name="arena", bufs=1))
         ps = ctx.enter_context(tc.psum_pool(name="ps", bufs=1))
 
-        list1 = sb.tile([P, S // 16], U16, name="list1")
-        list2 = sb.tile([P, S // 16], U16, name="list2")
-        list3 = sb.tile([P, NP // 16], U16, name="list3")
-        words = [sb.tile([P, T], I32, name=f"words{a}", tag=f"wide{a}") for a in range(2)]
-        planes = sb.tile([P, T], U8, name="planes", tag="planes", align_bytes=64)
-        picked = [sb.tile([P, S], U32, name="picked0", align_bytes=64)]
-        picked_scales = sb.tile([P, S], U8, name="picked_scales", align_bytes=64)
-        weights = sb.tile([P, S], F32, name="weights")
-        w2c = sb.tile([P, 2, 2 * N], U8, name="w2c", align_bytes=64)
-        w2s = sb.tile([P, 2, N], U8, name="w2s", align_bytes=64)
-        ident = sb.tile([P, P], F32, name="ident")
-        gain_last = sb.tile([P, 1], F32, name="gain_last")
-        gain_wide = sb.tile([P, 1, P], F32, name="gain_wide")
-        gain_rows = sb.tile([P, P], F32, name="gain_rows")
-        factor = {
-            name: sb.tile([P, TILES], F32, name=name)
-            for name in ("minus_gain",)
-        }
+        def place(name, shape, dtype, kb):
+            return arena.tile([P] + shape, dtype, name=name, offset=int(kb * KB), align_bytes=64)
 
-        raw, pages, stocks, quantised = {}, {}, {}, {}
-        sums, put, got, soft, size, signed, sized = {}, {}, {}, {}, {}, {}, {}
+        def bank(name, shape, index):
+            return ps.tile([P] + shape, F32, name=name, offset=index * 2 * KB)
 
         def half_cols(half):
             return slice(half * BANK, (half + 1) * BANK)
 
-        def load_w1(block):
-            width = len(block) * P
-            t = streamed.tile([P, 2, 4, width], F32, name=f"w1_raw{block[0]}", offset=block[0] * 4096)
+        def rows_of(dram, c):
+            if c < PLAIN:
+                return dram[c * P : (c + 1) * P, :]
+            return dram[PASS:, :].rearrange("(p t) n -> p t n", t=4)[:, c - PLAIN, :]
+
+        list1 = held.tile([P, S // 16], U16, name="list1")
+        list2 = held.tile([P, S // 16], U16, name="list2")
+        list3 = held.tile([P, NP // 16], U16, name="list3")
+        ident = held.tile([P, P], F32, name="ident")
+        minus_gain = held.tile([P, PLAIN], F32, name="minus_gain")
+        gain_dealt = held.tile([P, 4], F32, name="gain_dealt")
+        ones = held.tile([P, 3], F32, name="ones")
+        w2c = held.tile([P, 2, 2 * N], U8, name="w2c", align_bytes=64)
+        w2s = held.tile([P, 2, N], U8, name="w2s", align_bytes=64)
+
+        WORDS, RAW, SLOT, PAGE, LATE, STAGE, PLANES = 0, 32, 65, 97, 125, 133, 141
+        EDGE = 1 / 16
+        PAGE_AT = (PAGE, PAGE + 8, PAGE + 16, 226) + (PAGE, PAGE + 8) * 2
+        words = [place(f"words{a}", [T], I32, WORDS + 16 * a) for a in range(2)]
+        planes = place("planes", [T], U8, PLANES)
+        picked = [place("picked0", [S], U32, 145)]
+        picked_scales = place("picked_scales", [S], U8, 149)
+        weights = place("weights", [S], F32, 160)
+        gain_rows = place("gain_rows", [P], F32, LATE)
+        raw = {0: place("raw0", [2, 4, P], F32, RAW), 1: place("raw1", [2, 4, P], F32, RAW + 4)}
+        raw23 = place("raw23", [2, 4, 2 * P], F32, RAW + 8)
+        raw_dealt = [place(f"raw_dealt{a}", [4, PASS], F32, RAW + 16 + 8 * a) for a in range(2)]
+        for i in range(2):
+            raw[2 + i] = raw23[:, :, :, i * P : (i + 1) * P]
+
+        pages, stocks, quantised = {}, {}, {}
+        sums, put, got, soft, size = {}, {}, {}, {}, {}
+        STOCK_AT = (RAW, SLOT, RAW + 12, 172, RAW + 16, 168, SLOT + 4, 164)
+
+        def load_w1(tile, first, width):
             for a in range(2):
-                rows = w1[a * BANK : (a + 1) * BANK, block[0] * P : block[0] * P + width]
-                nc.sync.dma_start(out=t[:, a, :, :], in_=rows.rearrange("(p j) c -> p j c", j=4))
-            for i, c in enumerate(block):
-                raw[c] = t[:, :, :, i * P : (i + 1) * P]
+                rows = w1[a * PASS : (a + 1) * PASS, first : first + width]
+                nc.sync.dma_start(out=tile[:, a, :, :], in_=rows.rearrange("(p j) c -> p j c", j=4))
+
+        def load_w1_dealt(a):
+            rows = w1[a * PASS : (a + 1) * PASS, PASS:]
+            nc.sync.dma_start(out=raw_dealt[a][:], in_=rows.rearrange("(p j) c -> p j c", j=4))
 
         def load_page(c):
-            pages[c] = sb.tile([P, T2], F32, name="page", tag="page", bufs=2)
-            nc.sync.dma_start(out=pages[c][:], in_=page0[c * P : (c + 1) * P, :])
+            pages[c] = place(f"page{c}", [T2], F32, PAGE_AT[c])
+            nc.sync.dma_start(out=pages[c][:], in_=rows_of(page0, c))
 
         def load_stock(c):
-            if c < TILES - 2:
-                stocks[c] = streamed.tile([P, NP], F32, name=f"stock{c}", offset=c * 4096)[:]
-            else:
-                stocks[c] = slot[c - (TILES - 2)]
-            nc.sync.dma_start(out=stocks[c], in_=stock[c * P : (c + 1) * P, :])
+            stocks[c] = place(f"stock{c}", [NP], F32, STOCK_AT[c])
+            nc.sync.dma_start(out=stocks[c][:], in_=rows_of(stock, c))
 
         def round_w1(c, stage, i):
             nc.scalar.copy(
                 out=stage[:, i * 1024 : (i + 1) * 1024].rearrange("p (a c i t) -> p a c t i", a=2, i=4, t=4),
-                in_=raw[c].rearrange("p a t (c i) -> p a c t i", i=4),
+                in_=raw[c][:].rearrange("p a t (c i) -> p a c t i", i=4),
+            )
+
+        def round_w1_dealt(a, stage):
+            nc.scalar.copy(
+                out=stage[:].rearrange("p (t a m j) -> p a m t j", t=4, a=2, j=4)[:, a, :, :, :],
+                in_=raw_dealt[a][:].rearrange("p j (m t) -> p m t j", t=4),
             )
 
         def quantise_w1(group, stage):
-            if group == (1,):
-                codes = shared.tile([P, 2 * P], U32, name="w1c1", offset=4096, align_bytes=64)
-            else:
-                codes = sb.tile([P, len(group) * 2 * P], U32, name=f"w1c{group[0]}", tag=f"w1c{group[0]}", align_bytes=64)
-            scales = sb.tile([P, len(group) * 2 * P], U8, name=f"w1s{group[0]}", tag=f"w1s{group[0]}", align_bytes=64)
-            nc.vector.quantize_mx(out=codes[:].bitcast(FP8X4), scales=scales[:], in_=stage[:, : len(group) * 1024])
+            first, count = group[0], len(group)
+            codes = place(f"w1c{first}", [count * 2 * P], U32, 150 + first if first else STAGE + 2)
+            scales = place(f"w1s{first}", [count * 2 * P], U8, 158 + first / 4 if first else STAGE + 4)
+            nc.vector.quantize_mx(out=codes[:].bitcast(FP8X4), scales=scales[:], in_=stage[:])
             for i, c in enumerate(group):
                 quantised[c] = (codes[:, i * 2 * P : (i + 1) * 2 * P], scales[:, i * 2 * P : (i + 1) * 2 * P])
 
@@ -104,7 +121,7 @@ def tile_list_vaccine_dispatch_kernel(
             codes, scales = quantised[c]
             for half in range(2):
                 cols = half_cols(half)
-                acc = ps.tile([P, BANK], F32, name="acc", tag="acc", bufs=2)
+                acc = bank(f"acc{c}_{half}", [BANK], 2 * (c % 2) + half)
                 for a in range(2):
                     nc.tensor.matmul_mx(
                         out=acc[:],
@@ -115,107 +132,69 @@ def tile_list_vaccine_dispatch_kernel(
                         start=(a == 0),
                         stop=(a == 1),
                     )
-                nc.scalar.copy(out=sums[c][:, cols], in_=acc[:])
+                nc.scalar.copy(out=sums[c][half], in_=acc[:])
 
-        def weigh_and_scatter(c, pieces):
-            width = S // pieces
-            for lo in range(0, S, width):
-                cols = slice(lo, lo + width)
-                nc.gpsimd.tensor_tensor(put[c][:, cols], sums[c][:, cols], weights[:, cols], ALU.mult)
-                nc.vector.tensor_copy(pages[c][:].indirect(list2[:, lo // 16 : (lo + width) // 16]), put[c][:, cols])
+        def halves_of(tile):
+            return [tile[:, half_cols(half)] for half in range(2)]
 
-        def fused_scatter(c, lo, hi):
-            nc.vector.tensor_tensor(
-                pages[c][:].indirect(list2[:, lo // 16 : hi // 16]), sums[c][:, lo:hi], weights[:, lo:hi], ALU.mult
-            )
+        def scatter(c, lo, hi):
+            nc.vector.tensor_copy(pages[c][:].indirect(list2[:, lo // 16 : hi // 16]), put[c][:, lo:hi])
 
         def gather(c, lo, hi):
             nc.vector.tensor_copy(got[c][:, lo:hi], pages[c][:].indirect(list3[:, lo // 16 : hi // 16]))
 
-        def times(engine, dst, src, name, c):
-            by = factor[name][:, c : c + 1]
-            engine.tensor_scalar(out=dst, in0=src, scalar1=by, scalar2=0.0, op0=ALU.mult, op1=ALU.add)
+        def times(dst, src, by):
+            nc.gpsimd.tensor_scalar(out=dst, in0=src, scalar1=by, scalar2=0.0, op0=ALU.mult, op1=ALU.add)
 
-        zt = {
-            (a, lo): sb.tile([P, (hi - lo) // 64, P, 2], BF16, name=f"zt{a}_{lo}", tag=f"zt{a}_{lo}")
-            for a in range(2)
-            for lo, hi in PIECES[a]
-        }
-        zc, zs, woven = {}, {}, {}
+        def exponentials(c):
+            for half in range(2):
+                nc.scalar.activation(out=size[c][:, half_cols(half)], in_=got[c][:, half_cols(half)], func=ACT.Abs)
+            for half in range(2):
+                nc.scalar.activation(
+                    out=soft[c][:, half_cols(half)], in_=size[c][:, half_cols(half)], func=ACT.Exp, scale=-1.0
+                )
 
-        def copy_on(engine, dst, src):
-            if engine == "scalar":
-                nc.scalar.copy(out=dst, in_=src)
-            else:
-                nc.vector.tensor_copy(out=dst, in_=src)
+        def logarithms(pair, one):
+            for half in range(2):
+                t = pair[:, :, half_cols(half)]
+                nc.scalar.activation(out=t, in_=t, func=ACT.Ln, bias=one)
 
-        def turn(terms, tag):
-            blocks = terms[0].shape[1] // P
-            turned = ps.tile([P, blocks, P], F32, name="turned", tag=tag, bufs=BANKS[tag])
-            for term, src in enumerate(terms):
-                for b in range(blocks):
-                    nc.tensor.matmul(
-                        turned[:, b, :], src[:, b * P : (b + 1) * P], ident[:], is_transpose=True,
-                        start=(term == 0 and b == 0), stop=(term == len(terms) - 1 and b == blocks - 1),
-                    )
-            return turned
+        def minus_relu(c):
+            for t in halves_of(got[c]):
+                times(t, t, minus_gain[:, c : c + 1])
+            for t in halves_of(got[c]):
+                nc.gpsimd.tensor_scalar(out=t, in0=t, scalar1=0.0, scalar2=-HUGE, op0=ALU.min, op1=ALU.max)
 
         def pairs(t, u):
             return t.rearrange("m b (p u e) -> m b u p e", u=2, e=2)[:, :, u, :, :]
 
-        def sum_and_round(c, half, engine, tag="turn"):
-            a, cc = divmod(c, 4)
+        def sum_and_round(c, half, zt):
             cols = half_cols(half)
-            turned = turn([stocks[c][:, cols], sized[c][:, cols], soft[c][half]], tag)
-            for lo, hi in PIECES[a]:
-                if lo // BANK == half:
-                    for u in range(2):
-                        dst = zt[a, lo][:, u::2, cc * 32 : cc * 32 + 32, :]
-                        src = pairs(turned[:, lo % BANK // P : lo % BANK // P + (hi - lo) // P, :], u)
-                        if engine == "scalar":
-                            nc.scalar.activation(out=dst, in_=src, func=ACT.Copy, scale=-1.0)
-                        else:
-                            nc.vector.tensor_scalar(out=dst, in0=src, scalar1=-1.0, scalar2=None, op0=ALU.mult)
-
-        def weave_z(a, lo, hi, engines, tag):
-            woven[a, lo] = sb.tile([P, hi - lo, 2], F32, name=f"woven{a}_{lo}", tag=f"woven{a}_{lo}", align_bytes=64)
-            for pair in range((hi - lo) // 256):
-                back = ps.tile([P, 2, 2, P], F32, name="back", tag=tag, bufs=BANKS[tag])
-                for b in range(2):
-                    for u in range(2):
-                        src = zt[a, lo][:, (pair * 2 + b) * 2 + u, :, :].rearrange("m p e -> m (p e)").bitcast(F32)
-                        nc.tensor.transpose(back[:, b, u, :], src, ident[:])
-                copy_on(
-                    engines[pair],
-                    woven[a, lo][:, pair * 256 : (pair + 1) * 256, :].rearrange("p (b m) u -> p b m u", b=2),
-                    back[:].rearrange("p b u m -> p b m u"),
-                )
-
-        def quantise_z(a, lo, hi):
-            nc.vector.quantize_mx(
-                out=zc[a, lo].bitcast(FP8X4), scales=zs[a][:, lo:hi],
-                in_=woven[a, lo][:].rearrange("p m u -> p (m u)").bitcast(BF16),
-            )
-
-        def second_pass(acc, a, nt, lo, hi, start, stop):
-            first = max(x for x, end in PIECES[a] if x <= lo)
-            nc.tensor.matmul_mx(
-                out=acc,
-                lhsT=w2c[:, a, nt * 2 * P : (nt + 1) * 2 * P].bitcast(FP4X4),
-                lhsT_scale=w2s[:, a, nt * P : (nt + 1) * P],
-                rhs=zc[a, first][:, lo - first : hi - first].bitcast(FP8X4),
-                rhs_scale=zs[a][:, lo:hi],
-                start=start,
-                stop=stop,
-            )
-
-        def narrow_passes(acc, a, pair, lo):
-            for i in range(2):
-                for s in range(2):
-                    second_pass(
-                        acc[:, i, s * P : (s + 1) * P], a, 2 * pair + i, lo + s * P, lo + (s + 1) * P,
-                        a == 0 and i == 0 and s == 0, a == 1 and i == 1 and s == 1,
+            turned = bank(f"turned{c}_{half}", [4, P], 4 + 2 * (c % 2) + half)
+            terms = [got[c][:, cols], stocks[c][:, cols], soft[c][:, cols]]
+            for term, src in enumerate(terms):
+                for b in range(4):
+                    nc.tensor.matmul(
+                        turned[:, b, :], src[:, b * P : (b + 1) * P], ident[:], is_transpose=True,
+                        start=(term == 0 and b == 0), stop=(term == 2 and b == 3),
                     )
+            for u in range(2):
+                dst = zt[:, 8 * half + u : 8 * half + 8 : 2, c * 32 : c * 32 + 32, :]
+                nc.scalar.activation(out=dst, in_=pairs(turned[:], u), func=ACT.Copy, scale=-1.0)
+
+        def second_pass(acc, a, pair, j, codes, scales):
+            cols = slice(j * CHUNK, (j + 1) * CHUNK)
+            for i in range(2):
+                nt = 2 * pair + i
+                nc.tensor.matmul_mx(
+                    out=acc[:, i, :],
+                    lhsT=w2c[:, a, nt * 2 * P : (nt + 1) * 2 * P].bitcast(FP4X4),
+                    lhsT_scale=w2s[:, a, nt * P : (nt + 1) * P],
+                    rhs=codes[:, cols].bitcast(FP8X4),
+                    rhs_scale=scales[:, cols],
+                    start=(a == 0 and i == 0),
+                    stop=(a == 1 and i == 1),
+                )
 
         nc.vector.memset(planes[:].bitcast(I32), 0)
         nc.sync.dma_start(list1[:], offs)
@@ -231,234 +210,257 @@ def tile_list_vaccine_dispatch_kernel(
                     out=planes[32 * q + 4 * a : 32 * q + 4 * a + 4, :].bitcast(I32),
                     in_=tab_scales[a, 4 * q : 4 * q + 4, :].bitcast(I32),
                 )
-        load_w1(W1_BLOCKS[0])
+        load_w1(raw[0], 0, P)
         nc.sync.dma_start(out=words[1][:], in_=tab_words[1].rearrange("p t i -> p (t i)").bitcast(I32))
         nc.sync.dma_start(out=weights[:, :BANK], in_=wgs[:, :BANK])
         load_page(0)
         nc.sync.dma_start(out=weights[:, BANK:], in_=wgs[:, BANK:])
-        load_w1(W1_BLOCKS[1])
+        load_w1(raw[1], P, P)
         nc.sync.dma_start(list3[:], offs3)
         nc.gpsimd.memset(gain_rows[:], 0.0)
-        nc.sync.dma_start(out=gain_rows[0:TILES, :], in_=gain.rearrange("(c p) -> c p", p=P))
-        load_w1(W1_BLOCKS[2])
+        nc.sync.dma_start(out=gain_rows[0:PLAIN, :], in_=gain[:PASS].rearrange("(c p) -> c p", p=P))
+        load_w1(raw23, 2 * P, 2 * P)
+        load_w1_dealt(0)
         load_page(1)
-        nc.sync.dma_start(out=gain_last[:], in_=gain[H - P : H].rearrange("(p o) -> p o", o=1))
-        load_w1(W1_BLOCKS[3])
-        load_w1(W1_BLOCKS[4])
+        load_w1_dealt(1)
+        nc.sync.dma_start(out=gain_dealt[:], in_=gain[PASS:].rearrange("(p t) -> p t", t=4))
+        load_page(2)
 
         make_identity(nc, ident[:])
         nc.gpsimd.memset(w2s[:].rearrange("p a n -> p (a n)").bitcast(I32), 0)
 
         nc.vector.tensor_copy(picked[0][:], words[0][:].bitcast(U32).indirect(list1[:]))
         nc.vector.tensor_copy(picked_scales[:], planes[:].indirect(list1[:]))
-        stage0 = sb.tile([P, 1024], BF16, name="stage0", align_bytes=64)
+        stage0 = place("stage0", [1024], BF16, STAGE)
         round_w1(0, stage0, 0)
         quantise_w1((0,), stage0)
-        picked.append(sb.tile([P, S], U32, name="picked1", tag="planes", align_bytes=64))
+        picked.append(place("picked1", [S], U32, PLANES))
         for half in range(2):
             nc.vector.tensor_copy(
                 picked[1][:, half_cols(half)],
                 words[1][:].bitcast(U32).indirect(list1[:, half * 32 : (half + 1) * 32]),
             )
-        slots = [sb.tile([P, 4, S], F32, name=f"slots{a}", tag=f"wide{a}") for a in range(2)]
-        slot = [slots[i // 4][:, i % 4, :] for i in range(TILES)]
-        sums[0] = shared.tile([P, S], F32, name="sums0", offset=0, align_bytes=64)
-        for c, offset in ((1, 2 * 4096), (2, 6 * 4096), (3, 7 * 4096)):
-            sums[c] = streamed.tile([P, S], F32, name=f"sums{c}", offset=offset)[:]
-        for c in range(4, TILES):
-            sums[c] = slot[c - 2]
-        last = TILES - 1
-        for c in range(last):
-            sized[c] = sums[c + 2] if c + 2 < TILES else slot[c]
-        size[last] = slot[last]
-        softs = [
-            logs.tile([P, count, NP], F32, name=f"softs{i}", offset=offset, align_bytes=64)
-            for i, (count, offset) in enumerate(((4, 0), (2, 4 * 4096), (3, 0)))
-        ]
-        for group, t in zip(LN_GROUPS, softs):
-            for i, c in enumerate(group):
-                soft[c] = [t[:, i, half_cols(half)] for half in range(2)]
-        soft_last = logs.tile([P, NP], F32, name="soft_last", offset=0, align_bytes=64)
-        soft[last] = [soft_last[:, half_cols(half)] for half in range(2)]
+
+        sums_at = {1: RAW + 8, 2: RAW + 24 + EDGE, 3: RAW + 28 + EDGE}
+        whole = {c: place(f"sums{c}", [S], F32, sums_at.get(c, SLOT + 4 * c)) for c in range(TILES)}
+        for c in range(TILES):
+            sums[c] = halves_of(whole[c])
+
+        def weighted_scatter(c):
+            for half in range(2):
+                offsets = list2[:, half * 32 : (half + 1) * 32]
+                nc.vector.tensor_tensor(pages[c][:].indirect(offsets), sums[c][half], weights[:, half_cols(half)], ALU.mult)
 
         first_product(0)
-        fused_scatter(0, 0, BANK)
-        fused_scatter(0, BANK, S)
-
-        stage1 = sb.tile([P, 1024], BF16, name="stage1", tag="w1c0", align_bytes=64)
+        weighted_scatter(0)
+        stage1 = place("stage1", [1024], BF16, STAGE + 2)
         round_w1(1, stage1, 0)
         quantise_w1((1,), stage1)
-        got[0] = sb.tile([P, NP], F32, name="got0", tag="w1c0", align_bytes=64)
+        got[0] = place("got0", [NP], F32, RAW + 4)
         gather(0, 0, NP)
-        load_page(2)
-        stage23 = sb.tile([P, 2048], BF16, name="stage23", tag="w1s0", align_bytes=64)
+        stage23 = place("stage23", [2048], BF16, STAGE + 4)
         round_w1(2, stage23, 0)
         round_w1(3, stage23, 1)
         quantise_w1((2, 3), stage23)
-        stage47 = shared.tile([P, 6160], BF16, name="stage47", offset=0, align_bytes=64)
         first_product(1)
-        gain_t = ps.tile([P, P], F32, name="gain_t", tag="acc", bufs=BANKS["acc"])
+        weighted_scatter(1)
+        gain_t = bank("gain_t", [P], 3)
         nc.tensor.transpose(gain_t[:], gain_rows[:], ident[:])
-        for name, by in (("minus_gain", -1.0),):
-            nc.scalar.activation(out=factor[name][:], in_=gain_t[:, 0:TILES], func=ACT.Copy, scale=by)
-        fused_scatter(1, 0, BANK)
-        fused_scatter(1, BANK, S)
-        for c in range(4, TILES):
-            round_w1(c, stage47, c - 4)
-        quantise_w1((4, 5, 6, 7), stage47)
-        got[1] = shared.tile([P, NP], F32, name="got1", offset=4096, align_bytes=64)
-        put[2] = shared.tile([P, S], F32, name="put2", offset=0, align_bytes=64)
-        early_size = shared.tile([P, NP], F32, name="early_size", offset=8192, align_bytes=64)
-        for c in range(4):
-            size[c] = early_size[:]
-        for c in (4, 5):
-            size[c] = logs.tile([P, NP], F32, name=f"size{c}", offset=3 * 4096 + (c - 4) * 2048, align_bytes=64)[:]
-        inverse_last = shared.tile([P, 1], F32, name="inverse_last", offset=3 * 4096)
-        nc.vector.reciprocal(inverse_last[:], gain_last[:])
+        nc.scalar.activation(out=minus_gain[:], in_=gain_t[:, 0:PLAIN], func=ACT.Copy, scale=-1.0)
+        stage_dealt = place("stage_dealt", [4096], BF16, LATE - EDGE)
+        for a in range(2):
+            round_w1_dealt(a, stage_dealt)
+        quantise_w1((4, 5, 6, 7), stage_dealt)
+        got[1] = place("got1", [NP], F32, RAW + 20 + EDGE)
         gather(1, 0, NP)
+        inverse_last = place("inverse_last", [1], F32, RAW + 20)
+        nc.vector.reciprocal(inverse_last[:], gain_dealt[:, 3:4])
+
+        dealt = place("dealt", [4 * S], F32, WORDS)
+        for q in (0, 2, 1, 3):
+            nc.sync.dma_start(out=dealt[32 * q : 32 * q + 32, :], in_=wgs.rearrange("(q t) j -> q (t j)", t=4))
         load_page(3)
         for c in range(TILES):
             load_stock(c)
         for a in range(2):
             nc.sync.dma_start(out=w2c[:, a, :].bitcast(I32), in_=w2_words[a].bitcast(I32))
         for q in range(4):
-            nc.sync.dma_start(
-                out=w2s[32 * q : 32 * q + 4, :, :].bitcast(I32),
-                in_=w2_scales[:, 4 * q : 4 * q + 4, :].rearrange("a r n -> r a n").bitcast(I32),
-            )
+            for a in range(2):
+                nc.sync.dma_start(
+                    out=w2s[32 * q : 32 * q + 4, a, :].bitcast(I32), in_=w2_scales[a, 4 * q : 4 * q + 4, :].bitcast(I32)
+                )
 
+        load_page(4)
+        load_page(5)
 
-        for c in range(3, TILES):
-            put[c] = sb.tile([P, S], F32, name=f"put{c}", tag=f"put{c}", align_bytes=64)
-        for c in range(2, TILES - 1):
-            got[c] = put[c]
-        got[last] = sb.tile([P, NP], F32, name="got_last")
-        for c in range(last):
-            signed[c] = got[c]
+        for c in (2, 3):
+            put[c] = place(f"put{c}", [S], F32, LATE - 4 + 8 * (c - 2))
+        got[2] = place("got2", [NP], F32, SLOT + 8)
+        put[4] = got[4] = place("put4", [S], F32, SLOT + 12)
+        for c in range(PLAIN + 1, TILES):
+            put[c] = whole[c]
+            got[c] = whole[c]
+        softs = [place(f"softs{i}", [2, NP], F32, kb) for i, kb in enumerate((16, 24, 176))]
+        for c in range(6):
+            soft[c] = softs[c // 2][:, c % 2, :]
+        early_size = place("early_size", [NP], F32, LATE)
+        for c in range(3):
+            size[c] = early_size
+
+        def weigh(c, lo, hi):
+            by = weights[:, lo:hi] if c < PLAIN else dealt[:, (c - PLAIN) * S + lo : (c - PLAIN) * S + hi]
+            nc.gpsimd.tensor_tensor(put[c][:, lo:hi], whole[c][:, lo:hi], by, ALU.mult)
+
+        def stream(c, cuts=(0, NP)):
+            scatter(c, 0, S)
+            for lo, hi in zip(cuts, cuts[1:]):
+                gather(c, lo, hi)
+
         first_product(2)
         first_product(3)
-
-        def stream(c):
-            weigh_and_scatter(c, 2 if c == 2 else 1)
-            if c == last - 1:
-                gather(c, 0, BANK)
-                gather(c, BANK, NP)
-            elif c < last:
-                gather(c, 0, NP)
-            if c + 2 < TILES:
-                load_page(c + 2)
-                first_product(c + 2)
-
-        def soften(c):
-            for half in range(2):
-                cols = half_cols(half)
-                nc.scalar.activation(out=size[c][:, cols], in_=got[c][:, cols], func=ACT.Abs)
-            for half in range(2):
-                nc.scalar.activation(out=soft[c][half], in_=size[c][:, half_cols(half)], func=ACT.Exp, scale=-1.0)
-            times(nc.gpsimd, got[c][:], got[c][:], "minus_gain", c)
-            nc.gpsimd.tensor_scalar(out=sized[c], in0=got[c][:], scalar1=0.0, scalar2=FLOOR, op0=ALU.min, op1=ALU.max)
-
-        def logarithm(group):
-            for half in range(2):
-                t = softs[LN_GROUPS.index(group)][:, 0 : len(group), half_cols(half)]
-                nc.scalar.activation(out=t, in_=t, func=ACT.Ln, bias=1.0)
-
-        def scale_logs(group):
-            for half in range(2):
-                for c in group:
-                    times(nc.gpsimd, soft[c][half], soft[c][half], "minus_gain", c)
-
-        def finish(c, engine, tag="turn"):
-            for half in range(2):
-                sum_and_round(c, half, engine, tag)
-
-        stream(2)
+        for half in range(2):
+            weigh(2, half * BANK, (half + 1) * BANK)
+            scatter(2, half * BANK, (half + 1) * BANK)
+        gather(2, 0, NP)
+        weigh(3, 0, S)
+        exponentials(0)
+        minus_relu(0)
+        first_product(4)
+        first_product(5)
+        weigh(4, 0, S)
+        got[3] = place("got3", [NP], F32, SLOT + 16)
         stream(3)
-        soften(0)
         stream(4)
-        soften(1)
+        load_page(6)
+        exponentials(1)
+        minus_relu(1)
+        logarithms(softs[0], 1.0)
+        for c in (0, 1):
+            times(soft[c], soft[c], minus_gain[:, c : c + 1])
+        first_product(6)
+        first_product(7)
+        weigh(5, 0, S)
         stream(5)
-        soften(2)
-        logarithm(LN_GROUPS[0])
-        scale_logs(LN_GROUPS[0])
-        stream(6)
-        soften(3)
-        for c in LN_GROUPS[0]:
-            finish(c, "scalar", "res" if c == 2 else "turn")
-        stock_over_gain = sb.tile([P, NP], F32, name="stock_over_gain", tag="w1c0", align_bytes=64)
-        nc.gpsimd.tensor_scalar(
-            out=stock_over_gain[:], in0=stocks[last], scalar1=inverse_last[:], scalar2=-1.0, op0=ALU.mult, op1=ALU.mult
-        )
-        spread = turn([gain_last[:].to_broadcast([P, P])], "res")
-        nc.scalar.copy(out=gain_wide[:], in_=spread[:])
-        stream(7)
-        for half in range(2):
-            cols = half_cols(half)
-            gather(last, half * BANK, half * BANK + BANK // 2)
-            gather(last, half * BANK + BANK // 2, (half + 1) * BANK)
-            nc.vector.tensor_scalar(
-                out=size[last][:, cols], in0=got[last][:, cols], scalar1=KNEE, scalar2=None, op0=ALU.min
-            )
-        soften(4)
-        logarithm(LN_GROUPS[1])
-        scale_logs(LN_GROUPS[1])
-        finish(3, "scalar")
-        finish(4, "scalar")
-        soften(5)
-        for half in range(2):
-            weave_z(0, half * BANK, (half + 1) * BANK, ("scalar", "scalar"), ("res", "acc")[half])
-        size[6] = sb.tile([P, NP], F32, name="size6", tag="zt0_512")[:]
-        soften(6)
-        logarithm(LN_GROUPS[2])
-        scale_logs(LN_GROUPS[2])
-        sum_and_round(5, 0, "scalar")
-        sum_and_round(5, 1, "vector")
-        sum_and_round(6, 0, "vector")
+        load_page(7)
+        exponentials(2)
+        minus_relu(2)
+        zt = place("zt", [16, P, 2], BF16, 218)
+        for c in (0, 1):
+            for half in range(2):
+                sum_and_round(c, half, zt)
+        weigh(6, 0, S)
+        stream(6, (0, BANK, NP))
+        size[3] = size[4] = place("mid_size", [NP], F32, 16)
+        exponentials(3)
+        minus_relu(3)
+        logarithms(softs[1], 1.0)
+        nc.scalar.activation(out=ones[:, 2:3], in_=soft[3][:, 0:1], func=ACT.Exp, scale=0.0)
+        for c in (2, 3):
+            times(soft[c], soft[c], minus_gain[:, c : c + 1])
+        weigh(7, 0, S)
+        stream(7, range(0, NP + 1, CHUNK))
 
-        codes0 = logs.tile([P, NP], U32, name="zc0", offset=4096, align_bytes=64)
+        exponentials(4)
+        nc.scalar.activation(out=got[4][:], in_=got[4][:], func=ACT.Relu, scale=gain_dealt[:, 0:1])
+        nc.gpsimd.tensor_tensor(got[4][:], got[4][:], stocks[4][:], ALU.subtract)
         for half in range(2):
-            zc[0, half * BANK] = codes0[:, half_cols(half)]
-        signed[last] = logs.tile([P, NP], F32, name="signed_last", offset=2 * 4096, align_bytes=64)
-        for lo, hi in PIECES[1]:
-            zc[1, lo] = sb.tile([P, hi - lo], U32, name=f"zc1_{lo}", align_bytes=64)[:]
-        for a in range(2):
-            zs[a] = sb.tile([P, NP], U8, name=f"zs{a}", align_bytes=64)
+            for c in (2, 3):
+                sum_and_round(c, half, zt)
+        woven0 = place("woven0", [NP, 2], F32, STAGE)
+        for j in range(CHUNKS):
+            back = bank(f"back{j}", [2, 2, P], j)
+            for b in range(2):
+                for u in range(2):
+                    src = zt[:, (2 * j + b) * 2 + u, :, :].rearrange("m p e -> m (p e)").bitcast(F32)
+                    nc.tensor.transpose(back[:, b, u, :], src, ident[:])
+            nc.scalar.copy(
+                out=woven0[:, j * CHUNK : (j + 1) * CHUNK, :].rearrange("p (b m) u -> p b m u", b=2),
+                in_=back[:].rearrange("p b u m -> p b m u"),
+            )
+
+        size[5] = place("late_size", [NP], F32, 218)
+        exponentials(5)
+        for t in halves_of(got[5]):
+            times(t, t, gain_dealt[:, 1:2])
+        for t in halves_of(got[5]):
+            nc.gpsimd.tensor_scalar(out=t, in0=t, scalar1=HUGE, scalar2=0.0, op0=ALU.min, op1=ALU.max)
+        for t, less in zip(halves_of(got[5]), halves_of(stocks[5])):
+            nc.gpsimd.tensor_tensor(t, t, less, ALU.subtract)
+        logarithms(softs[2], ones[:, 2:3])
+        nc.scalar.activation(out=ones[:, 0:1], in_=soft[5][:, 0:1], func=ACT.Exp, scale=0.0)
+        planes_z = place("planes_z", [2, NP, 2], BF16, 196)
+        logs = place("logs", [2, NP], F32, 218)
+        scaled = (soft[4], logs[:, 0, :])
+        for e in range(2):
+            times(scaled[e], soft[PLAIN + e], gain_dealt[:, e : e + 1])
+        for e in range(2):
+            nc.gpsimd.tensor_tensor(planes_z[:, 0, :, e], scaled[e], got[PLAIN + e][:], ALU.add)
+
+        rests = place("rests", [2, NP], F32, 176)
+        size[6], soft[6] = logs[:, 1, :], place("soft6", [NP], F32, 184)[:]
+        exponentials(6)
+        nc.scalar.activation(out=got[6][:], in_=got[6][:], func=ACT.Relu, scale=gain_dealt[:, 2:3])
+        nc.gpsimd.tensor_tensor(rests[:, 0, :], got[6][:], stocks[6][:], ALU.subtract)
+        for t in halves_of(soft[6]):
+            nc.scalar.activation(out=t, in_=t, func=ACT.Ln, bias=ones[:, 0:1])
+        nc.scalar.activation(out=ones[:, 1:2], in_=soft[6][:, 0:1], func=ACT.Exp, scale=0.0)
+        nc.gpsimd.tensor_scalar(
+            out=logs[:, 0, :], in0=soft[6], scalar1=gain_dealt[:, 2:3], scalar2=inverse_last[:], op0=ALU.mult, op1=ALU.mult
+        )
+
+        last = TILES - 1
+        exp_last = place("exp_last", [NP], F32, 192)
+        spread = logs[:, 1, :].rearrange("p (j k i) -> p k j i", j=CHUNKS, k=CHUNKS)
+        for k in range(CHUNKS):
+            cols = slice(k * CHUNK, (k + 1) * CHUNK)
+            nc.scalar.activation(
+                out=spread[:, k, :, :], in_=got[last][:, cols].rearrange("p (j i) -> p j i", j=CHUNKS), func=ACT.Abs
+            )
+            nc.scalar.activation(
+                out=exp_last[:, cols].rearrange("p (j i) -> p j i", j=CHUNKS), in_=spread[:, k, :, :], func=ACT.Exp, scale=-1.0
+            )
+        codes0 = place("codes0", [NP], U32, PAGE_AT[last])
+        scales0 = place("scales0", [NP], U8, 216)
+        codes1 = place("codes1", [NP], U32, 212)
+        scales1 = place("scales1", [NP], U8, 217)
+        woven1 = place("woven1", [NP, 2], F32, 204)
         for half in range(2):
             cols = half_cols(half)
             nc.vector.tensor_scalar(
-                out=signed[last][:, cols], in0=got[last][:, cols], scalar1=KNEE, scalar2=0.0,
-                op0=ALU.subtract, op1=ALU.max,
+                out=rests[:, 1, cols], in0=got[last][:, cols], scalar1=0.0, scalar2=gain_dealt[:, 3:4], op0=ALU.max, op1=ALU.mult
             )
-            nc.scalar.activation(out=soft[last][half], in_=size[last][:, cols], func=ACT.Exp)
-            if half == 0:
-                quantise_z(0, 0, BANK)
-        sum_and_round(6, 1, "vector")
-        quantise_z(0, BANK, NP)
-        for lo, hi in PIECES[1]:
-            nc.scalar.activation(out=soft_last[:, lo:hi], in_=soft_last[:, lo:hi], func=ACT.Ln, bias=1.0)
-        for lo, hi in PIECES[1]:
-            turned = turn([stock_over_gain[:, lo:hi], signed[last][:, lo:hi], soft_last[:, lo:hi]], "acc" if lo < BANK else "turn")
-            for u in range(2):
-                along = pairs(gain_wide[:], u).to_broadcast([P, (hi - lo) // P, 32, 2])
-                nc.vector.tensor_tensor(zt[1, lo][:, u::2, 96:P, :], pairs(turned[:], u), along, ALU.mult)
-        for lo, hi in PIECES[1][:2]:
-            weave_z(1, lo, hi, ("vector" if lo == 0 else "scalar",), "turn")
-            quantise_z(1, lo, hi)
-        weave_z(1, BANK, NP, ("scalar", "scalar"), "turn")
-        quantise_z(1, BANK, NP)
-        for j in range(2):
+            nc.vector.quantize_mx(
+                out=codes0[:, cols].bitcast(FP8X4), scales=scales0[:, cols],
+                in_=woven0[:, cols, :].rearrange("p m u -> p (m u)").bitcast(BF16),
+            )
+            nc.vector.tensor_tensor(rests[:, 1, cols], rests[:, 1, cols], stocks[last][:, cols], ALU.subtract)
+        accs = [[bank(f"res{j}_{pair}", [2, CHUNK], 2 * j + pair) for pair in range(2)] for j in range(CHUNKS)]
+        for j in range(CHUNKS):
             for pair in range(2):
-                acc = ps.tile([P, 2, 256], F32, name="res", tag=("res", "acc")[j], bufs=2)
-                for a in range(2):
-                    narrow_passes(acc, a, pair, j * 256)
-                staged = sb.tile([P, 2, 256], F32, name="staged", tag="staged", bufs=8)
-                copy_on(("vector", "scalar", "vector", "scalar")[2 * j + pair], staged[:], acc[:])
-                rows = out[2 * pair * P : (2 * pair + 2) * P, j * 256 : (j + 1) * 256]
+                second_pass(accs[j][pair], 0, pair, j, codes0, scales0)
+        for j in range(CHUNKS):
+            cols = slice(j * CHUNK, (j + 1) * CHUNK)
+            nc.scalar.activation(out=logs[:, 1, cols], in_=exp_last[:, cols], func=ACT.Ln, bias=ones[:, 1:2])
+        for j in range(CHUNKS):
+            cols = slice(j * CHUNK, (j + 1) * CHUNK)
+            nc.vector.scalar_tensor_tensor(
+                out=planes_z[:, 1, cols, :], in0=logs[:, :, cols].rearrange("p e m -> p m e"), scalar=gain_dealt[:, 3:4],
+                in1=rests[:, :, cols].rearrange("p e m -> p m e"), op0=ALU.mult, op1=ALU.add,
+            )
+            nc.vector.tensor_copy(
+                out=woven1[:, cols, :],
+                in_=planes_z[:, :, cols, :].rearrange("p u m e -> p u (m e)").bitcast(F32).rearrange("p u m -> p m u"),
+            )
+            nc.vector.quantize_mx(
+                out=codes1[:, cols].bitcast(FP8X4), scales=scales1[:, cols],
+                in_=woven1[:, cols, :].rearrange("p m u -> p (m u)").bitcast(BF16),
+            )
+            for pair in range(2):
+                second_pass(accs[j][pair], 1, pair, j, codes1, scales1)
+                staged = place(f"staged{j}_{pair}", [2, CHUNK], F32, WORDS + 2 * (2 * j + pair))
+                if j == CHUNKS - 1 and pair == 1:
+                    nc.vector.tensor_copy(out=staged[:], in_=accs[j][pair][:])
+                else:
+                    nc.scalar.copy(out=staged[:], in_=accs[j][pair][:])
+                rows = out[2 * pair * P : (2 * pair + 2) * P, cols]
                 nc.sync.dma_start(out=rows.rearrange("(i p) n -> p i n", p=P), in_=staged[:])
-        for nt in range(4):
-            acc = ps.tile([P, BANK], F32, name="res_b", tag="turn", bufs=BANKS["turn"])
-            for a in range(2):
-                second_pass(acc[:], a, nt, BANK, NP, a == 0, a == 1)
-            staged = sb.tile([P, BANK], F32, name="staged", tag="staged", bufs=8)
-            copy_on(("scalar", "vector")[nt % 2], staged[:], acc[:])
-            nc.sync.dma_start(out=out[nt * P : (nt + 1) * P, BANK:], in_=staged[:])

@@ -40,8 +40,8 @@ def tile_list_vaccine_dispatch_kernel(
         def place(name, shape, dtype, kb):
             return arena.tile([P] + shape, dtype, name=name, offset=int(kb * KB), align_bytes=64)
 
-        def bank(name, shape, index):
-            return ps.tile([P] + shape, F32, name=name, offset=index * 2 * KB)
+        def bank(name, shape, index, dtype=F32):
+            return ps.tile([P] + shape, dtype, name=name, offset=index * 2 * KB)
 
         def half_cols(half):
             return slice(half * BANK, (half + 1) * BANK)
@@ -57,7 +57,8 @@ def tile_list_vaccine_dispatch_kernel(
         ident = held.tile([P, P], F32, name="ident")
         minus_gain = held.tile([P, PLAIN], F32, name="minus_gain")
         gain_dealt = held.tile([P, 4], F32, name="gain_dealt")
-        ones = held.tile([P, 3], F32, name="ones")
+        minus_dealt = held.tile([P, 2], F32, name="minus_dealt")
+        ones = held.tile([P, 2], F32, name="ones")
         w2c = held.tile([P, 2, 2 * N], U8, name="w2c", align_bytes=64)
         w2s = held.tile([P, 2, N], U8, name="w2s", align_bytes=64)
 
@@ -69,7 +70,7 @@ def tile_list_vaccine_dispatch_kernel(
         picked = [place("picked0", [S], U32, 145)]
         picked_scales = place("picked_scales", [S], U8, 149)
         weights = place("weights", [S], F32, 160)
-        gain_rows = place("gain_rows", [P], F32, LATE)
+        gain_rows = place("gain_rows", [P], F32, 234)
         raw = {0: place("raw0", [2, 4, P], F32, RAW), 1: place("raw1", [2, 4, P], F32, RAW + 4)}
         raw23 = place("raw23", [2, 4, 2 * P], F32, RAW + 8)
         raw_dealt = [place(f"raw_dealt{a}", [4, PASS], F32, RAW + 16 + 8 * a) for a in range(2)]
@@ -77,7 +78,7 @@ def tile_list_vaccine_dispatch_kernel(
             raw[2 + i] = raw23[:, :, :, i * P : (i + 1) * P]
 
         pages, stocks, quantised = {}, {}, {}
-        sums, put, got, soft, size = {}, {}, {}, {}, {}
+        sums, put, got, soft, size, bent, scaled = {}, {}, {}, {}, {}, {}, {}
         STOCK_AT = (RAW, SLOT, RAW + 12, 172, RAW + 16, 168, SLOT + 4, 164)
 
         def load_w1(tile, first, width):
@@ -112,7 +113,7 @@ def tile_list_vaccine_dispatch_kernel(
         def quantise_w1(group, stage):
             first, count = group[0], len(group)
             codes = place(f"w1c{first}", [count * 2 * P], U32, 150 + first if first else STAGE + 2)
-            scales = place(f"w1s{first}", [count * 2 * P], U8, 158 + first / 4 if first else STAGE + 4)
+            scales = place(f"w1s{first}", [count * 2 * P], U8, {0: STAGE + 4, 1: LATE + 1}.get(first, 158 + first / 4))
             nc.vector.quantize_mx(out=codes[:].bitcast(FP8X4), scales=scales[:], in_=stage[:])
             for i, c in enumerate(group):
                 quantised[c] = (codes[:, i * 2 * P : (i + 1) * 2 * P], scales[:, i * 2 * P : (i + 1) * 2 * P])
@@ -159,25 +160,37 @@ def tile_list_vaccine_dispatch_kernel(
                 t = pair[:, :, half_cols(half)]
                 nc.scalar.activation(out=t, in_=t, func=ACT.Ln, bias=one)
 
+        def minus_by(c):
+            return minus_gain[:, c : c + 1] if c < PLAIN else minus_dealt[:, c - PLAIN : c - PLAIN + 1]
+
         def minus_relu(c):
-            for t in halves_of(got[c]):
-                times(t, t, minus_gain[:, c : c + 1])
-            for t in halves_of(got[c]):
+            for t, src in zip(halves_of(bent[c]), halves_of(got[c])):
+                times(t, src, minus_by(c))
+            for t in halves_of(bent[c]):
                 nc.gpsimd.tensor_scalar(out=t, in0=t, scalar1=0.0, scalar2=-HUGE, op0=ALU.min, op1=ALU.max)
+
+        def scale_logs(pair):
+            for half in range(2):
+                for c in pair:
+                    times(scaled[c][:, half_cols(half)], soft[c][:, half_cols(half)], minus_by(c))
 
         def pairs(t, u):
             return t.rearrange("m b (p u e) -> m b u p e", u=2, e=2)[:, :, u, :, :]
 
-        def sum_and_round(c, half, zt):
+        def summed(c, half):
             cols = half_cols(half)
             turned = bank(f"turned{c}_{half}", [4, P], 4 + 2 * (c % 2) + half)
-            terms = [got[c][:, cols], stocks[c][:, cols], soft[c][:, cols]]
+            terms = [bent[c][:, cols], stocks[c][:, cols], scaled[c][:, cols]]
             for term, src in enumerate(terms):
                 for b in range(4):
                     nc.tensor.matmul(
                         turned[:, b, :], src[:, b * P : (b + 1) * P], ident[:], is_transpose=True,
                         start=(term == 0 and b == 0), stop=(term == 2 and b == 3),
                     )
+            return turned
+
+        def sum_and_round(c, half, zt):
+            turned = summed(c, half)
             for u in range(2):
                 dst = zt[:, 8 * half + u : 8 * half + 8 : 2, c * 32 : c * 32 + 32, :]
                 nc.scalar.activation(out=dst, in_=pairs(turned[:], u), func=ACT.Copy, scale=-1.0)
@@ -220,8 +233,8 @@ def tile_list_vaccine_dispatch_kernel(
         nc.gpsimd.memset(gain_rows[:], 0.0)
         nc.sync.dma_start(out=gain_rows[0:PLAIN, :], in_=gain[:PASS].rearrange("(c p) -> c p", p=P))
         load_w1(raw23, 2 * P, 2 * P)
-        load_w1_dealt(0)
         load_page(1)
+        load_w1_dealt(0)
         load_w1_dealt(1)
         nc.sync.dma_start(out=gain_dealt[:], in_=gain[PASS:].rearrange("(p t) -> p t", t=4))
         load_page(2)
@@ -256,6 +269,9 @@ def tile_list_vaccine_dispatch_kernel(
         stage1 = place("stage1", [1024], BF16, STAGE + 2)
         round_w1(1, stage1, 0)
         quantise_w1((1,), stage1)
+        gain_t = bank("gain_t", [P], 0)
+        nc.tensor.transpose(gain_t[:], gain_rows[:], ident[:])
+        nc.scalar.activation(out=minus_gain[:], in_=gain_t[:, 0:PLAIN], func=ACT.Copy, scale=-1.0)
         got[0] = place("got0", [NP], F32, RAW + 4)
         gather(0, 0, NP)
         stage23 = place("stage23", [2048], BF16, STAGE + 4)
@@ -264,34 +280,31 @@ def tile_list_vaccine_dispatch_kernel(
         quantise_w1((2, 3), stage23)
         first_product(1)
         weighted_scatter(1)
-        gain_t = bank("gain_t", [P], 3)
-        nc.tensor.transpose(gain_t[:], gain_rows[:], ident[:])
-        nc.scalar.activation(out=minus_gain[:], in_=gain_t[:, 0:PLAIN], func=ACT.Copy, scale=-1.0)
         stage_dealt = place("stage_dealt", [4096], BF16, LATE - EDGE)
         for a in range(2):
             round_w1_dealt(a, stage_dealt)
         quantise_w1((4, 5, 6, 7), stage_dealt)
         got[1] = place("got1", [NP], F32, RAW + 20 + EDGE)
         gather(1, 0, NP)
-        inverse_last = place("inverse_last", [1], F32, RAW + 20)
-        nc.vector.reciprocal(inverse_last[:], gain_dealt[:, 3:4])
+        times(minus_dealt[:], gain_dealt[:, 0:2], -1.0)
 
         dealt = place("dealt", [4 * S], F32, WORDS)
         for q in (0, 2, 1, 3):
             nc.sync.dma_start(out=dealt[32 * q : 32 * q + 32, :], in_=wgs.rearrange("(q t) j -> q (t j)", t=4))
         load_page(3)
-        for c in range(TILES):
+        load_page(4)
+        load_stock(0)
+        load_stock(1)
+        load_page(5)
+        for c in range(2, TILES):
             load_stock(c)
         for a in range(2):
             nc.sync.dma_start(out=w2c[:, a, :].bitcast(I32), in_=w2_words[a].bitcast(I32))
         for q in range(4):
-            for a in range(2):
-                nc.sync.dma_start(
-                    out=w2s[32 * q : 32 * q + 4, a, :].bitcast(I32), in_=w2_scales[a, 4 * q : 4 * q + 4, :].bitcast(I32)
-                )
-
-        load_page(4)
-        load_page(5)
+            nc.sync.dma_start(
+                out=w2s[32 * q : 32 * q + 4, :, :].bitcast(I32),
+                in_=w2_scales[:, 4 * q : 4 * q + 4, :].rearrange("a r n -> r a n").bitcast(I32),
+            )
 
         for c in (2, 3):
             put[c] = place(f"put{c}", [S], F32, LATE - 4 + 8 * (c - 2))
@@ -316,6 +329,10 @@ def tile_list_vaccine_dispatch_kernel(
             for lo, hi in zip(cuts, cuts[1:]):
                 gather(c, lo, hi)
 
+        for c in range(PLAIN):
+            bent[c] = got.get(c)
+        scaled[0], scaled[1] = soft[0], soft[1]
+
         first_product(2)
         first_product(3)
         for half in range(2):
@@ -328,7 +345,7 @@ def tile_list_vaccine_dispatch_kernel(
         first_product(4)
         first_product(5)
         weigh(4, 0, S)
-        got[3] = place("got3", [NP], F32, SLOT + 16)
+        got[3] = bent[3] = place("got3", [NP], F32, SLOT + 16)
         stream(3)
         stream(4)
         load_page(6)
@@ -336,7 +353,7 @@ def tile_list_vaccine_dispatch_kernel(
         minus_relu(1)
         logarithms(softs[0], 1.0)
         for c in (0, 1):
-            times(soft[c], soft[c], minus_gain[:, c : c + 1])
+            times(soft[c], soft[c], minus_by(c))
         first_product(6)
         first_product(7)
         weigh(5, 0, S)
@@ -354,15 +371,19 @@ def tile_list_vaccine_dispatch_kernel(
         exponentials(3)
         minus_relu(3)
         logarithms(softs[1], 1.0)
-        nc.scalar.activation(out=ones[:, 2:3], in_=soft[3][:, 0:1], func=ACT.Exp, scale=0.0)
-        for c in (2, 3):
-            times(soft[c], soft[c], minus_gain[:, c : c + 1])
-        weigh(7, 0, S)
-        stream(7, range(0, NP + 1, CHUNK))
+        nc.scalar.activation(out=ones[:, 0:1], in_=soft[3][:, 0:1], func=ACT.Exp, scale=0.0)
+        for i, kb in enumerate((141, 149)):
+            both = place(f"scaled{i}", [2, NP], F32, kb)
+            scaled[2 + 2 * i], scaled[3 + 2 * i] = both[:, 0, :], both[:, 1, :]
+        scale_logs((2, 3))
 
         exponentials(4)
-        nc.scalar.activation(out=got[4][:], in_=got[4][:], func=ACT.Relu, scale=gain_dealt[:, 0:1])
-        nc.gpsimd.tensor_tensor(got[4][:], got[4][:], stocks[4][:], ALU.subtract)
+        bent[4] = place("bent4", [NP], F32, 28)
+        minus_relu(4)
+        weigh(7, 0, S)
+        stream(7, range(0, NP + 1, CHUNK))
+        ident16 = place("ident16", [P], BF16, 157)
+        nc.scalar.copy(out=ident16[:], in_=ident[:])
         for half in range(2):
             for c in (2, 3):
                 sum_and_round(c, half, zt)
@@ -380,36 +401,37 @@ def tile_list_vaccine_dispatch_kernel(
 
         size[5] = place("late_size", [NP], F32, 218)
         exponentials(5)
-        for t in halves_of(got[5]):
-            times(t, t, gain_dealt[:, 1:2])
-        for t in halves_of(got[5]):
-            nc.gpsimd.tensor_scalar(out=t, in0=t, scalar1=HUGE, scalar2=0.0, op0=ALU.min, op1=ALU.max)
-        for t, less in zip(halves_of(got[5]), halves_of(stocks[5])):
-            nc.gpsimd.tensor_tensor(t, t, less, ALU.subtract)
-        logarithms(softs[2], ones[:, 2:3])
-        nc.scalar.activation(out=ones[:, 0:1], in_=soft[5][:, 0:1], func=ACT.Exp, scale=0.0)
-        planes_z = place("planes_z", [2, NP, 2], BF16, 196)
-        logs = place("logs", [2, NP], F32, 218)
-        scaled = (soft[4], logs[:, 0, :])
-        for e in range(2):
-            times(scaled[e], soft[PLAIN + e], gain_dealt[:, e : e + 1])
-        for e in range(2):
-            nc.gpsimd.tensor_tensor(planes_z[:, 0, :, e], scaled[e], got[PLAIN + e][:], ALU.add)
+        bent[5] = place("bent5", [NP], F32, 222)
+        minus_relu(5)
+        logarithms(softs[2], ones[:, 0:1])
+        nc.scalar.activation(out=ones[:, 1:2], in_=soft[5][:, 0:1], func=ACT.Exp, scale=0.0)
+        scale_logs((4, 5))
 
-        rests = place("rests", [2, NP], F32, 176)
-        size[6], soft[6] = logs[:, 1, :], place("soft6", [NP], F32, 184)[:]
+        exps = place("exps", [2, NP], F32, 184)
+        size[6], soft[6] = place("size6", [NP], F32, 218), exps[:, 0, :]
         exponentials(6)
-        nc.scalar.activation(out=got[6][:], in_=got[6][:], func=ACT.Relu, scale=gain_dealt[:, 2:3])
-        nc.gpsimd.tensor_tensor(rests[:, 0, :], got[6][:], stocks[6][:], ALU.subtract)
-        for t in halves_of(soft[6]):
-            nc.scalar.activation(out=t, in_=t, func=ACT.Ln, bias=ones[:, 0:1])
-        nc.scalar.activation(out=ones[:, 1:2], in_=soft[6][:, 0:1], func=ACT.Exp, scale=0.0)
-        nc.gpsimd.tensor_scalar(
-            out=logs[:, 0, :], in0=soft[6], scalar1=gain_dealt[:, 2:3], scalar2=inverse_last[:], op0=ALU.mult, op1=ALU.mult
-        )
+        rests = place("rests", [2, NP], F32, 176)
+        for t, src in zip(halves_of(rests[:, 0, :]), halves_of(got[6])):
+            times(t, src, gain_dealt[:, 2:3])
+        for t in halves_of(rests[:, 0, :]):
+            nc.gpsimd.tensor_scalar(out=t, in0=t, scalar1=HUGE, scalar2=0.0, op0=ALU.min, op1=ALU.max)
+        for t, less in zip(halves_of(rests[:, 0, :]), halves_of(stocks[6])):
+            nc.gpsimd.tensor_tensor(t, t, less, ALU.subtract)
+
+        planes_z = place("planes_z", [4, NP], BF16, 196)
+        turned16 = place("turned16", [2, 2, 4, P], BF16, 224)
+        for half in range(2):
+            for t in range(2):
+                nc.scalar.activation(out=turned16[:, t, half, :, :], in_=summed(PLAIN + t, half)[:], func=ACT.Copy, scale=-1.0)
+        for half in range(2):
+            for t in range(2):
+                back = bank(f"back16_{t}{half}", [4, P], 2 * half + t, BF16)
+                for b in range(4):
+                    nc.tensor.transpose(back[:, b, :], turned16[:, t, half, b, :], ident16[:])
+                nc.scalar.copy(out=planes_z[:, t, half_cols(half)], in_=back[:].rearrange("p b m -> p (b m)"))
 
         last = TILES - 1
-        exp_last = place("exp_last", [NP], F32, 192)
+        logs = place("logs", [2, NP], F32, 226)
         spread = logs[:, 1, :].rearrange("p (j k i) -> p k j i", j=CHUNKS, k=CHUNKS)
         for k in range(CHUNKS):
             cols = slice(k * CHUNK, (k + 1) * CHUNK)
@@ -417,13 +439,13 @@ def tile_list_vaccine_dispatch_kernel(
                 out=spread[:, k, :, :], in_=got[last][:, cols].rearrange("p (j i) -> p j i", j=CHUNKS), func=ACT.Abs
             )
             nc.scalar.activation(
-                out=exp_last[:, cols].rearrange("p (j i) -> p j i", j=CHUNKS), in_=spread[:, k, :, :], func=ACT.Exp, scale=-1.0
+                out=exps[:, 1, cols].rearrange("p (j i) -> p j i", j=CHUNKS), in_=spread[:, k, :, :], func=ACT.Exp, scale=-1.0
             )
         codes0 = place("codes0", [NP], U32, PAGE_AT[last])
-        scales0 = place("scales0", [NP], U8, 216)
+        scales0 = place("scales0", [NP], U8, 225)
         codes1 = place("codes1", [NP], U32, 212)
         scales1 = place("scales1", [NP], U8, 217)
-        woven1 = place("woven1", [NP, 2], F32, 204)
+        woven1 = place("woven1", [NP, 4], BF16, 204)
         for half in range(2):
             cols = half_cols(half)
             nc.vector.tensor_scalar(
@@ -440,20 +462,21 @@ def tile_list_vaccine_dispatch_kernel(
                 second_pass(accs[j][pair], 0, pair, j, codes0, scales0)
         for j in range(CHUNKS):
             cols = slice(j * CHUNK, (j + 1) * CHUNK)
-            nc.scalar.activation(out=logs[:, 1, cols], in_=exp_last[:, cols], func=ACT.Ln, bias=ones[:, 1:2])
+            nc.scalar.activation(out=logs[:, :, cols], in_=exps[:, :, cols], func=ACT.Ln, bias=ones[:, 1:2])
         for j in range(CHUNKS):
             cols = slice(j * CHUNK, (j + 1) * CHUNK)
-            nc.vector.scalar_tensor_tensor(
-                out=planes_z[:, 1, cols, :], in0=logs[:, :, cols].rearrange("p e m -> p m e"), scalar=gain_dealt[:, 3:4],
-                in1=rests[:, :, cols].rearrange("p e m -> p m e"), op0=ALU.mult, op1=ALU.add,
-            )
+            for e in range(2):
+                nc.vector.scalar_tensor_tensor(
+                    out=planes_z[:, 2 + e, cols], in0=logs[:, e, cols], scalar=gain_dealt[:, 2 + e : 3 + e],
+                    in1=rests[:, e, cols], op0=ALU.mult, op1=ALU.add,
+                )
             nc.vector.tensor_copy(
-                out=woven1[:, cols, :],
-                in_=planes_z[:, :, cols, :].rearrange("p u m e -> p u (m e)").bitcast(F32).rearrange("p u m -> p m u"),
+                out=woven1[:, cols, :].rearrange("p (c i) t -> p c t i", i=4),
+                in_=planes_z[:, :, cols].rearrange("p t (c i) -> p c t i", i=4),
             )
             nc.vector.quantize_mx(
                 out=codes1[:, cols].bitcast(FP8X4), scales=scales1[:, cols],
-                in_=woven1[:, cols, :].rearrange("p m u -> p (m u)").bitcast(BF16),
+                in_=woven1[:, cols, :].rearrange("p m t -> p (m t)"),
             )
             for pair in range(2):
                 second_pass(accs[j][pair], 1, pair, j, codes1, scales1)

@@ -24,6 +24,10 @@ TILES = H // P
 PLAIN = 4
 CHUNK = 256
 CHUNKS = NP // CHUNK
+PIECES = (0, 256, 512, 768, 1024)
+CUTS = (0, 256, 512, 768, 1024)
+COPIES_ON_VECTOR = (7,)
+WEAVES_ON_SCALAR = ()
 HUGE = 3.0e38
 KB = 1024
 
@@ -38,7 +42,7 @@ def tile_list_vaccine_dispatch_kernel(
         ps = ctx.enter_context(tc.psum_pool(name="ps", bufs=1))
 
         def place(name, shape, dtype, kb):
-            return arena.tile([P] + shape, dtype, name=name, offset=int(kb * KB), align_bytes=64)
+            return arena.tile([P] + list(shape), dtype, name=name, offset=int(kb * KB), align_bytes=64)
 
         def bank(name, shape, index, dtype=F32):
             return ps.tile([P] + shape, dtype, name=name, offset=index * 2 * KB)
@@ -58,13 +62,13 @@ def tile_list_vaccine_dispatch_kernel(
         minus_gain = held.tile([P, PLAIN], F32, name="minus_gain")
         gain_dealt = held.tile([P, 4], F32, name="gain_dealt")
         minus_dealt = held.tile([P, 2], F32, name="minus_dealt")
-        ones = held.tile([P, 2], F32, name="ones")
+        ones = held.tile([P, 3], F32, name="ones")
         w2c = held.tile([P, 2, 2 * N], U8, name="w2c", align_bytes=64)
         w2s = held.tile([P, 2, N], U8, name="w2s", align_bytes=64)
 
         WORDS, RAW, SLOT, PAGE, LATE, STAGE, PLANES = 0, 32, 65, 97, 125, 133, 141
         EDGE = 1 / 16
-        PAGE_AT = (PAGE, PAGE + 8, PAGE + 16, 226) + (PAGE, PAGE + 8) * 2
+        PAGE_AT = (PAGE, PAGE + 8, PAGE + 16, 226, PAGE, PAGE + 8, PAGE + 16, PAGE + 8)
         words = [place(f"words{a}", [T], I32, WORDS + 16 * a) for a in range(2)]
         planes = place("planes", [T], U8, PLANES)
         picked = [place("picked0", [S], U32, 145)]
@@ -195,10 +199,10 @@ def tile_list_vaccine_dispatch_kernel(
                 dst = zt[:, 8 * half + u : 8 * half + 8 : 2, c * 32 : c * 32 + 32, :]
                 nc.scalar.activation(out=dst, in_=pairs(turned[:], u), func=ACT.Copy, scale=-1.0)
 
-        def second_pass(acc, a, pair, j, codes, scales):
-            cols = slice(j * CHUNK, (j + 1) * CHUNK)
-            for i in range(2):
-                nt = 2 * pair + i
+        def second_pass(acc, first, a, cols, codes, scales):
+            count = acc.shape[1]
+            for i in range(count):
+                nt = first + i
                 nc.tensor.matmul_mx(
                     out=acc[:, i, :],
                     lhsT=w2c[:, a, nt * 2 * P : (nt + 1) * 2 * P].bitcast(FP4X4),
@@ -206,7 +210,7 @@ def tile_list_vaccine_dispatch_kernel(
                     rhs=codes[:, cols].bitcast(FP8X4),
                     rhs_scale=scales[:, cols],
                     start=(a == 0 and i == 0),
-                    stop=(a == 1 and i == 1),
+                    stop=(a == 1 and i == count - 1),
                 )
 
         nc.vector.memset(planes[:].bitcast(I32), 0)
@@ -288,15 +292,13 @@ def tile_list_vaccine_dispatch_kernel(
         gather(1, 0, NP)
         times(minus_dealt[:], gain_dealt[:, 0:2], -1.0)
 
+        load_page(3)
         dealt = place("dealt", [4 * S], F32, WORDS)
         for q in (0, 2, 1, 3):
             nc.sync.dma_start(out=dealt[32 * q : 32 * q + 32, :], in_=wgs.rearrange("(q t) j -> q (t j)", t=4))
-        load_page(3)
         load_page(4)
-        load_stock(0)
-        load_stock(1)
         load_page(5)
-        for c in range(2, TILES):
+        for c in range(TILES):
             load_stock(c)
         for a in range(2):
             nc.sync.dma_start(out=w2c[:, a, :].bitcast(I32), in_=w2_words[a].bitcast(I32))
@@ -308,16 +310,16 @@ def tile_list_vaccine_dispatch_kernel(
 
         for c in (2, 3):
             put[c] = place(f"put{c}", [S], F32, LATE - 4 + 8 * (c - 2))
-        got[2] = place("got2", [NP], F32, SLOT + 8)
-        put[4] = got[4] = place("put4", [S], F32, SLOT + 12)
-        for c in range(PLAIN + 1, TILES):
+        put[4] = place("put4", [S], F32, SLOT + 12)
+        put[5] = got[5] = place("put5", [S], F32, 192)
+        for c in range(PLAIN + 2, TILES):
             put[c] = whole[c]
             got[c] = whole[c]
         softs = [place(f"softs{i}", [2, NP], F32, kb) for i, kb in enumerate((16, 24, 176))]
         for c in range(6):
             soft[c] = softs[c // 2][:, c % 2, :]
         early_size = place("early_size", [NP], F32, LATE)
-        for c in range(3):
+        for c in range(2):
             size[c] = early_size
 
         def weigh(c, lo, hi):
@@ -329,8 +331,7 @@ def tile_list_vaccine_dispatch_kernel(
             for lo, hi in zip(cuts, cuts[1:]):
                 gather(c, lo, hi)
 
-        for c in range(PLAIN):
-            bent[c] = got.get(c)
+        bent[0], bent[1] = got[0], got[1]
         scaled[0], scaled[1] = soft[0], soft[1]
 
         first_product(2)
@@ -338,50 +339,53 @@ def tile_list_vaccine_dispatch_kernel(
         for half in range(2):
             weigh(2, half * BANK, (half + 1) * BANK)
             scatter(2, half * BANK, (half + 1) * BANK)
-        gather(2, 0, NP)
         weigh(3, 0, S)
+        scatter(3, 0, S)
+        got[2] = bent[2] = place("got2", [NP], F32, sums_at[3])
+        gather(2, 0, NP)
         exponentials(0)
         minus_relu(0)
         first_product(4)
         first_product(5)
         weigh(4, 0, S)
         got[3] = bent[3] = place("got3", [NP], F32, SLOT + 16)
-        stream(3)
-        stream(4)
+        gather(3, 0, NP)
         load_page(6)
         exponentials(1)
         minus_relu(1)
         logarithms(softs[0], 1.0)
+        nc.scalar.activation(out=ones[:, 2:3], in_=soft[1][:, 0:1], func=ACT.Exp, scale=0.0)
         for c in (0, 1):
             times(soft[c], soft[c], minus_by(c))
         first_product(6)
         first_product(7)
         weigh(5, 0, S)
-        stream(5)
+        scatter(4, 0, S)
+        scatter(5, 0, S)
+        got[4] = place("got4", [NP], F32, SLOT + 20)
+        gather(4, 0, NP)
+        gather(5, 0, NP)
         load_page(7)
-        exponentials(2)
-        minus_relu(2)
         zt = place("zt", [16, P, 2], BF16, 218)
         for c in (0, 1):
             for half in range(2):
                 sum_and_round(c, half, zt)
         weigh(6, 0, S)
         stream(6, (0, BANK, NP))
-        size[3] = size[4] = place("mid_size", [NP], F32, 16)
+        size[2] = size[3] = place("mid_size", [NP], F32, 16)
+        exponentials(2)
+        minus_relu(2)
         exponentials(3)
         minus_relu(3)
-        logarithms(softs[1], 1.0)
+        logarithms(softs[1], ones[:, 2:3])
         nc.scalar.activation(out=ones[:, 0:1], in_=soft[3][:, 0:1], func=ACT.Exp, scale=0.0)
         for i, kb in enumerate((141, 149)):
             both = place(f"scaled{i}", [2, NP], F32, kb)
             scaled[2 + 2 * i], scaled[3 + 2 * i] = both[:, 0, :], both[:, 1, :]
         scale_logs((2, 3))
-
-        exponentials(4)
-        bent[4] = place("bent4", [NP], F32, 28)
-        minus_relu(4)
         weigh(7, 0, S)
-        stream(7, range(0, NP + 1, CHUNK))
+        stream(7, PIECES)
+
         ident16 = place("ident16", [P], BF16, 157)
         nc.scalar.copy(out=ident16[:], in_=ident[:])
         for half in range(2):
@@ -399,16 +403,17 @@ def tile_list_vaccine_dispatch_kernel(
                 in_=back[:].rearrange("p b u m -> p b m u"),
             )
 
-        size[5] = place("late_size", [NP], F32, 218)
-        exponentials(5)
-        bent[5] = place("bent5", [NP], F32, 222)
-        minus_relu(5)
+        size[4] = size[5] = place("late_size", [NP], F32, 218.5)
+        bent[4], bent[5] = place("bent4", [NP], F32, 214.5), place("bent5", [NP], F32, 222.5)
+        for c in (4, 5):
+            exponentials(c)
+            minus_relu(c)
         logarithms(softs[2], ones[:, 0:1])
         nc.scalar.activation(out=ones[:, 1:2], in_=soft[5][:, 0:1], func=ACT.Exp, scale=0.0)
         scale_logs((4, 5))
 
         exps = place("exps", [2, NP], F32, 184)
-        size[6], soft[6] = place("size6", [NP], F32, 218), exps[:, 0, :]
+        size[6], soft[6] = place("size6", [NP], F32, 218.5), exps[:, 0, :]
         exponentials(6)
         rests = place("rests", [2, NP], F32, 176)
         for t, src in zip(halves_of(rests[:, 0, :]), halves_of(got[6])):
@@ -431,16 +436,12 @@ def tile_list_vaccine_dispatch_kernel(
                 nc.scalar.copy(out=planes_z[:, t, half_cols(half)], in_=back[:].rearrange("p b m -> p (b m)"))
 
         last = TILES - 1
+        chunks = [slice(lo, hi) for lo, hi in zip(CUTS, CUTS[1:])]
+        size[last] = place("size_last", [NP], F32, 226)
+        for cols in [slice(lo, hi) for lo, hi in zip(PIECES, PIECES[1:])]:
+            nc.scalar.activation(out=size[last][:, cols], in_=got[last][:, cols], func=ACT.Abs)
+            nc.scalar.activation(out=exps[:, 1, cols], in_=size[last][:, cols], func=ACT.Exp, scale=-1.0)
         logs = place("logs", [2, NP], F32, 226)
-        spread = logs[:, 1, :].rearrange("p (j k i) -> p k j i", j=CHUNKS, k=CHUNKS)
-        for k in range(CHUNKS):
-            cols = slice(k * CHUNK, (k + 1) * CHUNK)
-            nc.scalar.activation(
-                out=spread[:, k, :, :], in_=got[last][:, cols].rearrange("p (j i) -> p j i", j=CHUNKS), func=ACT.Abs
-            )
-            nc.scalar.activation(
-                out=exps[:, 1, cols].rearrange("p (j i) -> p j i", j=CHUNKS), in_=spread[:, k, :, :], func=ACT.Exp, scale=-1.0
-            )
         codes0 = place("codes0", [NP], U32, PAGE_AT[last])
         scales0 = place("scales0", [NP], U8, 225)
         codes1 = place("codes1", [NP], U32, 212)
@@ -456,21 +457,24 @@ def tile_list_vaccine_dispatch_kernel(
                 in_=woven0[:, cols, :].rearrange("p m u -> p (m u)").bitcast(BF16),
             )
             nc.vector.tensor_tensor(rests[:, 1, cols], rests[:, 1, cols], stocks[last][:, cols], ALU.subtract)
-        accs = [[bank(f"res{j}_{pair}", [2, CHUNK], 2 * j + pair) for pair in range(2)] for j in range(CHUNKS)]
-        for j in range(CHUNKS):
-            for pair in range(2):
-                second_pass(accs[j][pair], 0, pair, j, codes0, scales0)
-        for j in range(CHUNKS):
-            cols = slice(j * CHUNK, (j + 1) * CHUNK)
-            nc.scalar.activation(out=logs[:, :, cols], in_=exps[:, :, cols], func=ACT.Ln, bias=ones[:, 1:2])
-        for j in range(CHUNKS):
-            cols = slice(j * CHUNK, (j + 1) * CHUNK)
+        accs = []
+        for j, cols in enumerate(chunks):
+            width = cols.stop - cols.start
+            count = BANK // width
+            for first in range(0, N // P, count):
+                accs.append((j, first, bank(f"res{j}_{first}", [count, width], len(accs))))
+        for j, first, acc in accs:
+            second_pass(acc, first, 0, chunks[j], codes0, scales0)
+        for cols in chunks:
+            for e in range(2):
+                nc.scalar.activation(out=logs[:, e, cols], in_=exps[:, e, cols], func=ACT.Ln, bias=ones[:, 1:2])
+        for j, cols in enumerate(chunks):
             for e in range(2):
                 nc.vector.scalar_tensor_tensor(
                     out=planes_z[:, 2 + e, cols], in0=logs[:, e, cols], scalar=gain_dealt[:, 2 + e : 3 + e],
                     in1=rests[:, e, cols], op0=ALU.mult, op1=ALU.add,
                 )
-            nc.vector.tensor_copy(
+            (nc.scalar.copy if j in WEAVES_ON_SCALAR else nc.vector.tensor_copy)(
                 out=woven1[:, cols, :].rearrange("p (c i) t -> p c t i", i=4),
                 in_=planes_z[:, :, cols].rearrange("p t (c i) -> p c t i", i=4),
             )
@@ -478,12 +482,14 @@ def tile_list_vaccine_dispatch_kernel(
                 out=codes1[:, cols].bitcast(FP8X4), scales=scales1[:, cols],
                 in_=woven1[:, cols, :].rearrange("p m t -> p (m t)"),
             )
-            for pair in range(2):
-                second_pass(accs[j][pair], 1, pair, j, codes1, scales1)
-                staged = place(f"staged{j}_{pair}", [2, CHUNK], F32, WORDS + 2 * (2 * j + pair))
-                if j == CHUNKS - 1 and pair == 1:
-                    nc.vector.tensor_copy(out=staged[:], in_=accs[j][pair][:])
-                else:
-                    nc.scalar.copy(out=staged[:], in_=accs[j][pair][:])
-                rows = out[2 * pair * P : (2 * pair + 2) * P, cols]
-                nc.sync.dma_start(out=rows.rearrange("(i p) n -> p i n", p=P), in_=staged[:])
+            for index, (jj, first, acc) in enumerate(accs):
+                if jj == j:
+                    count = acc.shape[1]
+                    second_pass(acc, first, 1, cols, codes1, scales1)
+                    staged = place(f"staged{index}", acc.shape[1:], F32, WORDS + 2 * index)
+                    if index in COPIES_ON_VECTOR:
+                        nc.vector.tensor_copy(out=staged[:], in_=acc[:])
+                    else:
+                        nc.scalar.copy(out=staged[:], in_=acc[:])
+                    rows = out[first * P : (first + count) * P, cols]
+                    nc.sync.dma_start(out=rows.rearrange("(i p) n -> p i n", p=P), in_=staged[:])

@@ -28,6 +28,7 @@ PIECES = (0, 256, 512, 768, 1024)
 CUTS = (0, 256, 512, 768, 1024)
 COPIES_ON_VECTOR = (7,)
 WEAVES_ON_SCALAR = ()
+OPENING = 256
 HUGE = 3.0e38
 KB = 1024
 
@@ -62,7 +63,7 @@ def tile_list_vaccine_dispatch_kernel(
         minus_gain = held.tile([P, PLAIN], F32, name="minus_gain")
         gain_dealt = held.tile([P, 4], F32, name="gain_dealt")
         minus_dealt = held.tile([P, 2], F32, name="minus_dealt")
-        ones = held.tile([P, 3], F32, name="ones")
+        ones = held.tile([P, 4], F32, name="ones")
         w2c = held.tile([P, 2, 2 * N], U8, name="w2c", align_bytes=64)
         w2s = held.tile([P, 2, N], U8, name="w2s", align_bytes=64)
 
@@ -70,9 +71,9 @@ def tile_list_vaccine_dispatch_kernel(
         EDGE = 1 / 16
         PAGE_AT = (PAGE, PAGE + 8, PAGE + 16, 226, PAGE, PAGE + 8, PAGE + 16, PAGE + 8)
         words = [place(f"words{a}", [T], I32, WORDS + 16 * a) for a in range(2)]
-        planes = place("planes", [T], U8, PLANES)
-        picked = [place("picked0", [S], U32, 145)]
-        picked_scales = place("picked_scales", [S], U8, 149)
+        planes = place("planes", [T], U8, PLANES + 2)
+        picked = [place("picked0", [S], U32, PLANES + 6)]
+        picked_scales = place("picked_scales", [S], U8, 197)
         weights = place("weights", [S], F32, 160)
         gain_rows = place("gain_rows", [P], F32, 234)
         raw = {0: place("raw0", [2, 4, P], F32, RAW), 1: place("raw1", [2, 4, P], F32, RAW + 4)}
@@ -82,7 +83,7 @@ def tile_list_vaccine_dispatch_kernel(
             raw[2 + i] = raw23[:, :, :, i * P : (i + 1) * P]
 
         pages, stocks, quantised = {}, {}, {}
-        sums, put, got, soft, size, bent, scaled = {}, {}, {}, {}, {}, {}, {}
+        put, got, soft, size, bent, scaled = {}, {}, {}, {}, {}, {}
         STOCK_AT = (RAW, SLOT, RAW + 12, 172, RAW + 16, 168, SLOT + 4, 164)
 
         def load_w1(tile, first, width):
@@ -122,11 +123,11 @@ def tile_list_vaccine_dispatch_kernel(
             for i, c in enumerate(group):
                 quantised[c] = (codes[:, i * 2 * P : (i + 1) * 2 * P], scales[:, i * 2 * P : (i + 1) * 2 * P])
 
-        def first_product(c):
+        def first_product(c, pieces=((0, BANK, 0), (BANK, S, 1))):
             codes, scales = quantised[c]
-            for half in range(2):
-                cols = half_cols(half)
-                acc = bank(f"acc{c}_{half}", [BANK], 2 * (c % 2) + half)
+            for lo, hi, index in pieces:
+                cols = slice(lo, hi)
+                acc = bank(f"acc{c}_{lo}", [hi - lo], 2 * (c % 2) + index)
                 for a in range(2):
                     nc.tensor.matmul_mx(
                         out=acc[:],
@@ -137,7 +138,7 @@ def tile_list_vaccine_dispatch_kernel(
                         start=(a == 0),
                         stop=(a == 1),
                     )
-                nc.scalar.copy(out=sums[c][half], in_=acc[:])
+                nc.scalar.copy(out=whole[c][:, cols], in_=acc[:])
 
         def halves_of(tile):
             return [tile[:, half_cols(half)] for half in range(2)]
@@ -214,41 +215,42 @@ def tile_list_vaccine_dispatch_kernel(
                 )
 
         nc.vector.memset(planes[:].bitcast(I32), 0)
+        nc.gpsimd.memset(gain_rows[:], 0.0)
         nc.sync.dma_start(list1[:], offs)
         nc.sync.dma_start(list2[:], offs2)
+        nc.sync.dma_start(list3[:], offs3)
+        nc.sync.dma_start(out=gain_dealt[:], in_=gain[PASS:].rearrange("(p t) -> p t", t=4))
         nc.sync.dma_start(out=words[0][:], in_=tab_words[0].rearrange("p t i -> p (t i)").bitcast(I32))
         for q in range(2):
             nc.gpsimd.dma_start(
                 out=planes[32 * q : 32 * q + 8, :].bitcast(I32), in_=tab_scales[:, 4 * q : 4 * q + 4, :].bitcast(I32)
             )
+        load_w1(raw[0], 0, P)
+        nc.sync.dma_start(out=weights[:, :OPENING], in_=wgs[:, :OPENING])
+        nc.sync.dma_start(out=gain_rows[0:PLAIN, :], in_=gain[:PASS].rearrange("(c p) -> c p", p=P))
         for q in range(2, 4):
             for a in range(2):
-                nc.scalar.dma_start(
+                nc.sync.dma_start(
                     out=planes[32 * q + 4 * a : 32 * q + 4 * a + 4, :].bitcast(I32),
                     in_=tab_scales[a, 4 * q : 4 * q + 4, :].bitcast(I32),
                 )
-        load_w1(raw[0], 0, P)
         nc.sync.dma_start(out=words[1][:], in_=tab_words[1].rearrange("p t i -> p (t i)").bitcast(I32))
-        nc.sync.dma_start(out=weights[:, :BANK], in_=wgs[:, :BANK])
         load_page(0)
-        nc.sync.dma_start(out=weights[:, BANK:], in_=wgs[:, BANK:])
+        nc.sync.dma_start(out=weights[:, OPENING:], in_=wgs[:, OPENING:])
         load_w1(raw[1], P, P)
-        nc.sync.dma_start(list3[:], offs3)
-        nc.gpsimd.memset(gain_rows[:], 0.0)
-        nc.sync.dma_start(out=gain_rows[0:PLAIN, :], in_=gain[:PASS].rearrange("(c p) -> c p", p=P))
         load_w1(raw23, 2 * P, 2 * P)
         load_page(1)
         load_w1_dealt(0)
         load_w1_dealt(1)
-        nc.sync.dma_start(out=gain_dealt[:], in_=gain[PASS:].rearrange("(p t) -> p t", t=4))
         load_page(2)
 
         make_identity(nc, ident[:])
+        nc.scalar.activation(out=ones[:, 3:4], in_=ident[:, 0:1], func=ACT.Exp, scale=0.0)
         nc.gpsimd.memset(w2s[:].rearrange("p a n -> p (a n)").bitcast(I32), 0)
 
         nc.vector.tensor_copy(picked[0][:], words[0][:].bitcast(U32).indirect(list1[:]))
         nc.vector.tensor_copy(picked_scales[:], planes[:].indirect(list1[:]))
-        stage0 = place("stage0", [1024], BF16, STAGE)
+        stage0 = place("stage0", [1024], BF16, PLANES)
         round_w1(0, stage0, 0)
         quantise_w1((0,), stage0)
         picked.append(place("picked1", [S], U32, PLANES))
@@ -260,16 +262,14 @@ def tile_list_vaccine_dispatch_kernel(
 
         sums_at = {1: RAW + 8, 2: RAW + 24 + EDGE, 3: RAW + 28 + EDGE}
         whole = {c: place(f"sums{c}", [S], F32, sums_at.get(c, SLOT + 4 * c)) for c in range(TILES)}
-        for c in range(TILES):
-            sums[c] = halves_of(whole[c])
 
-        def weighted_scatter(c):
-            for half in range(2):
-                offsets = list2[:, half * 32 : (half + 1) * 32]
-                nc.vector.tensor_tensor(pages[c][:].indirect(offsets), sums[c][half], weights[:, half_cols(half)], ALU.mult)
+        def weighted_scatter(c, cut):
+            for lo, hi in ((0, cut), (cut, S)):
+                offsets = list2[:, lo // 16 : hi // 16]
+                nc.vector.tensor_tensor(pages[c][:].indirect(offsets), whole[c][:, lo:hi], weights[:, lo:hi], ALU.mult)
 
-        first_product(0)
-        weighted_scatter(0)
+        first_product(0, ((0, OPENING, 0), (OPENING, BANK, 2), (BANK, S, 1)))
+        weighted_scatter(0, OPENING)
         stage1 = place("stage1", [1024], BF16, STAGE + 2)
         round_w1(1, stage1, 0)
         quantise_w1((1,), stage1)
@@ -283,7 +283,7 @@ def tile_list_vaccine_dispatch_kernel(
         round_w1(3, stage23, 1)
         quantise_w1((2, 3), stage23)
         first_product(1)
-        weighted_scatter(1)
+        weighted_scatter(1, BANK)
         stage_dealt = place("stage_dealt", [4096], BF16, LATE - EDGE)
         for a in range(2):
             round_w1_dealt(a, stage_dealt)
@@ -353,7 +353,7 @@ def tile_list_vaccine_dispatch_kernel(
         load_page(6)
         exponentials(1)
         minus_relu(1)
-        logarithms(softs[0], 1.0)
+        logarithms(softs[0], ones[:, 3:4])
         nc.scalar.activation(out=ones[:, 2:3], in_=soft[1][:, 0:1], func=ACT.Exp, scale=0.0)
         for c in (0, 1):
             times(soft[c], soft[c], minus_by(c))

@@ -22,14 +22,11 @@ BANK = 512
 PASS = 512
 TILES = H // P
 PLAIN = 4
-CHUNK = 256
-CHUNKS = NP // CHUNK
-PIECES = (0, 256, 512, 768, 1024)
-CUTS = (0, 256, 512, 768, 1024)
-COPIES_ON_VECTOR = (7,)
-WEAVES_ON_SCALAR = ()
+LAST = TILES - 1
+KNEE = 24.0
 OPENING = 256
-HUGE = 3.0e38
+TAIL_CUTS = (0, 128, 256, 512, 768, 1024)
+LAST_PIECES = (0, 256, 512, 768, 896, 1024)
 KB = 1024
 
 
@@ -60,40 +57,40 @@ def tile_list_vaccine_dispatch_kernel(
         list2 = held.tile([P, S // 16], U16, name="list2")
         list3 = held.tile([P, NP // 16], U16, name="list3")
         ident = held.tile([P, P], F32, name="ident")
-        minus_gain = held.tile([P, PLAIN], F32, name="minus_gain")
-        gain_dealt = held.tile([P, 4], F32, name="gain_dealt")
-        minus_dealt = held.tile([P, 2], F32, name="minus_dealt")
-        ones = held.tile([P, 4], F32, name="ones")
+        gains = held.tile([P, 2, 8], F32, name="gains")
+        minus = held.tile([P, 2, 4], F32, name="minus")
+        inverse = held.tile([P, 2, 4], F32, name="inverse")
+        lift = held.tile([P, 2, 4], F32, name="lift")
+        drop = held.tile([P, 2, 4], F32, name="drop")
+        knee = held.tile([P, 1], F32, name="knee")
+        first_one = held.tile([P, 1], F32, name="first_one")
         w2c = held.tile([P, 2, 2 * N], U8, name="w2c", align_bytes=64)
         w2s = held.tile([P, 2, N], U8, name="w2s", align_bytes=64)
 
-        WORDS, RAW, SLOT, PAGE, LATE, STAGE, PLANES = 0, 32, 65, 97, 125, 133, 141
-        EDGE = 1 / 16
-        PAGE_AT = (PAGE, PAGE + 8, PAGE + 16, 226, PAGE, PAGE + 8, PAGE + 16, PAGE + 8)
-        words = [place(f"words{a}", [T], I32, WORDS + 16 * a) for a in range(2)]
-        planes = place("planes", [T], U8, PLANES + 2)
-        picked = [place("picked0", [S], U32, PLANES + 6)]
-        picked_scales = place("picked_scales", [S], U8, 197)
-        weights = place("weights", [S], F32, 160)
-        gain_rows = place("gain_rows", [P], F32, 234)
-        raw = {0: place("raw0", [2, 4, P], F32, RAW), 1: place("raw1", [2, 4, P], F32, RAW + 4)}
-        raw23 = place("raw23", [2, 4, 2 * P], F32, RAW + 8)
-        raw_dealt = [place(f"raw_dealt{a}", [4, PASS], F32, RAW + 16 + 8 * a) for a in range(2)]
-        for i in range(2):
-            raw[2 + i] = raw23[:, :, :, i * P : (i + 1) * P]
+        def column(tile, c):
+            return tile[:, c // PLAIN, c % PLAIN : c % PLAIN + 1]
 
-        pages, stocks, quantised = {}, {}, {}
-        put, got, soft, size, bent, scaled = {}, {}, {}, {}, {}, {}
-        STOCK_AT = (RAW, SLOT, RAW + 12, 172, RAW + 16, 168, SLOT + 4, 164)
+        words = [place(f"words{a}", [T], I32, 16 * a) for a in range(2)]
+        planes = place("planes", [T], U8, 34)
+        stage0 = place("stage0", [1024], BF16, 32)
+        picked = [place("picked0", [S], U32, 38), place("picked1", [S], U32, 32)]
+        picked_scales = place("picked_scales", [S], U8, 42)
+        weights = place("weights", [S], F32, 43)
+        gain_rows = place("gain_rows", [P], F32, 234)
+        PAGE_AT = (58, 66, 74, 82, 58, 66, 74, 226)
+        raw = {0: place("raw0", [2, 4, P], F32, 90), 1: place("raw1", [2, 4, P], F32, 94)}
+        raw23 = [place(f"raw23_{a}", [4, 2 * P], F32, 98 + 4 * a) for a in range(2)]
+        raw_dealt = [place(f"raw_dealt{a}", [4, PASS], F32, 106 + 8 * a) for a in range(2)]
+
+        pages, stocks, quantised, sums, put, got, bent, soft, logs = {}, {}, {}, {}, {}, {}, {}, {}, {}
+        STOCK_AT = (16, 20, 24, 28, 106, 128, 90, 102)
+        EDGE = 1 / 16
+        CODES_AT = {0: (47, 55), 1: (122, 55.25), 2: (128, 55.5), 4: (51, 132)}
 
         def load_w1(tile, first, width):
             for a in range(2):
                 rows = w1[a * PASS : (a + 1) * PASS, first : first + width]
                 nc.sync.dma_start(out=tile[:, a, :, :], in_=rows.rearrange("(p j) c -> p j c", j=4))
-
-        def load_w1_dealt(a):
-            rows = w1[a * PASS : (a + 1) * PASS, PASS:]
-            nc.sync.dma_start(out=raw_dealt[a][:], in_=rows.rearrange("(p j) c -> p j c", j=4))
 
         def load_page(c):
             pages[c] = place(f"page{c}", [T2], F32, PAGE_AT[c])
@@ -109,96 +106,150 @@ def tile_list_vaccine_dispatch_kernel(
                 in_=raw[c][:].rearrange("p a t (c i) -> p a c t i", i=4),
             )
 
+        def round_w1_pair(a, stage):
+            nc.scalar.copy(
+                out=stage[:].rearrange("p (w a c i t) -> p a w c t i", w=2, a=2, i=4, t=4)[:, a, :, :, :, :],
+                in_=raw23[a][:].rearrange("p t (w c i) -> p w c t i", w=2, i=4),
+            )
+
         def round_w1_dealt(a, stage):
             nc.scalar.copy(
                 out=stage[:].rearrange("p (t a m j) -> p a m t j", t=4, a=2, j=4)[:, a, :, :, :],
                 in_=raw_dealt[a][:].rearrange("p j (m t) -> p m t j", t=4),
             )
 
-        def quantise_w1(group, stage):
-            first, count = group[0], len(group)
-            codes = place(f"w1c{first}", [count * 2 * P], U32, 150 + first if first else STAGE + 2)
-            scales = place(f"w1s{first}", [count * 2 * P], U8, {0: STAGE + 4, 1: LATE + 1}.get(first, 158 + first / 4))
+        def quantise_w1(first, count, stage):
+            codes = place(f"w1c{first}", [count * 2 * P], U32, CODES_AT[first][0])
+            scales = place(f"w1s{first}", [count * 2 * P], U8, CODES_AT[first][1])
             nc.vector.quantize_mx(out=codes[:].bitcast(FP8X4), scales=scales[:], in_=stage[:])
-            for i, c in enumerate(group):
-                quantised[c] = (codes[:, i * 2 * P : (i + 1) * 2 * P], scales[:, i * 2 * P : (i + 1) * 2 * P])
+            for i in range(count):
+                part = slice(i * 2 * P, (i + 1) * 2 * P)
+                quantised[first + i] = (codes[:, part], scales[:, part])
 
-        def first_product(c, pieces=((0, BANK, 0), (BANK, S, 1))):
+        def product(c, lo, hi, index, dst):
             codes, scales = quantised[c]
-            for lo, hi, index in pieces:
-                cols = slice(lo, hi)
-                acc = bank(f"acc{c}_{lo}", [hi - lo], 2 * (c % 2) + index)
-                for a in range(2):
-                    nc.tensor.matmul_mx(
-                        out=acc[:],
-                        lhsT=codes[:, a * P : (a + 1) * P].bitcast(FP8X4),
-                        lhsT_scale=scales[:, a * P : (a + 1) * P],
-                        rhs=picked[a][:, cols].bitcast(FP8X4),
-                        rhs_scale=picked_scales[4 * a : P, cols],
-                        start=(a == 0),
-                        stop=(a == 1),
-                    )
-                nc.scalar.copy(out=whole[c][:, cols], in_=acc[:])
+            acc = bank(f"acc{c}_{lo}", [hi - lo], index)
+            for a in range(2):
+                nc.tensor.matmul_mx(
+                    out=acc[:],
+                    lhsT=codes[:, a * P : (a + 1) * P].bitcast(FP8X4),
+                    lhsT_scale=scales[:, a * P : (a + 1) * P],
+                    rhs=picked[a][:, lo:hi].bitcast(FP8X4),
+                    rhs_scale=picked_scales[4 * a : P, lo:hi],
+                    start=(a == 0),
+                    stop=(a == 1),
+                )
+            nc.scalar.copy(out=dst, in_=acc[:])
 
-        def halves_of(tile):
+        def whole_product(c, kb):
+            sums[c] = place(f"sums{c}", [S], F32, kb)
+            for half in range(2):
+                product(c, half * BANK, (half + 1) * BANK, 2 * ((c + 1) % 2) + half, sums[c][:, half_cols(half)])
+
+        def weighted_scatter(c, lo, hi, src):
+            nc.vector.tensor_tensor(pages[c][:].indirect(list2[:, lo // 16 : hi // 16]), src, weights[:, lo:hi], ALU.mult)
+
+        def scatter(c, src, lo=0, hi=S):
+            nc.vector.tensor_copy(pages[c][:].indirect(list2[:, lo // 16 : hi // 16]), src)
+
+        def fetch(c, dst, lo, hi):
+            nc.vector.tensor_copy(dst, pages[c][:].indirect(list3[:, lo // 16 : hi // 16]))
+
+        def gather(c, kb, cuts=(0, NP)):
+            got[c] = place(f"got{c}", [NP], F32, kb)
+            for lo, hi in zip(cuts, cuts[1:]):
+                fetch(c, got[c][:, lo:hi], lo, hi)
+
+        def weigh(c, dst, src, lo=0, hi=S):
+            by = weights[:, lo:hi] if c < PLAIN else dealt[:, (c - PLAIN) * S + lo : (c - PLAIN) * S + hi]
+            nc.gpsimd.tensor_tensor(dst, src, by, ALU.mult)
+
+        def weigh_whole(c, kb=None):
+            put[c] = sums[c] if kb is None else place(f"put{c}", [S], F32, kb)
+            weigh(c, put[c][:], sums[c][:])
+
+        def bend(c, dst, src):
+            nc.scalar.activation(out=dst, in_=src, func=ACT.Relu, scale=column(gains, c), bias=column(lift, c))
+
+        def exponential(c, dst, src):
+            nc.scalar.activation(out=dst, in_=src, func=ACT.Exp, scale=column(inverse, c), bias=knee[:])
+
+        def logarithm(dst, src, one):
+            nc.scalar.activation(out=dst, in_=src, func=ACT.Ln, bias=one)
+
+        def halves(tile):
             return [tile[:, half_cols(half)] for half in range(2)]
 
-        def scatter(c, lo, hi):
-            nc.vector.tensor_copy(pages[c][:].indirect(list2[:, lo // 16 : hi // 16]), put[c][:, lo:hi])
+        def exponentials(c, bent_kb, soft_kb, side_kb=None):
+            bent[c] = place(f"bent{c}", [NP], F32, bent_kb)
+            logs[c] = place(f"soft{c}", [NP], F32, soft_kb)
+            soft[c] = halves(logs[c])
+            if side_kb is not None:
+                side = place(f"side{c}", [BANK], F32, side_kb)
+                soft[c][0] = side[:]
+            for dst, src in zip(halves(bent[c]), halves(got[c])):
+                bend(c, dst, src)
+            for dst, src in zip(soft[c], halves(bent[c])):
+                exponential(c, dst, src)
 
-        def gather(c, lo, hi):
-            nc.vector.tensor_copy(got[c][:, lo:hi], pages[c][:].indirect(list3[:, lo // 16 : hi // 16]))
+        def next_one(one):
+            nc.scalar.activation(out=one, in_=knee[:], func=ACT.Exp, scale=0.0)
+            return one
 
-        def times(dst, src, by):
-            nc.gpsimd.tensor_scalar(out=dst, in0=src, scalar1=by, scalar2=0.0, op0=ALU.mult, op1=ALU.add)
+        def logarithms(pair, one, kb):
+            logs[pair[0]] = place(f"log{pair[0]}", [NP], F32, kb)
+            for c in pair:
+                for dst, src in zip(halves(logs[c]), soft[c]):
+                    logarithm(dst, src, one)
+            return next_one(soft[pair[1]][0][:, 0:1])
 
-        def exponentials(c):
-            for half in range(2):
-                nc.scalar.activation(out=size[c][:, half_cols(half)], in_=got[c][:, half_cols(half)], func=ACT.Abs)
-            for half in range(2):
-                nc.scalar.activation(
-                    out=soft[c][:, half_cols(half)], in_=size[c][:, half_cols(half)], func=ACT.Exp, scale=-1.0
+        def scale_log(c, cols):
+            t = logs[c][:, cols]
+            nc.gpsimd.tensor_scalar(out=t, in0=t, scalar1=column(gains, c), scalar2=column(drop, c), op0=ALU.mult, op1=ALU.add)
+
+        def negate_stock(c, kb):
+            src = stocks[c]
+            stocks[c] = place(f"less{c}", [NP], F32, kb)
+            nc.gpsimd.tensor_scalar(out=stocks[c][:], in0=src[:], scalar1=-1.0, scalar2=0.0, op0=ALU.mult, op1=ALU.add)
+
+        turned = {}
+
+        def add_turned(c, half, src, first, final):
+            if first:
+                turned[c, half] = bank(f"turned{c}_{half}", [4, P], 4 + 2 * (c % 2) + half)
+            for b in range(4):
+                lo = half * BANK + b * P
+                nc.tensor.matmul(
+                    turned[c, half][:, b, :], src[:, lo : lo + P], ident[:], is_transpose=True,
+                    start=(first and b == 0), stop=(final and b == 3),
                 )
 
-        def logarithms(pair, one):
+        def open_sums(c):
             for half in range(2):
-                t = pair[:, :, half_cols(half)]
-                nc.scalar.activation(out=t, in_=t, func=ACT.Ln, bias=one)
+                add_turned(c, half, bent[c], True, False)
+                add_turned(c, half, stocks[c], False, False)
 
-        def minus_by(c):
-            return minus_gain[:, c : c + 1] if c < PLAIN else minus_dealt[:, c - PLAIN : c - PLAIN + 1]
+        def close_and_round(c, half):
+            add_turned(c, half, logs[c], False, True)
+            nc.scalar.copy(
+                out=zt[:, 8 * half : 8 * half + 8, c * 32 : c * 32 + 32, :].rearrange("m (b u) p e -> m b u p e", u=2),
+                in_=turned[c, half][:].rearrange("m b (p u e) -> m b u p e", u=2, e=2),
+            )
 
-        def minus_relu(c):
-            for t, src in zip(halves_of(bent[c]), halves_of(got[c])):
-                times(t, src, minus_by(c))
-            for t in halves_of(bent[c]):
-                nc.gpsimd.tensor_scalar(out=t, in0=t, scalar1=0.0, scalar2=-HUGE, op0=ALU.min, op1=ALU.max)
+        def less_stock(c, kb=None):
+            src = stocks[c]
+            if kb is not None:
+                stocks[c] = place(f"rest{c}", [NP], F32, kb)
+            for dst, more, less in zip(halves(stocks[c]), halves(bent[c]), halves(src)):
+                nc.gpsimd.tensor_tensor(dst, more, less, ALU.subtract)
 
-        def scale_logs(pair):
-            for half in range(2):
-                for c in pair:
-                    times(scaled[c][:, half_cols(half)], soft[c][:, half_cols(half)], minus_by(c))
+        def pair_slot(c, cols):
+            half = cols.start // BANK
+            t = c - PLAIN
+            return pairs[half][:, t // 2, cols.start - half * BANK : cols.stop - half * BANK, t % 2]
 
-        def pairs(t, u):
-            return t.rearrange("m b (p u e) -> m b u p e", u=2, e=2)[:, :, u, :, :]
-
-        def summed(c, half):
-            cols = half_cols(half)
-            turned = bank(f"turned{c}_{half}", [4, P], 4 + 2 * (c % 2) + half)
-            terms = [bent[c][:, cols], stocks[c][:, cols], scaled[c][:, cols]]
-            for term, src in enumerate(terms):
-                for b in range(4):
-                    nc.tensor.matmul(
-                        turned[:, b, :], src[:, b * P : (b + 1) * P], ident[:], is_transpose=True,
-                        start=(term == 0 and b == 0), stop=(term == 2 and b == 3),
-                    )
-            return turned
-
-        def sum_and_round(c, half, zt):
-            turned = summed(c, half)
-            for u in range(2):
-                dst = zt[:, 8 * half + u : 8 * half + 8 : 2, c * 32 : c * 32 + 32, :]
-                nc.scalar.activation(out=dst, in_=pairs(turned[:], u), func=ACT.Copy, scale=-1.0)
+        def join(c, cols):
+            nc.gpsimd.tensor_tensor(pair_slot(c, cols), logs[c][:, cols], stocks[c][:, cols], ALU.add)
 
         def second_pass(acc, first, a, cols, codes, scales):
             count = acc.shape[1]
@@ -218,8 +269,7 @@ def tile_list_vaccine_dispatch_kernel(
         nc.gpsimd.memset(gain_rows[:], 0.0)
         nc.sync.dma_start(list1[:], offs)
         nc.sync.dma_start(list2[:], offs2)
-        nc.sync.dma_start(list3[:], offs3)
-        nc.sync.dma_start(out=gain_dealt[:], in_=gain[PASS:].rearrange("(p t) -> p t", t=4))
+        nc.sync.dma_start(out=gains[:, 1, 0:4], in_=gain[PASS:].rearrange("(p t) -> p t", t=4))
         nc.sync.dma_start(out=words[0][:], in_=tab_words[0].rearrange("p t i -> p (t i)").bitcast(I32))
         for q in range(2):
             nc.gpsimd.dma_start(
@@ -236,69 +286,86 @@ def tile_list_vaccine_dispatch_kernel(
                 )
         nc.sync.dma_start(out=words[1][:], in_=tab_words[1].rearrange("p t i -> p (t i)").bitcast(I32))
         load_page(0)
-        nc.sync.dma_start(out=weights[:, OPENING:], in_=wgs[:, OPENING:])
+        nc.sync.dma_start(out=weights[:, OPENING:BANK], in_=wgs[:, OPENING:BANK])
         load_w1(raw[1], P, P)
-        load_w1(raw23, 2 * P, 2 * P)
+        nc.sync.dma_start(out=weights[:, BANK:], in_=wgs[:, BANK:])
         load_page(1)
-        load_w1_dealt(0)
-        load_w1_dealt(1)
+        nc.sync.dma_start(list3[:], offs3)
+        for a in range(2):
+            rows = w1[a * PASS : (a + 1) * PASS, 2 * P : 4 * P]
+            nc.sync.dma_start(out=raw23[a][:], in_=rows.rearrange("(p j) c -> p j c", j=4))
+        for a in range(2):
+            rows = w1[a * PASS : (a + 1) * PASS, PASS:]
+            nc.sync.dma_start(out=raw_dealt[a][:], in_=rows.rearrange("(p j) c -> p j c", j=4))
         load_page(2)
+        load_page(3)
+        load_stock(0)
+        load_stock(1)
 
         make_identity(nc, ident[:])
-        nc.scalar.activation(out=ones[:, 3:4], in_=ident[:, 0:1], func=ACT.Exp, scale=0.0)
+        nc.gpsimd.memset(knee[:], KNEE)
         nc.gpsimd.memset(w2s[:].rearrange("p a n -> p (a n)").bitcast(I32), 0)
+        one = next_one(first_one[:])
 
+        gain_t = bank("gain_t", [P], 7)
+        nc.tensor.transpose(gain_t[:], gain_rows[:], ident[:])
+        nc.scalar.copy(out=gains[:, 0, 0:4], in_=gain_t[:, 0:PLAIN])
+        both = gains[:, :, 0:4]
+        nc.vector.tensor_scalar(out=minus[:], in0=both, scalar1=-1.0, scalar2=0.0, op0=ALU.mult, op1=ALU.add)
+        nc.vector.tensor_scalar(out=lift[:], in0=both, scalar1=KNEE, scalar2=0.0, op0=ALU.mult, op1=ALU.add)
+        nc.vector.tensor_scalar(out=drop[:], in0=both, scalar1=-KNEE, scalar2=0.0, op0=ALU.mult, op1=ALU.add)
+        nc.vector.reciprocal(out=inverse[:], in_=minus[:])
         nc.vector.tensor_copy(picked[0][:], words[0][:].bitcast(U32).indirect(list1[:]))
         nc.vector.tensor_copy(picked_scales[:], planes[:].indirect(list1[:]))
-        stage0 = place("stage0", [1024], BF16, PLANES)
         round_w1(0, stage0, 0)
-        quantise_w1((0,), stage0)
-        picked.append(place("picked1", [S], U32, PLANES))
-        for half in range(2):
-            nc.vector.tensor_copy(
-                picked[1][:, half_cols(half)],
-                words[1][:].bitcast(U32).indirect(list1[:, half * 32 : (half + 1) * 32]),
-            )
+        quantise_w1(0, 1, stage0)
+        for lo, hi in ((0, OPENING), (OPENING, BANK), (BANK, S)):
+            nc.vector.tensor_copy(picked[1][:, lo:hi], words[1][:].bitcast(U32).indirect(list1[:, lo // 16 : hi // 16]))
 
-        sums_at = {1: RAW + 8, 2: RAW + 24 + EDGE, 3: RAW + 28 + EDGE}
-        whole = {c: place(f"sums{c}", [S], F32, sums_at.get(c, SLOT + 4 * c)) for c in range(TILES)}
-
-        def weighted_scatter(c, cut):
-            for lo, hi in ((0, cut), (cut, S)):
-                offsets = list2[:, lo // 16 : hi // 16]
-                nc.vector.tensor_tensor(pages[c][:].indirect(offsets), whole[c][:, lo:hi], weights[:, lo:hi], ALU.mult)
-
-        first_product(0, ((0, OPENING, 0), (OPENING, BANK, 2), (BANK, S, 1)))
-        weighted_scatter(0, OPENING)
-        stage1 = place("stage1", [1024], BF16, STAGE + 2)
+        early0 = place("early0", [BANK], F32, 144)
+        late0 = place("late0", [BANK], F32, 94)
+        for index, (lo, hi) in enumerate(((0, OPENING), (OPENING, BANK))):
+            product(0, lo, hi, index, early0[:, lo:hi])
+            weighted_scatter(0, lo, hi, early0[:, lo:hi])
+        stage1 = place("stage1", [1024], BF16, 126)
         round_w1(1, stage1, 0)
-        quantise_w1((1,), stage1)
-        gain_t = bank("gain_t", [P], 0)
-        nc.tensor.transpose(gain_t[:], gain_rows[:], ident[:])
-        nc.scalar.activation(out=minus_gain[:], in_=gain_t[:, 0:PLAIN], func=ACT.Copy, scale=-1.0)
-        got[0] = place("got0", [NP], F32, RAW + 4)
-        gather(0, 0, NP)
-        stage23 = place("stage23", [2048], BF16, STAGE + 4)
-        round_w1(2, stage23, 0)
-        round_w1(3, stage23, 1)
-        quantise_w1((2, 3), stage23)
-        first_product(1)
-        weighted_scatter(1, BANK)
-        stage_dealt = place("stage_dealt", [4096], BF16, LATE - EDGE)
+        quantise_w1(1, 1, stage1)
+        product(0, BANK, S, 2, late0[:])
+        weighted_scatter(0, BANK, S, late0[:])
+        early1 = place("early1", [BANK], F32, 146)
+        late1 = place("late1", [BANK], F32, 102)
+        product(1, 0, BANK, 0, early1[:])
+        weighted_scatter(1, 0, BANK, early1[:])
+        stage23 = place("stage23", [2048], BF16, 122)
+        round_w1_pair(0, stage23)
+        gather(0, 98)
+        round_w1_pair(1, stage23)
+        quantise_w1(2, 2, stage23)
+        product(1, BANK, S, 1, late1[:])
+        weighted_scatter(1, BANK, S, late1[:])
+        stage_dealt = place("stage_dealt", [4096], BF16, 136)
         for a in range(2):
             round_w1_dealt(a, stage_dealt)
-        quantise_w1((4, 5, 6, 7), stage_dealt)
-        got[1] = place("got1", [NP], F32, RAW + 20 + EDGE)
-        gather(1, 0, NP)
-        times(minus_dealt[:], gain_dealt[:, 0:2], -1.0)
+        quantise_w1(4, 4, stage_dealt)
+        early2 = place("early2", [BANK], F32, 114 + EDGE)
+        late2 = place("late2", [BANK], F32, 120 + EDGE)
+        product(2, 0, BANK, 2, early2[:])
+        product(2, BANK, S, 3, late2[:])
+        whole_product(3, 116 + EDGE)
+        weighted_scatter(2, 0, BANK, early2[:])
+        gather(1, 136)
+        put[2] = place("put2", [BANK], F32, 114 + EDGE)
+        weigh(2, put[2][:], late2[:], BANK, S)
+        scatter(2, put[2][:], BANK, S)
+        weigh_whole(3, 120 + EDGE)
+        scatter(3, put[3][:])
 
-        load_page(3)
-        dealt = place("dealt", [4 * S], F32, WORDS)
+        dealt = place("dealt", [4 * S], F32, 0)
         for q in (0, 2, 1, 3):
             nc.sync.dma_start(out=dealt[32 * q : 32 * q + 32, :], in_=wgs.rearrange("(q t) j -> q (t j)", t=4))
         load_page(4)
         load_page(5)
-        for c in range(TILES):
+        for c in range(2, TILES):
             load_stock(c)
         for a in range(2):
             nc.sync.dma_start(out=w2c[:, a, :].bitcast(I32), in_=w2_words[a].bitcast(I32))
@@ -308,155 +375,117 @@ def tile_list_vaccine_dispatch_kernel(
                 in_=w2_scales[:, 4 * q : 4 * q + 4, :].rearrange("a r n -> r a n").bitcast(I32),
             )
 
-        for c in (2, 3):
-            put[c] = place(f"put{c}", [S], F32, LATE - 4 + 8 * (c - 2))
-        put[4] = place("put4", [S], F32, SLOT + 12)
-        put[5] = got[5] = place("put5", [S], F32, 192)
-        for c in range(PLAIN + 2, TILES):
-            put[c] = whole[c]
-            got[c] = whole[c]
-        softs = [place(f"softs{i}", [2, NP], F32, kb) for i, kb in enumerate((16, 24, 176))]
-        for c in range(6):
-            soft[c] = softs[c // 2][:, c % 2, :]
-        early_size = place("early_size", [NP], F32, LATE)
-        for c in range(2):
-            size[c] = early_size
-
-        def weigh(c, lo, hi):
-            by = weights[:, lo:hi] if c < PLAIN else dealt[:, (c - PLAIN) * S + lo : (c - PLAIN) * S + hi]
-            nc.gpsimd.tensor_tensor(put[c][:, lo:hi], whole[c][:, lo:hi], by, ALU.mult)
-
-        def stream(c, cuts=(0, NP)):
-            scatter(c, 0, S)
-            for lo, hi in zip(cuts, cuts[1:]):
-                gather(c, lo, hi)
-
-        bent[0], bent[1] = got[0], got[1]
-        scaled[0], scaled[1] = soft[0], soft[1]
-
-        first_product(2)
-        first_product(3)
-        for half in range(2):
-            weigh(2, half * BANK, (half + 1) * BANK)
-            scatter(2, half * BANK, (half + 1) * BANK)
-        weigh(3, 0, S)
-        scatter(3, 0, S)
-        got[2] = bent[2] = place("got2", [NP], F32, sums_at[3])
-        gather(2, 0, NP)
-        exponentials(0)
-        minus_relu(0)
-        first_product(4)
-        first_product(5)
-        weigh(4, 0, S)
-        got[3] = bent[3] = place("got3", [NP], F32, SLOT + 16)
-        gather(3, 0, NP)
+        zt = place("zt", [16, P, 2], BF16, 226)
+        exponentials(0, 110 + EDGE, 176)
+        whole_product(4, 98)
+        whole_product(5, 168)
+        whole_product(6, 156)
+        whole_product(7, 160)
+        exponentials(1, 51, 180, 174)
+        negate_stock(0, 132)
+        negate_stock(1, 16)
+        open_sums(0)
+        open_sums(1)
+        weigh_whole(4, 20)
+        one = logarithms((0, 1), one, 136)
+        gather(2, 43)
+        gather(3, 98)
         load_page(6)
-        exponentials(1)
-        minus_relu(1)
-        logarithms(softs[0], ones[:, 3:4])
-        nc.scalar.activation(out=ones[:, 2:3], in_=soft[1][:, 0:1], func=ACT.Exp, scale=0.0)
-        for c in (0, 1):
-            times(soft[c], soft[c], minus_by(c))
-        first_product(6)
-        first_product(7)
-        weigh(5, 0, S)
-        scatter(4, 0, S)
-        scatter(5, 0, S)
-        got[4] = place("got4", [NP], F32, SLOT + 20)
-        gather(4, 0, NP)
-        gather(5, 0, NP)
-        load_page(7)
-        zt = place("zt", [16, P, 2], BF16, 218)
         for c in (0, 1):
             for half in range(2):
-                sum_and_round(c, half, zt)
-        weigh(6, 0, S)
-        stream(6, (0, BANK, NP))
-        size[2] = size[3] = place("mid_size", [NP], F32, 16)
-        exponentials(2)
-        minus_relu(2)
-        exponentials(3)
-        minus_relu(3)
-        logarithms(softs[1], ones[:, 2:3])
-        nc.scalar.activation(out=ones[:, 0:1], in_=soft[3][:, 0:1], func=ACT.Exp, scale=0.0)
-        for i, kb in enumerate((141, 149)):
-            both = place(f"scaled{i}", [2, NP], F32, kb)
-            scaled[2 + 2 * i], scaled[3 + 2 * i] = both[:, 0, :], both[:, 1, :]
-        scale_logs((2, 3))
-        weigh(7, 0, S)
-        stream(7, PIECES)
-
-        ident16 = place("ident16", [P], BF16, 157)
-        nc.scalar.copy(out=ident16[:], in_=ident[:])
+                scale_log(c, half_cols(half))
+                close_and_round(c, half)
+        scatter(4, put[4][:])
+        weigh_whole(5, 176)
+        scatter(5, put[5][:])
+        exponentials(2, 180, 184)
+        negate_stock(2, 170)
+        exponentials(3, 43, 192, 140)
+        negate_stock(3, 24)
+        open_sums(2)
+        open_sums(3)
+        weigh_whole(6, 28)
+        weigh_whole(7, 156)
+        one = logarithms((2, 3), one, 98)
+        gather(4, 166)
+        gather(5, 196)
+        scatter(6, put[6][:])
         for half in range(2):
             for c in (2, 3):
-                sum_and_round(c, half, zt)
-        woven0 = place("woven0", [NP, 2], F32, STAGE)
-        for j in range(CHUNKS):
+                scale_log(c, half_cols(half))
+                close_and_round(c, half)
+        shifted = place("shifted", [NP], F32, 184)
+        nc.gpsimd.tensor_scalar(out=shifted[:], in0=stocks[LAST][:], scalar1=column(lift, LAST), scalar2=1.0, op0=ALU.add, op1=ALU.mult)
+        woven0 = place("woven0", [NP, 2], F32, 144)
+        for j in range(4):
             back = bank(f"back{j}", [2, 2, P], j)
             for b in range(2):
                 for u in range(2):
                     src = zt[:, (2 * j + b) * 2 + u, :, :].rearrange("m p e -> m (p e)").bitcast(F32)
                     nc.tensor.transpose(back[:, b, u, :], src, ident[:])
             nc.scalar.copy(
-                out=woven0[:, j * CHUNK : (j + 1) * CHUNK, :].rearrange("p (b m) u -> p b m u", b=2),
+                out=woven0[:, j * 256 : (j + 1) * 256, :].rearrange("p (b m) u -> p b m u", b=2),
                 in_=back[:].rearrange("p b u m -> p b m u"),
             )
+        gather(6, 208, (0, BANK, NP))
+        exponentials(4, 226, 200)
+        less_stock(4)
+        load_page(LAST)
+        scatter(LAST, put[LAST][:])
+        pieces = [slice(lo, hi) for lo, hi in zip(LAST_PIECES, LAST_PIECES[1:])]
+        fetched = [place(f"fetched{half}", [BANK], F32, 220 + 4 * half) for half in range(2)]
 
-        size[4] = size[5] = place("late_size", [NP], F32, 218.5)
-        bent[4], bent[5] = place("bent4", [NP], F32, 214.5), place("bent5", [NP], F32, 222.5)
+        def fetched_piece(cols):
+            half = cols.start // BANK
+            return fetched[half][:, cols.start - half * BANK : cols.stop - half * BANK]
+
+        for piece in pieces:
+            fetch(LAST, fetched_piece(piece), piece.start, piece.stop)
+
+        pairs = [place(f"pairs{half}", [2, BANK, 2], BF16, kb) for half, kb in enumerate((51, 110))]
+        exponentials(5, 166, 204, 142)
+        less_stock(5)
+        one = logarithms((4, 5), one, 196)
         for c in (4, 5):
-            exponentials(c)
-            minus_relu(c)
-        logarithms(softs[2], ones[:, 0:1])
-        nc.scalar.activation(out=ones[:, 1:2], in_=soft[5][:, 0:1], func=ACT.Exp, scale=0.0)
-        scale_logs((4, 5))
-
-        exps = place("exps", [2, NP], F32, 184)
-        size[6], soft[6] = place("size6", [NP], F32, 218.5), exps[:, 0, :]
-        exponentials(6)
-        rests = place("rests", [2, NP], F32, 176)
-        for t, src in zip(halves_of(rests[:, 0, :]), halves_of(got[6])):
-            times(t, src, gain_dealt[:, 2:3])
-        for t in halves_of(rests[:, 0, :]):
-            nc.gpsimd.tensor_scalar(out=t, in0=t, scalar1=HUGE, scalar2=0.0, op0=ALU.min, op1=ALU.max)
-        for t, less in zip(halves_of(rests[:, 0, :]), halves_of(stocks[6])):
-            nc.gpsimd.tensor_tensor(t, t, less, ALU.subtract)
-
-        planes_z = place("planes_z", [4, NP], BF16, 196)
-        turned16 = place("turned16", [2, 2, 4, P], BF16, 224)
+            for half in range(2):
+                scale_log(c, half_cols(half))
+            for half in range(2):
+                join(c, half_cols(half))
+        exponentials(6, 200, 212)
+        less_stock(6, 196)
+        for t in soft[6]:
+            logarithm(t, t, one)
+        logs[6] = place("scaled6", [NP], F32, 216)
         for half in range(2):
-            for t in range(2):
-                nc.scalar.activation(out=turned16[:, t, half, :, :], in_=summed(PLAIN + t, half)[:], func=ACT.Copy, scale=-1.0)
-        for half in range(2):
-            for t in range(2):
-                back = bank(f"back16_{t}{half}", [4, P], 2 * half + t, BF16)
-                for b in range(4):
-                    nc.tensor.transpose(back[:, b, :], turned16[:, t, half, b, :], ident16[:])
-                nc.scalar.copy(out=planes_z[:, t, half_cols(half)], in_=back[:].rearrange("p b m -> p (b m)"))
+            nc.scalar.activation(
+                out=logs[6][:, half_cols(half)], in_=soft[6][half], func=ACT.Identity, scale=column(gains, 6), bias=column(drop, 6)
+            )
+            join(6, half_cols(half))
+        one = next_one(soft[6][0][:, 0:1])
 
-        last = TILES - 1
-        chunks = [slice(lo, hi) for lo, hi in zip(CUTS, CUTS[1:])]
-        size[last] = place("size_last", [NP], F32, 226)
-        for cols in [slice(lo, hi) for lo, hi in zip(PIECES, PIECES[1:])]:
-            nc.scalar.activation(out=size[last][:, cols], in_=got[last][:, cols], func=ACT.Abs)
-            nc.scalar.activation(out=exps[:, 1, cols], in_=size[last][:, cols], func=ACT.Exp, scale=-1.0)
-        logs = place("logs", [2, NP], F32, 226)
-        codes0 = place("codes0", [NP], U32, PAGE_AT[last])
-        scales0 = place("scales0", [NP], U8, 225)
-        codes1 = place("codes1", [NP], U32, 212)
-        scales1 = place("scales1", [NP], U8, 217)
-        woven1 = place("woven1", [NP, 4], BF16, 204)
+        bent[LAST] = place("bent7", [NP], F32, 200)
+        soft[LAST] = place("soft7", [NP], F32, 98)
+        bend(LAST, bent[LAST][:, pieces[0]], fetched_piece(pieces[0]))
+        for before, piece in zip(pieces, pieces[1:]):
+            bend(LAST, bent[LAST][:, piece], fetched_piece(piece))
+            exponential(LAST, soft[LAST][:, before], bent[LAST][:, before])
+        exponential(LAST, soft[LAST][:, pieces[-1]], bent[LAST][:, pieces[-1]])
+        codes0 = place("codes0", [NP], U32, 220)
+        scales0 = place("scales0", [NP], U8, 57)
+        codes1 = place("codes1", [NP], U32, 106)
+        scales1 = place("scales1", [NP], U8, 47)
+        woven1 = place("woven1", [NP, 2, 2], BF16, 156)
+        rests = place("rests", [NP], F32, 196)
         for half in range(2):
             cols = half_cols(half)
-            nc.vector.tensor_scalar(
-                out=rests[:, 1, cols], in0=got[last][:, cols], scalar1=0.0, scalar2=gain_dealt[:, 3:4], op0=ALU.max, op1=ALU.mult
-            )
             nc.vector.quantize_mx(
                 out=codes0[:, cols].bitcast(FP8X4), scales=scales0[:, cols],
                 in_=woven0[:, cols, :].rearrange("p m u -> p (m u)").bitcast(BF16),
             )
-            nc.vector.tensor_tensor(rests[:, 1, cols], rests[:, 1, cols], stocks[last][:, cols], ALU.subtract)
+        for half in range(2):
+            cols = half_cols(half)
+            nc.vector.tensor_tensor(rests[:, cols], bent[LAST][:, cols], shifted[:, cols], ALU.subtract)
+        chunks = [slice(lo, hi) for lo, hi in zip(TAIL_CUTS, TAIL_CUTS[1:])]
         accs = []
         for j, cols in enumerate(chunks):
             width = cols.stop - cols.start
@@ -465,31 +494,43 @@ def tile_list_vaccine_dispatch_kernel(
                 accs.append((j, first, bank(f"res{j}_{first}", [count, width], len(accs))))
         for j, first, acc in accs:
             second_pass(acc, first, 0, chunks[j], codes0, scales0)
+        logs[LAST] = place("log7", [NP], F32, 224)
         for cols in chunks:
-            for e in range(2):
-                nc.scalar.activation(out=logs[:, e, cols], in_=exps[:, e, cols], func=ACT.Ln, bias=ones[:, 1:2])
-        for j, cols in enumerate(chunks):
-            for e in range(2):
-                nc.vector.scalar_tensor_tensor(
-                    out=planes_z[:, 2 + e, cols], in0=logs[:, e, cols], scalar=gain_dealt[:, 2 + e : 3 + e],
-                    in1=rests[:, e, cols], op0=ALU.mult, op1=ALU.add,
-                )
-            (nc.scalar.copy if j in WEAVES_ON_SCALAR else nc.vector.tensor_copy)(
-                out=woven1[:, cols, :].rearrange("p (c i) t -> p c t i", i=4),
-                in_=planes_z[:, :, cols].rearrange("p t (c i) -> p c t i", i=4),
+            logarithm(logs[LAST][:, cols], soft[LAST][:, cols], one)
+
+        def last_join(cols):
+            nc.vector.scalar_tensor_tensor(
+                out=pair_slot(LAST, cols), in0=logs[LAST][:, cols], scalar=column(gains, LAST),
+                in1=rests[:, cols], op0=ALU.mult, op1=ALU.add,
             )
+
+        def weave(cols):
+            half = cols.start // BANK
+            src = pairs[half][:, :, cols.start - half * BANK : cols.stop - half * BANK, :]
+            nc.vector.tensor_copy(out=woven1[:, cols, :, :], in_=src.rearrange("p u m e -> p m u e"))
+
+        def finish(j):
+            cols = chunks[j]
             nc.vector.quantize_mx(
                 out=codes1[:, cols].bitcast(FP8X4), scales=scales1[:, cols],
-                in_=woven1[:, cols, :].rearrange("p m t -> p (m t)"),
+                in_=woven1[:, cols, :, :].rearrange("p m u e -> p (m u e)"),
             )
             for index, (jj, first, acc) in enumerate(accs):
                 if jj == j:
                     count = acc.shape[1]
                     second_pass(acc, first, 1, cols, codes1, scales1)
-                    staged = place(f"staged{index}", acc.shape[1:], F32, WORDS + 2 * index)
-                    if index in COPIES_ON_VECTOR:
+                    staged = place(f"staged{index}", acc.shape[1:], F32, 2 * index)
+                    if index == len(accs) - 1:
                         nc.vector.tensor_copy(out=staged[:], in_=acc[:])
                     else:
                         nc.scalar.copy(out=staged[:], in_=acc[:])
                     rows = out[first * P : (first + count) * P, cols]
                     nc.sync.dma_start(out=rows.rearrange("(i p) n -> p i n", p=P), in_=staged[:])
+
+        for step in range(len(chunks) + 2):
+            if step < len(chunks):
+                last_join(chunks[step])
+            if step >= 2:
+                finish(step - 2)
+            if 1 <= step <= len(chunks):
+                weave(chunks[step - 1])

@@ -25,8 +25,8 @@ PLAIN = 4
 LAST = TILES - 1
 KNEE = 24.0
 OPENING = 256
-TAIL_CUTS = (0, 128, 256, 512, 768, 1024)
-LAST_PIECES = (0, 256, 512, 768, 896, 1024)
+TAIL_CUTS = (0, 256, 512, 768, 1024)
+LAST_PIECES = (0, 384, 768, 1024)
 KB = 1024
 
 
@@ -180,13 +180,13 @@ def tile_list_vaccine_dispatch_kernel(
         def halves(tile):
             return [tile[:, half_cols(half)] for half in range(2)]
 
-        def exponentials(c, bent_kb, soft_kb, side_kb=None):
+        def exponentials(c, bent_kb, soft_kb, side_kb=None, side_half=0):
             bent[c] = place(f"bent{c}", [NP], F32, bent_kb)
             logs[c] = place(f"soft{c}", [NP], F32, soft_kb)
             soft[c] = halves(logs[c])
             if side_kb is not None:
                 side = place(f"side{c}", [BANK], F32, side_kb)
-                soft[c][0] = side[:]
+                soft[c][side_half] = side[:]
             for dst, src in zip(halves(bent[c]), halves(got[c])):
                 bend(c, dst, src)
             for dst, src in zip(soft[c], halves(bent[c])):
@@ -229,24 +229,25 @@ def tile_list_vaccine_dispatch_kernel(
                 add_turned(c, half, bent[c], True, False)
                 add_turned(c, half, stocks[c], False, False)
 
-        def close_and_round(c, half):
+        def close_sum(c, half):
             add_turned(c, half, logs[c], False, True)
+
+        def round_sum(c, half):
             nc.scalar.copy(
                 out=zt[:, 8 * half : 8 * half + 8, c * 32 : c * 32 + 32, :].rearrange("m (b u) p e -> m b u p e", u=2),
                 in_=turned[c, half][:].rearrange("m b (p u e) -> m b u p e", u=2, e=2),
             )
 
-        def less_stock(c, kb=None):
+        def less_stock(c, kb=None, parts=(slice(0, BANK), slice(BANK, NP))):
             src = stocks[c]
             if kb is not None:
                 stocks[c] = place(f"rest{c}", [NP], F32, kb)
-            for dst, more, less in zip(halves(stocks[c]), halves(bent[c]), halves(src)):
-                nc.gpsimd.tensor_tensor(dst, more, less, ALU.subtract)
+            for cols in parts:
+                nc.gpsimd.tensor_tensor(stocks[c][:, cols], bent[c][:, cols], src[:, cols], ALU.subtract)
 
         def pair_slot(c, cols):
-            half = cols.start // BANK
             t = c - PLAIN
-            return pairs[half][:, t // 2, cols.start - half * BANK : cols.stop - half * BANK, t % 2]
+            return pairs[:, t // 2, cols, t % 2]
 
         def join(c, cols):
             nc.gpsimd.tensor_tensor(pair_slot(c, cols), logs[c][:, cols], stocks[c][:, cols], ALU.add)
@@ -394,7 +395,8 @@ def tile_list_vaccine_dispatch_kernel(
         for c in (0, 1):
             for half in range(2):
                 scale_log(c, half_cols(half))
-                close_and_round(c, half)
+                close_sum(c, half)
+                round_sum(c, half)
         scatter(4, put[4][:])
         weigh_whole(5, 176)
         scatter(5, put[5][:])
@@ -405,17 +407,24 @@ def tile_list_vaccine_dispatch_kernel(
         open_sums(2)
         open_sums(3)
         weigh_whole(6, 28)
-        weigh_whole(7, 156)
         one = logarithms((2, 3), one, 98)
         gather(4, 166)
         gather(5, 196)
         scatter(6, put[6][:])
+        for c in (2, 3):
+            for half in range(2):
+                scale_log(c, half_cols(half))
+                close_sum(c, half)
         for half in range(2):
             for c in (2, 3):
-                scale_log(c, half_cols(half))
-                close_and_round(c, half)
+                round_sum(c, half)
+        weigh_whole(7, 192)
         shifted = place("shifted", [NP], F32, 184)
         nc.gpsimd.tensor_scalar(out=shifted[:], in0=stocks[LAST][:], scalar1=column(lift, LAST), scalar2=1.0, op0=ALU.add, op1=ALU.mult)
+        shifted6 = place("shifted6", [NP], F32, 160)
+        nc.gpsimd.tensor_scalar(
+            out=shifted6[:], in0=stocks[6][:], scalar1=column(lift, 6), scalar2=1.0, op0=ALU.add, op1=ALU.mult
+        )
         woven0 = place("woven0", [NP, 2], F32, 144)
         for j in range(4):
             back = bank(f"back{j}", [2, 2, P], j)
@@ -433,35 +442,38 @@ def tile_list_vaccine_dispatch_kernel(
         load_page(LAST)
         scatter(LAST, put[LAST][:])
         pieces = [slice(lo, hi) for lo, hi in zip(LAST_PIECES, LAST_PIECES[1:])]
-        fetched = [place(f"fetched{half}", [BANK], F32, 220 + 4 * half) for half in range(2)]
+        first_cut = LAST_PIECES[1]
+        fetched = [place("fetched0", [first_cut], F32, 220), place("fetched1", [NP - first_cut], F32, 86)]
 
         def fetched_piece(cols):
-            half = cols.start // BANK
-            return fetched[half][:, cols.start - half * BANK : cols.stop - half * BANK]
+            if cols.start == 0:
+                return fetched[0][:]
+            return fetched[1][:, cols.start - first_cut : cols.stop - first_cut]
 
         for piece in pieces:
             fetch(LAST, fetched_piece(piece), piece.start, piece.stop)
 
-        pairs = [place(f"pairs{half}", [2, BANK, 2], BF16, kb) for half, kb in enumerate((51, 110))]
+        pairs = place("pairs", [2, NP, 2], BF16, 66)
         exponentials(5, 166, 204, 142)
         less_stock(5)
         one = logarithms((4, 5), one, 196)
-        for c in (4, 5):
-            for half in range(2):
-                scale_log(c, half_cols(half))
-            for half in range(2):
-                join(c, half_cols(half))
-        exponentials(6, 200, 212)
-        less_stock(6, 196)
-        for t in soft[6]:
-            logarithm(t, t, one)
-        logs[6] = place("scaled6", [NP], F32, 216)
+        everything = slice(0, NP)
         for half in range(2):
-            nc.scalar.activation(
-                out=logs[6][:, half_cols(half)], in_=soft[6][half], func=ACT.Identity, scale=column(gains, 6), bias=column(drop, 6)
-            )
-            join(6, half_cols(half))
-        one = next_one(soft[6][0][:, 0:1])
+            scale_log(4, half_cols(half))
+        join(4, half_cols(0))
+        scale_log(5, everything)
+        join(4, half_cols(1))
+        join(5, everything)
+        exponentials(6, 200, 212, 164, 1)
+        lower, upper = half_cols(0), half_cols(1)
+        rest6 = place("rest6", [NP], F32, 196)
+        nc.gpsimd.tensor_tensor(rest6[:], bent[6][:], shifted6[:], ALU.subtract)
+        for dst, src in zip(halves(logs[6]), soft[6]):
+            logarithm(dst, src, one)
+        scaled = place("scaled6", [BANK], F32, 216)
+        nc.scalar.activation(out=scaled[:], in_=logs[6][:, lower], func=ACT.Copy, scale=column(gains, 6))
+        nc.gpsimd.tensor_tensor(pair_slot(6, lower), scaled[:], rest6[:, lower], ALU.add)
+        one = next_one(soft[6][1][:, 0:1])
 
         bent[LAST] = place("bent7", [NP], F32, 200)
         soft[LAST] = place("soft7", [NP], F32, 98)
@@ -474,17 +486,15 @@ def tile_list_vaccine_dispatch_kernel(
         scales0 = place("scales0", [NP], U8, 57)
         codes1 = place("codes1", [NP], U32, 106)
         scales1 = place("scales1", [NP], U8, 47)
-        woven1 = place("woven1", [NP, 2, 2], BF16, 156)
-        rests = place("rests", [NP], F32, 196)
-        for half in range(2):
-            cols = half_cols(half)
-            nc.vector.quantize_mx(
-                out=codes0[:, cols].bitcast(FP8X4), scales=scales0[:, cols],
-                in_=woven0[:, cols, :].rearrange("p m u -> p (m u)").bitcast(BF16),
-            )
-        for half in range(2):
-            cols = half_cols(half)
-            nc.vector.tensor_tensor(rests[:, cols], bent[LAST][:, cols], shifted[:, cols], ALU.subtract)
+        woven1 = place("woven1", [NP, 2, 2], BF16, 74)
+        rests = place("rests", [NP], F32, 216)
+        nc.vector.quantize_mx(
+            out=codes0[:].bitcast(FP8X4), scales=scales0[:], in_=woven0[:].rearrange("p m u -> p (m u)").bitcast(BF16)
+        )
+        nc.vector.scalar_tensor_tensor(
+            out=pair_slot(6, upper), in0=logs[6][:, upper], scalar=column(gains, 6), in1=rest6[:, upper], op0=ALU.mult, op1=ALU.add
+        )
+        nc.vector.tensor_tensor(rests[:], bent[LAST][:], shifted[:], ALU.subtract)
         chunks = [slice(lo, hi) for lo, hi in zip(TAIL_CUTS, TAIL_CUTS[1:])]
         accs = []
         for j, cols in enumerate(chunks):
@@ -494,7 +504,7 @@ def tile_list_vaccine_dispatch_kernel(
                 accs.append((j, first, bank(f"res{j}_{first}", [count, width], len(accs))))
         for j, first, acc in accs:
             second_pass(acc, first, 0, chunks[j], codes0, scales0)
-        logs[LAST] = place("log7", [NP], F32, 224)
+        logs[LAST] = place("log7", [NP], F32, 86)
         for cols in chunks:
             logarithm(logs[LAST][:, cols], soft[LAST][:, cols], one)
 
@@ -505,9 +515,7 @@ def tile_list_vaccine_dispatch_kernel(
             )
 
         def weave(cols):
-            half = cols.start // BANK
-            src = pairs[half][:, :, cols.start - half * BANK : cols.stop - half * BANK, :]
-            nc.vector.tensor_copy(out=woven1[:, cols, :, :], in_=src.rearrange("p u m e -> p m u e"))
+            nc.vector.tensor_copy(out=woven1[:, cols, :, :], in_=pairs[:, :, cols, :].rearrange("p u m e -> p m u e"))
 
         def finish(j):
             cols = chunks[j]

@@ -1,3 +1,4 @@
+import math
 from contextlib import ExitStack
 
 import concourse.mybir as mybir
@@ -24,6 +25,8 @@ TILES = H // P
 PLAIN = 4
 LAST = TILES - 1
 KNEE = 24.0
+CAP = math.exp(KNEE)
+EARLY = 768
 OPENING = 256
 TAIL_CUTS = (0, 256, 512, 768, 1024)
 LAST_PIECES = (0, 384, 768, 1024)
@@ -180,13 +183,13 @@ def tile_list_vaccine_dispatch_kernel(
         def halves(tile):
             return [tile[:, half_cols(half)] for half in range(2)]
 
-        def exponentials(c, bent_kb, soft_kb, side_kb=None, side_half=0):
+        def exponentials(c, bent_kb, soft_kb, side_kb=None):
             bent[c] = place(f"bent{c}", [NP], F32, bent_kb)
             logs[c] = place(f"soft{c}", [NP], F32, soft_kb)
             soft[c] = halves(logs[c])
             if side_kb is not None:
                 side = place(f"side{c}", [BANK], F32, side_kb)
-                soft[c][side_half] = side[:]
+                soft[c][0] = side[:]
             for dst, src in zip(halves(bent[c]), halves(got[c])):
                 bend(c, dst, src)
             for dst, src in zip(soft[c], halves(bent[c])):
@@ -419,8 +422,8 @@ def tile_list_vaccine_dispatch_kernel(
             for c in (2, 3):
                 round_sum(c, half)
         weigh_whole(7, 192)
-        shifted = place("shifted", [NP], F32, 184)
-        nc.gpsimd.tensor_scalar(out=shifted[:], in0=stocks[LAST][:], scalar1=column(lift, LAST), scalar2=1.0, op0=ALU.add, op1=ALU.mult)
+        shifted = place("shifted", [EARLY], F32, 184)
+        nc.gpsimd.tensor_scalar(out=shifted[:], in0=stocks[LAST][:, :EARLY], scalar1=column(lift, LAST), scalar2=1.0, op0=ALU.add, op1=ALU.mult)
         shifted6 = place("shifted6", [NP], F32, 160)
         nc.gpsimd.tensor_scalar(
             out=shifted6[:], in0=stocks[6][:], scalar1=column(lift, 6), scalar2=1.0, op0=ALU.add, op1=ALU.mult
@@ -442,13 +445,10 @@ def tile_list_vaccine_dispatch_kernel(
         load_page(LAST)
         scatter(LAST, put[LAST][:])
         pieces = [slice(lo, hi) for lo, hi in zip(LAST_PIECES, LAST_PIECES[1:])]
-        first_cut = LAST_PIECES[1]
-        fetched = [place("fetched0", [first_cut], F32, 220), place("fetched1", [NP - first_cut], F32, 86)]
+        fetched = [place(f"fetched{i}", [hi - lo], F32, kb) for i, (lo, hi, kb) in enumerate(zip(LAST_PIECES, LAST_PIECES[1:], (220, 86, 82)))]
 
         def fetched_piece(cols):
-            if cols.start == 0:
-                return fetched[0][:]
-            return fetched[1][:, cols.start - first_cut : cols.stop - first_cut]
+            return fetched[LAST_PIECES.index(cols.start)][:]
 
         for piece in pieces:
             fetch(LAST, fetched_piece(piece), piece.start, piece.stop)
@@ -464,24 +464,34 @@ def tile_list_vaccine_dispatch_kernel(
         scale_log(5, everything)
         join(4, half_cols(1))
         join(5, everything)
-        exponentials(6, 200, 212, 164, 1)
-        lower, upper = half_cols(0), half_cols(1)
+        lower, upper = slice(0, EARLY), slice(EARLY, NP)
+        bent[6] = place("bent6", [NP], F32, 200)
+        logs[6] = place("soft6", [NP], F32, 212)
+        side6 = place("side6", [NP - EARLY], F32, 152)
+        for dst, src in zip(halves(bent[6]), halves(got[6])):
+            bend(6, dst, src)
+        exponential(6, logs[6][:, :BANK], bent[6][:, :BANK])
+        exponential(6, logs[6][:, BANK:EARLY], bent[6][:, BANK:EARLY])
+        exponential(6, side6[:], bent[6][:, upper])
         rest6 = place("rest6", [NP], F32, 196)
         nc.gpsimd.tensor_tensor(rest6[:], bent[6][:], shifted6[:], ALU.subtract)
-        for dst, src in zip(halves(logs[6]), soft[6]):
-            logarithm(dst, src, one)
-        scaled = place("scaled6", [BANK], F32, 216)
+        logarithm(logs[6][:, lower], logs[6][:, lower], one)
+        logarithm(logs[6][:, upper], side6[:], one)
+        scaled = place("scaled6", [EARLY], F32, 216)
         nc.scalar.activation(out=scaled[:], in_=logs[6][:, lower], func=ACT.Copy, scale=column(gains, 6))
         nc.gpsimd.tensor_tensor(pair_slot(6, lower), scaled[:], rest6[:, lower], ALU.add)
-        one = next_one(soft[6][1][:, 0:1])
+        last_one = place("last_one", [1], F32, 152)
+        one = next_one(last_one[:])
 
-        bent[LAST] = place("bent7", [NP], F32, 200)
+        bent[LAST] = place("bent7", [EARLY], F32, 152 + EDGE)
         soft[LAST] = place("soft7", [NP], F32, 98)
-        bend(LAST, bent[LAST][:, pieces[0]], fetched_piece(pieces[0]))
-        for before, piece in zip(pieces, pieces[1:]):
+        raw_exp = place("raw_exp", [NP - EARLY], F32, 85 + EDGE)
+        floored = place("floored", [NP - EARLY], F32, 144)
+        for piece in pieces[:2]:
             bend(LAST, bent[LAST][:, piece], fetched_piece(piece))
-            exponential(LAST, soft[LAST][:, before], bent[LAST][:, before])
-        exponential(LAST, soft[LAST][:, pieces[-1]], bent[LAST][:, pieces[-1]])
+        for piece in pieces[:2]:
+            exponential(LAST, soft[LAST][:, piece], bent[LAST][:, piece])
+        nc.scalar.activation(out=raw_exp[:], in_=fetched_piece(pieces[2]), func=ACT.Exp, scale=-1.0)
         codes0 = place("codes0", [NP], U32, 220)
         scales0 = place("scales0", [NP], U8, 57)
         codes1 = place("codes1", [NP], U32, 106)
@@ -494,7 +504,12 @@ def tile_list_vaccine_dispatch_kernel(
         nc.vector.scalar_tensor_tensor(
             out=pair_slot(6, upper), in0=logs[6][:, upper], scalar=column(gains, 6), in1=rest6[:, upper], op0=ALU.mult, op1=ALU.add
         )
-        nc.vector.tensor_tensor(rests[:], bent[LAST][:], shifted[:], ALU.subtract)
+        nc.vector.tensor_tensor(rests[:, lower], bent[LAST][:], shifted[:], ALU.subtract)
+        nc.vector.tensor_scalar(
+            out=floored[:], in0=fetched_piece(pieces[2]), scalar1=-KNEE, scalar2=column(gains, LAST), op0=ALU.max, op1=ALU.mult
+        )
+        nc.vector.tensor_scalar_min(out=soft[LAST][:, upper], in0=raw_exp[:], scalar1=CAP)
+        nc.vector.tensor_tensor(rests[:, upper], floored[:], stocks[LAST][:, upper], ALU.subtract)
         chunks = [slice(lo, hi) for lo, hi in zip(TAIL_CUTS, TAIL_CUTS[1:])]
         accs = []
         for j, cols in enumerate(chunks):
@@ -504,7 +519,7 @@ def tile_list_vaccine_dispatch_kernel(
                 accs.append((j, first, bank(f"res{j}_{first}", [count, width], len(accs))))
         for j, first, acc in accs:
             second_pass(acc, first, 0, chunks[j], codes0, scales0)
-        logs[LAST] = place("log7", [NP], F32, 86)
+        logs[LAST] = place("log7", [NP], F32, 87.5 - EDGE)
         for cols in chunks:
             logarithm(logs[LAST][:, cols], soft[LAST][:, cols], one)
 
@@ -528,7 +543,7 @@ def tile_list_vaccine_dispatch_kernel(
                     count = acc.shape[1]
                     second_pass(acc, first, 1, cols, codes1, scales1)
                     staged = place(f"staged{index}", acc.shape[1:], F32, 2 * index)
-                    if index == len(accs) - 1:
+                    if index in (5, 7):
                         nc.vector.tensor_copy(out=staged[:], in_=acc[:])
                     else:
                         nc.scalar.copy(out=staged[:], in_=acc[:])

@@ -276,9 +276,11 @@ def tile_list_vaccine_dispatch_kernel(
         nc.sync.dma_start(out=gains[:, 1, 0:4], in_=gain[PASS:].rearrange("(p t) -> p t", t=4))
         nc.sync.dma_start(out=words[0][:], in_=tab_words[0].rearrange("p t i -> p (t i)").bitcast(I32))
         for q in range(2):
-            nc.gpsimd.dma_start(
-                out=planes[32 * q : 32 * q + 8, :].bitcast(I32), in_=tab_scales[:, 4 * q : 4 * q + 4, :].bitcast(I32)
-            )
+            for a in range(2):
+                nc.gpsimd.dma_start(
+                    out=planes[32 * q + 4 * a : 32 * q + 4 * a + 4, :].bitcast(I32),
+                    in_=tab_scales[a, 4 * q : 4 * q + 4, :].bitcast(I32),
+                )
         load_w1(raw[0], 0, P)
         nc.sync.dma_start(out=weights[:, :OPENING], in_=wgs[:, :OPENING])
         nc.sync.dma_start(out=gain_rows[0:PLAIN, :], in_=gain[:PASS].rearrange("(c p) -> c p", p=P))

import math
from contextlib import ExitStack

import concourse.mybir as mybir
from concourse.masks import make_identity

K, T, S, T2, NP, H, N = 1024, 4096, 1024, 2048, 1024, 1024, 512
FLOPS = 2 * K * H * S + 2 * H * N * NP

F32 = mybir.dt.float32
BF16 = mybir.dt.bfloat16
I32 = mybir.dt.int32
U32 = mybir.dt.uint32
U16 = mybir.dt.uint16
U8 = mybir.dt.uint8
FP8X4 = mybir.dt.float8_e4m3fn_x4
FP4X4 = mybir.dt.float4_e2m1fn_x4
ALU = mybir.AluOpType
ACT = mybir.ActivationFunctionType

P = 128
BANK = 512
PASS = 512
TILES = H // P
PLAIN = 4
LAST = TILES - 1
KNEE = 24.0
CAP = math.exp(KNEE)
EARLY = 768
OPENING = 256
TAIL_CUTS = (0, 256, 512, 768, 1024)
LAST_PIECES = (0, 384, 768, 1024)
KB = 1024


def tile_list_vaccine_dispatch_kernel(
    tc, tab_words, tab_scales, offs, w1, page0, wgs, offs2, offs3, gain, stock, w2_words, w2_scales, out
):
    nc = tc.nc
    with ExitStack() as ctx:
        held = ctx.enter_context(tc.tile_pool(name="held", bufs=1))
        arena = ctx.enter_context(tc.tile_pool(name="arena", bufs=1))
        ps = ctx.enter_context(tc.psum_pool(name="ps", bufs=1))

        def place(name, shape, dtype, kb):
            return arena.tile([P] + list(shape), dtype, name=name, offset=int(kb * KB), align_bytes=64)

        def bank(name, shape, index, dtype=F32):
            return ps.tile([P] + shape, dtype, name=name, offset=index * 2 * KB)

        def half_cols(half):
            return slice(half * BANK, (half + 1) * BANK)

        def rows_of(dram, c):
            if c < PLAIN:
                return dram[c * P : (c + 1) * P, :]
            return dram[PASS:, :].rearrange("(p t) n -> p t n", t=4)[:, c - PLAIN, :]

        list1 = held.tile([P, S // 16], U16, name="list1")
        list2 = held.tile([P, S // 16], U16, name="list2")
        list3 = held.tile([P, NP // 16], U16, name="list3")
        ident = held.tile([P, P], F32, name="ident")
        gains = held.tile([P, 2, 8], F32, name="gains")
        minus = held.tile([P, 2, 4], F32, name="minus")
        inverse = held.tile([P, 2, 4], F32, name="inverse")
        lift = held.tile([P, 2, 4], F32, name="lift")
        drop = held.tile([P, 2, 4], F32, name="drop")
        knee = held.tile([P, 1], F32, name="knee")
        first_one = held.tile([P, 1], F32, name="first_one")
        w2c = held.tile([P, 2, 2 * N], U8, name="w2c", align_bytes=64)
        w2s = held.tile([P, 2, N], U8, name="w2s", align_bytes=64)

        def column(tile, c):
            return tile[:, c // PLAIN, c % PLAIN : c % PLAIN + 1]

        words = [place(f"words{a}", [T], I32, 16 * a) for a in range(2)]
        planes = place("planes", [T], U8, 34)
        stage0 = place("stage0", [1024], BF16, 32)
        picked = [place("picked0", [S], U32, 38), place("picked1", [S], U32, 32)]
        picked_scales = place("picked_scales", [S], U8, 42)
        weights = place("weights", [S], F32, 43)
        gain_rows = place("gain_rows", [P], F32, 234)
        PAGE_AT = (58, 66, 74, 82, 58, 66, 74, 226)
        raw = {0: place("raw0", [2, 4, P], F32, 90), 1: place("raw1", [2, 4, P], F32, 94)}
        raw23 = [place(f"raw23_{a}", [4, 2 * P], F32, 98 + 4 * a) for a in range(2)]
        raw_dealt = [place(f"raw_dealt{a}", [4, PASS], F32, 106 + 8 * a) for a in range(2)]

        pages, stocks, quantised, sums, put, got, bent, soft, logs = {}, {}, {}, {}, {}, {}, {}, {}, {}
        STOCK_AT = (16, 20, 24, 28, 106, 128, 90, 102)
        EDGE = 1 / 16
        CODES_AT = {0: (47, 55), 1: (122, 55.25), 2: (128, 55.5), 4: (51, 132)}

        def load_w1(tile, first, width):
            for a in range(2):
                rows = w1[a * PASS : (a + 1) * PASS, first : first + width]
                nc.sync.dma_start(out=tile[:, a, :, :], in_=rows.rearrange("(p j) c -> p j c", j=4))

        def load_page(c):
            pages[c] = place(f"page{c}", [T2], F32, PAGE_AT[c])
            nc.sync.dma_start(out=pages[c][:], in_=rows_of(page0, c))

        def load_stock(c):
            stocks[c] = place(f"stock{c}", [NP], F32, STOCK_AT[c])
            nc.sync.dma_start(out=stocks[c][:], in_=rows_of(stock, c))

        def round_w1(c, stage, i):
            nc.scalar.copy(
                out=stage[:, i * 1024 : (i + 1) * 1024].rearrange("p (a c i t) -> p a c t i", a=2, i=4, t=4),
                in_=raw[c][:].rearrange("p a t (c i) -> p a c t i", i=4),
            )

        def round_w1_pair(a, stage):
            nc.scalar.copy(
                out=stage[:].rearrange("p (w a c i t) -> p a w c t i", w=2, a=2, i=4, t=4)[:, a, :, :, :, :],
                in_=raw23[a][:].rearrange("p t (w c i) -> p w c t i", w=2, i=4),
            )

        def round_w1_dealt(a, stage):
            nc.scalar.copy(
                out=stage[:].rearrange("p (t a m j) -> p a m t j", t=4, a=2, j=4)[:, a, :, :, :],
                in_=raw_dealt[a][:].rearrange("p j (m t) -> p m t j", t=4),
            )

        def quantise_w1(first, count, stage):
            codes = place(f"w1c{first}", [count * 2 * P], U32, CODES_AT[first][0])
            scales = place(f"w1s{first}", [count * 2 * P], U8, CODES_AT[first][1])
            nc.vector.quantize_mx(out=codes[:].bitcast(FP8X4), scales=scales[:], in_=stage[:])
            for i in range(count):
                part = slice(i * 2 * P, (i + 1) * 2 * P)
                quantised[first + i] = (codes[:, part], scales[:, part])

        def product(c, lo, hi, index, dst):
            codes, scales = quantised[c]
            acc = bank(f"acc{c}_{lo}", [hi - lo], index)
            for a in range(2):
                nc.tensor.matmul_mx(
                    out=acc[:],
                    lhsT=codes[:, a * P : (a + 1) * P].bitcast(FP8X4),
                    lhsT_scale=scales[:, a * P : (a + 1) * P],
                    rhs=picked[a][:, lo:hi].bitcast(FP8X4),
                    rhs_scale=picked_scales[4 * a : P, lo:hi],
                    start=(a == 0),
                    stop=(a == 1),
                )
            nc.scalar.copy(out=dst, in_=acc[:])

        def whole_product(c, kb):
            sums[c] = place(f"sums{c}", [S], F32, kb)
            for half in range(2):
                product(c, half * BANK, (half + 1) * BANK, 2 * ((c + 1) % 2) + half, sums[c][:, half_cols(half)])

        def weighted_scatter(c, lo, hi, src):
            nc.vector.tensor_tensor(pages[c][:].indirect(list2[:, lo // 16 : hi // 16]), src, weights[:, lo:hi], ALU.mult)

        def scatter(c, src, lo=0, hi=S):
            nc.vector.tensor_copy(pages[c][:].indirect(list2[:, lo // 16 : hi // 16]), src)

        def fetch(c, dst, lo, hi):
            nc.vector.tensor_copy(dst, pages[c][:].indirect(list3[:, lo // 16 : hi // 16]))

        def gather(c, kb, cuts=(0, NP)):
            got[c] = place(f"got{c}", [NP], F32, kb)
            for lo, hi in zip(cuts, cuts[1:]):
                fetch(c, got[c][:, lo:hi], lo, hi)

        def weigh(c, dst, src, lo=0, hi=S):
            by = weights[:, lo:hi] if c < PLAIN else dealt[:, (c - PLAIN) * S + lo : (c - PLAIN) * S + hi]
            nc.gpsimd.tensor_tensor(dst, src, by, ALU.mult)

        def weigh_whole(c, kb=None):
            put[c] = sums[c] if kb is None else place(f"put{c}", [S], F32, kb)
            weigh(c, put[c][:], sums[c][:])

        def bend(c, dst, src):
            nc.scalar.activation(out=dst, in_=src, func=ACT.Relu, scale=column(gains, c), bias=column(lift, c))

        def exponential(c, dst, src):
            nc.scalar.activation(out=dst, in_=src, func=ACT.Exp, scale=column(inverse, c), bias=knee[:])

        def logarithm(dst, src, one):
            nc.scalar.activation(out=dst, in_=src, func=ACT.Ln, bias=one)

        def halves(tile):
            return [tile[:, half_cols(half)] for half in range(2)]

        def exponentials(c, bent_kb, soft_kb, side_kb=None):
            bent[c] = place(f"bent{c}", [NP], F32, bent_kb)
            logs[c] = place(f"soft{c}", [NP], F32, soft_kb)
            soft[c] = halves(logs[c])
            if side_kb is not None:
                side = place(f"side{c}", [BANK], F32, side_kb)
                soft[c][0] = side[:]
            for dst, src in zip(halves(bent[c]), halves(got[c])):
                bend(c, dst, src)
            for dst, src in zip(soft[c], halves(bent[c])):
                exponential(c, dst, src)

        def next_one(one):
            nc.scalar.activation(out=one, in_=knee[:], func=ACT.Exp, scale=0.0)
            return one

        def logarithms(pair, one, kb):
            logs[pair[0]] = place(f"log{pair[0]}", [NP], F32, kb)
            for c in pair:
                for dst, src in zip(halves(logs[c]), soft[c]):
                    logarithm(dst, src, one)
            return next_one(soft[pair[1]][0][:, 0:1])

        def scale_log(c, cols):
            t = logs[c][:, cols]
            nc.gpsimd.tensor_scalar(out=t, in0=t, scalar1=column(gains, c), scalar2=column(drop, c), op0=ALU.mult, op1=ALU.add)

        def negate_stock(c, kb):
            src = stocks[c]
            stocks[c] = place(f"less{c}", [NP], F32, kb)
            nc.gpsimd.tensor_scalar(out=stocks[c][:], in0=src[:], scalar1=-1.0, scalar2=0.0, op0=ALU.mult, op1=ALU.add)

        turned = {}

        def add_turned(c, half, src, first, final):
            if first:
                turned[c, half] = bank(f"turned{c}_{half}", [4, P], 4 + 2 * (c % 2) + half)
            for b in range(4):
                lo = half * BANK + b * P
                nc.tensor.matmul(
                    turned[c, half][:, b, :], src[:, lo : lo + P], ident[:], is_transpose=True,
                    start=(first and b == 0), stop=(final and b == 3),
                )

        def open_sums(c):
            for half in range(2):
                add_turned(c, half, bent[c], True, False)
                add_turned(c, half, stocks[c], False, False)

        def close_sum(c, half):
            add_turned(c, half, logs[c], False, True)

        def round_sum(c, half):
            nc.scalar.copy(
                out=zt[:, 8 * half : 8 * half + 8, c * 32 : c * 32 + 32, :].rearrange("m (b u) p e -> m b u p e", u=2),
                in_=turned[c, half][:].rearrange("m b (p u e) -> m b u p e", u=2, e=2),
            )

        def less_stock(c, kb=None, parts=(slice(0, BANK), slice(BANK, NP))):
            src = stocks[c]
            if kb is not None:
                stocks[c] = place(f"rest{c}", [NP], F32, kb)
            for cols in parts:
                nc.gpsimd.tensor_tensor(stocks[c][:, cols], bent[c][:, cols], src[:, cols], ALU.subtract)

        def pair_slot(c, cols):
            t = c - PLAIN
            return pairs[:, t // 2, cols, t % 2]

        def join(c, cols):
            nc.gpsimd.tensor_tensor(pair_slot(c, cols), logs[c][:, cols], stocks[c][:, cols], ALU.add)

        def second_pass(acc, first, a, cols, codes, scales):
            count = acc.shape[1]
            for i in range(count):
                nt = first + i
                nc.tensor.matmul_mx(
                    out=acc[:, i, :],
                    lhsT=w2c[:, a, nt * 2 * P : (nt + 1) * 2 * P].bitcast(FP4X4),
                    lhsT_scale=w2s[:, a, nt * P : (nt + 1) * P],
                    rhs=codes[:, cols].bitcast(FP8X4),
                    rhs_scale=scales[:, cols],
                    start=(a == 0 and i == 0),
                    stop=(a == 1 and i == count - 1),
                )

        nc.vector.memset(planes[:].bitcast(I32), 0)
        nc.gpsimd.memset(gain_rows[:], 0.0)
        nc.sync.dma_start(list1[:], offs)
        nc.sync.dma_start(list2[:], offs2)
        nc.sync.dma_start(out=gains[:, 1, 0:4], in_=gain[PASS:].rearrange("(p t) -> p t", t=4))
        nc.sync.dma_start(out=words[0][:], in_=tab_words[0].rearrange("p t i -> p (t i)").bitcast(I32))
        for q in range(2):
            for a in range(2):
                nc.gpsimd.dma_start(
                    out=planes[32 * q + 4 * a : 32 * q + 4 * a + 4, :].bitcast(I32),
                    in_=tab_scales[a, 4 * q : 4 * q + 4, :].bitcast(I32),
                )
        load_w1(raw[0], 0, P)
        nc.sync.dma_start(out=weights[:, :OPENING], in_=wgs[:, :OPENING])
        nc.sync.dma_start(out=gain_rows[0:PLAIN, :], in_=gain[:PASS].rearrange("(c p) -> c p", p=P))
        for q in range(2, 4):
            for a in range(2):
                nc.sync.dma_start(
                    out=planes[32 * q + 4 * a : 32 * q + 4 * a + 4, :].bitcast(I32),
                    in_=tab_scales[a, 4 * q : 4 * q + 4, :].bitcast(I32),
                )
        nc.sync.dma_start(out=words[1][:], in_=tab_words[1].rearrange("p t i -> p (t i)").bitcast(I32))
        load_page(0)
        nc.sync.dma_start(out=weights[:, OPENING:BANK], in_=wgs[:, OPENING:BANK])
        load_w1(raw[1], P, P)
        nc.sync.dma_start(out=weights[:, BANK:], in_=wgs[:, BANK:])
        load_page(1)
        nc.sync.dma_start(list3[:], offs3)
        for a in range(2):
            rows = w1[a * PASS : (a + 1) * PASS, 2 * P : 4 * P]
            nc.sync.dma_start(out=raw23[a][:], in_=rows.rearrange("(p j) c -> p j c", j=4))
        for a in range(2):
            rows = w1[a * PASS : (a + 1) * PASS, PASS:]
            nc.sync.dma_start(out=raw_dealt[a][:], in_=rows.rearrange("(p j) c -> p j c", j=4))
        load_page(2)
        load_page(3)
        load_stock(0)
        load_stock(1)

        make_identity(nc, ident[:])
        nc.gpsimd.memset(knee[:], KNEE)
        nc.gpsimd.memset(w2s[:].rearrange("p a n -> p (a n)").bitcast(I32), 0)
        one = next_one(first_one[:])

        gain_t = bank("gain_t", [P], 7)
        nc.tensor.transpose(gain_t[:], gain_rows[:], ident[:])
        nc.scalar.copy(out=gains[:, 0, 0:4], in_=gain_t[:, 0:PLAIN])
        both = gains[:, :, 0:4]
        nc.vector.tensor_scalar(out=minus[:], in0=both, scalar1=-1.0, scalar2=0.0, op0=ALU.mult, op1=ALU.add)
        nc.vector.tensor_scalar(out=lift[:], in0=both, scalar1=KNEE, scalar2=0.0, op0=ALU.mult, op1=ALU.add)
        nc.vector.tensor_scalar(out=drop[:], in0=both, scalar1=-KNEE, scalar2=0.0, op0=ALU.mult, op1=ALU.add)
        nc.vector.reciprocal(out=inverse[:], in_=minus[:])
        nc.vector.tensor_copy(picked[0][:], words[0][:].bitcast(U32).indirect(list1[:]))
        nc.vector.tensor_copy(picked_scales[:], planes[:].indirect(list1[:]))
        round_w1(0, stage0, 0)
        quantise_w1(0, 1, stage0)
        for lo, hi in ((0, OPENING), (OPENING, BANK), (BANK, S)):
            nc.vector.tensor_copy(picked[1][:, lo:hi], words[1][:].bitcast(U32).indirect(list1[:, lo // 16 : hi // 16]))

        early0 = place("early0", [BANK], F32, 144)
        late0 = place("late0", [BANK], F32, 94)
        for index, (lo, hi) in enumerate(((0, OPENING), (OPENING, BANK))):
            product(0, lo, hi, index, early0[:, lo:hi])
            weighted_scatter(0, lo, hi, early0[:, lo:hi])
        stage1 = place("stage1", [1024], BF16, 126)
        round_w1(1, stage1, 0)
        quantise_w1(1, 1, stage1)
        product(0, BANK, S, 2, late0[:])
        weighted_scatter(0, BANK, S, late0[:])
        early1 = place("early1", [BANK], F32, 146)
        late1 = place("late1", [BANK], F32, 102)
        product(1, 0, BANK, 0, early1[:])
        weighted_scatter(1, 0, BANK, early1[:])
        stage23 = place("stage23", [2048], BF16, 122)
        round_w1_pair(0, stage23)
        gather(0, 98)
        round_w1_pair(1, stage23)
        quantise_w1(2, 2, stage23)
        product(1, BANK, S, 1, late1[:])
        weighted_scatter(1, BANK, S, late1[:])
        stage_dealt = place("stage_dealt", [4096], BF16, 136)
        for a in range(2):
            round_w1_dealt(a, stage_dealt)
        quantise_w1(4, 4, stage_dealt)
        early2 = place("early2", [BANK], F32, 114 + EDGE)
        late2 = place("late2", [BANK], F32, 120 + EDGE)
        product(2, 0, BANK, 2, early2[:])
        product(2, BANK, S, 3, late2[:])
        whole_product(3, 116 + EDGE)
        weighted_scatter(2, 0, BANK, early2[:])
        gather(1, 136)
        put[2] = place("put2", [BANK], F32, 114 + EDGE)
        weigh(2, put[2][:], late2[:], BANK, S)
        scatter(2, put[2][:], BANK, S)
        weigh_whole(3, 120 + EDGE)
        scatter(3, put[3][:])

        dealt = place("dealt", [4 * S], F32, 0)
        for q in (0, 2, 1, 3):
            nc.sync.dma_start(out=dealt[32 * q : 32 * q + 32, :], in_=wgs.rearrange("(q t) j -> q (t j)", t=4))
        load_page(4)
        load_page(5)
        for c in range(2, TILES):
            load_stock(c)
        for a in range(2):
            nc.sync.dma_start(out=w2c[:, a, :].bitcast(I32), in_=w2_words[a].bitcast(I32))
        for q in range(4):
            nc.sync.dma_start(
                out=w2s[32 * q : 32 * q + 4, :, :].bitcast(I32),
                in_=w2_scales[:, 4 * q : 4 * q + 4, :].rearrange("a r n -> r a n").bitcast(I32),
            )

        zt = place("zt", [16, P, 2], BF16, 226)
        exponentials(0, 110 + EDGE, 176)
        whole_product(4, 98)
        whole_product(5, 168)
        whole_product(6, 156)
        whole_product(7, 160)
        exponentials(1, 51, 180, 174)
        negate_stock(0, 132)
        negate_stock(1, 16)
        open_sums(0)
        open_sums(1)
        weigh_whole(4, 20)
        one = logarithms((0, 1), one, 136)
        gather(2, 43)
        gather(3, 98)
        load_page(6)
        for c in (0, 1):
            for half in range(2):
                scale_log(c, half_cols(half))
                close_sum(c, half)
                round_sum(c, half)
        scatter(4, put[4][:])
        weigh_whole(5, 176)
        scatter(5, put[5][:])
        exponentials(2, 180, 184)
        negate_stock(2, 170)
        exponentials(3, 43, 192, 140)
        negate_stock(3, 24)
        open_sums(2)
        open_sums(3)
        weigh_whole(6, 28)
        one = logarithms((2, 3), one, 98)
        gather(4, 166)
        gather(5, 196)
        scatter(6, put[6][:])
        for c in (2, 3):
            for half in range(2):
                scale_log(c, half_cols(half))
                close_sum(c, half)
        for half in range(2):
            for c in (2, 3):
                round_sum(c, half)
        weigh_whole(7, 192)
        shifted = place("shifted", [EARLY], F32, 184)
        nc.gpsimd.tensor_scalar(out=shifted[:], in0=stocks[LAST][:, :EARLY], scalar1=column(lift, LAST), scalar2=1.0, op0=ALU.add, op1=ALU.mult)
        shifted6 = place("shifted6", [NP], F32, 160)
        nc.gpsimd.tensor_scalar(
            out=shifted6[:], in0=stocks[6][:], scalar1=column(lift, 6), scalar2=1.0, op0=ALU.add, op1=ALU.mult
        )
        woven0 = place("woven0", [NP, 2], F32, 144)
        for j in range(4):
            back = bank(f"back{j}", [2, 2, P], j)
            for b in range(2):
                for u in range(2):
                    src = zt[:, (2 * j + b) * 2 + u, :, :].rearrange("m p e -> m (p e)").bitcast(F32)
                    nc.tensor.transpose(back[:, b, u, :], src, ident[:])
            nc.scalar.copy(
                out=woven0[:, j * 256 : (j + 1) * 256, :].rearrange("p (b m) u -> p b m u", b=2),
                in_=back[:].rearrange("p b u m -> p b m u"),
            )
        gather(6, 208, (0, BANK, NP))
        exponentials(4, 226, 200)
        less_stock(4)
        load_page(LAST)
        scatter(LAST, put[LAST][:])
        pieces = [slice(lo, hi) for lo, hi in zip(LAST_PIECES, LAST_PIECES[1:])]
        fetched = [place(f"fetched{i}", [hi - lo], F32, kb) for i, (lo, hi, kb) in enumerate(zip(LAST_PIECES, LAST_PIECES[1:], (220, 86, 82)))]

        def fetched_piece(cols):
            return fetched[LAST_PIECES.index(cols.start)][:]

        for piece in pieces:
            fetch(LAST, fetched_piece(piece), piece.start, piece.stop)

        pairs = place("pairs", [2, NP, 2], BF16, 66)
        exponentials(5, 166, 204, 142)
        less_stock(5)
        one = logarithms((4, 5), one, 196)
        everything = slice(0, NP)
        for half in range(2):
            scale_log(4, half_cols(half))
        join(4, half_cols(0))
        scale_log(5, everything)
        join(4, half_cols(1))
        join(5, everything)
        lower, upper = slice(0, EARLY), slice(EARLY, NP)
        bent[6] = place("bent6", [NP], F32, 200)
        logs[6] = place("soft6", [NP], F32, 212)
        side6 = place("side6", [NP - EARLY], F32, 152)
        for dst, src in zip(halves(bent[6]), halves(got[6])):
            bend(6, dst, src)
        exponential(6, logs[6][:, :BANK], bent[6][:, :BANK])
        exponential(6, logs[6][:, BANK:EARLY], bent[6][:, BANK:EARLY])
        exponential(6, side6[:], bent[6][:, upper])
        rest6 = place("rest6", [NP], F32, 196)
        nc.gpsimd.tensor_tensor(rest6[:], bent[6][:], shifted6[:], ALU.subtract)
        logarithm(logs[6][:, lower], logs[6][:, lower], one)
        logarithm(logs[6][:, upper], side6[:], one)
        scaled = place("scaled6", [EARLY], F32, 216)
        nc.scalar.activation(out=scaled[:], in_=logs[6][:, lower], func=ACT.Copy, scale=column(gains, 6))
        nc.gpsimd.tensor_tensor(pair_slot(6, lower), scaled[:], rest6[:, lower], ALU.add)
        last_one = place("last_one", [1], F32, 152)
        one = next_one(last_one[:])

        bent[LAST] = place("bent7", [EARLY], F32, 152 + EDGE)
        soft[LAST] = place("soft7", [NP], F32, 98)
        raw_exp = place("raw_exp", [NP - EARLY], F32, 85 + EDGE)
        floored = place("floored", [NP - EARLY], F32, 144)
        for piece in pieces[:2]:
            bend(LAST, bent[LAST][:, piece], fetched_piece(piece))
        for piece in pieces[:2]:
            exponential(LAST, soft[LAST][:, piece], bent[LAST][:, piece])
        nc.scalar.activation(out=raw_exp[:], in_=fetched_piece(pieces[2]), func=ACT.Exp, scale=-1.0)
        codes0 = place("codes0", [NP], U32, 220)
        scales0 = place("scales0", [NP], U8, 57)
        codes1 = place("codes1", [NP], U32, 106)
        scales1 = place("scales1", [NP], U8, 47)
        woven1 = place("woven1", [NP, 2, 2], BF16, 74)
        rests = place("rests", [NP], F32, 216)
        nc.vector.quantize_mx(
            out=codes0[:].bitcast(FP8X4), scales=scales0[:], in_=woven0[:].rearrange("p m u -> p (m u)").bitcast(BF16)
        )
        nc.vector.scalar_tensor_tensor(
            out=pair_slot(6, upper), in0=logs[6][:, upper], scalar=column(gains, 6), in1=rest6[:, upper], op0=ALU.mult, op1=ALU.add
        )
        nc.vector.tensor_tensor(rests[:, lower], bent[LAST][:], shifted[:], ALU.subtract)
        nc.vector.tensor_scalar(
            out=floored[:], in0=fetched_piece(pieces[2]), scalar1=-KNEE, scalar2=column(gains, LAST), op0=ALU.max, op1=ALU.mult
        )
        nc.vector.tensor_scalar_min(out=soft[LAST][:, upper], in0=raw_exp[:], scalar1=CAP)
        nc.vector.tensor_tensor(rests[:, upper], floored[:], stocks[LAST][:, upper], ALU.subtract)
        chunks = [slice(lo, hi) for lo, hi in zip(TAIL_CUTS, TAIL_CUTS[1:])]
        accs = []
        for j, cols in enumerate(chunks):
            width = cols.stop - cols.start
            count = BANK // width
            for first in range(0, N // P, count):
                accs.append((j, first, bank(f"res{j}_{first}", [count, width], len(accs))))
        for j, first, acc in accs:
            second_pass(acc, first, 0, chunks[j], codes0, scales0)
        logs[LAST] = place("log7", [NP], F32, 87.5 - EDGE)
        for cols in chunks:
            logarithm(logs[LAST][:, cols], soft[LAST][:, cols], one)

        def last_join(cols):
            nc.vector.scalar_tensor_tensor(
                out=pair_slot(LAST, cols), in0=logs[LAST][:, cols], scalar=column(gains, LAST),
                in1=rests[:, cols], op0=ALU.mult, op1=ALU.add,
            )

        def weave(cols):
            nc.vector.tensor_copy(out=woven1[:, cols, :, :], in_=pairs[:, :, cols, :].rearrange("p u m e -> p m u e"))

        def finish(j):
            cols = chunks[j]
            nc.vector.quantize_mx(
                out=codes1[:, cols].bitcast(FP8X4), scales=scales1[:, cols],
                in_=woven1[:, cols, :, :].rearrange("p m u e -> p (m u e)"),
            )
            for index, (jj, first, acc) in enumerate(accs):
                if jj == j:
                    count = acc.shape[1]
                    second_pass(acc, first, 1, cols, codes1, scales1)
                    staged = place(f"staged{index}", acc.shape[1:], F32, 2 * index)
                    if index in (5, 7):
                        nc.vector.tensor_copy(out=staged[:], in_=acc[:])
                    else:
                        nc.scalar.copy(out=staged[:], in_=acc[:])
                    rows = out[first * P : (first + count) * P, cols]
                    nc.sync.dma_start(out=rows.rearrange("(i p) n -> p i n", p=P), in_=staged[:])

        for step in range(len(chunks) + 2):
            if step < len(chunks):
                last_join(chunks[step])
            if step >= 2:
                finish(step - 2)
            if 1 <= step <= len(chunks):
                weave(chunks[step - 1])
